import numpy as np, ml_dtypes
CORES = [16,18,20,22]
N = 4
BF = ml_dtypes.bfloat16
def gentries(a):
    return np.ascontiguousarray(a.reshape(8, 16, -1).transpose(0, 2, 1)).reshape(8, -1)
def gtable(e):
    e = np.asarray(e); return np.ascontiguousarray(e.reshape(8, -1, 16).transpose(0, 2, 1)).reshape(128, -1).astype(np.int32)
R, M, L, F, RO = 512, 512, 3, 512, 3
V = R + L * M
AT = [0] + [R + i * M for i in range(L + 1)]
LEV = np.repeat(np.arange(L + 1), np.diff(AT))
TOP = np.concatenate([2 * np.array(AT)[LEV[R:]], np.full(R, 2 * V)])
LOW = np.array(AT)[LEV + 1]
def under(rng, shape, top):
    return np.minimum((rng.random(shape) * top).astype(np.int64), np.asarray(top) - 1)
def parts(rng):
    i = np.arange(16)[:, None]; sh = (N, 8, 1, V)
    p = rng.integers(0, 16, sh); p2 = (p + rng.integers(1, 16, sh)) % 16
    t = 1 + (255 * rng.random(sh) ** (1.5 + LEV)).astype(np.int64); t2 = 1 + (255 * rng.random(sh) ** (1.5 + LEV)).astype(np.int64)
    x = np.where(i == p, t, 0); x = np.where((i == p2) & (rng.random(sh) < 0.125), t2, x); x = np.where(rng.random(sh) < 0.02, 0, x)
    s = (256 * rng.random((N, 8, 16, R)) ** 1.5).astype(np.int64)
    c = rng.integers(0, 256, (N, 8, 16, R + F)) * (rng.random((N, 8, 16, R + F)) > 0.15)
    half = rng.random(sh) < 0.75
    o = np.argsort(rng.random((N, 8, 16, V)) + 10 * (half & (i >= 8)), axis=2)
    k = np.where(half, rng.choice(np.array([0, 1, 1, 2, 2, 3, 4, 8]), sh), rng.choice(np.array([1, 2, 3, 5, 12, 16]), sh))
    e = np.where(o < k, under(rng, (N, 8, 16, V), TOP), 2 * V)
    a = LOW + under(rng, (N, 8, 2, V), V + R + F - LOW)
    return x, s, c[..., :R].copy(), c[..., R:].copy(), e, a
def rich(rng, x, v):
    k = rng.integers(3, 17, (N, 8, 1, V)); o = np.argsort(rng.random(x.shape), axis=2)
    return np.where(rng.random((N, 8, 1, V)) < 0.25, np.where(o < k, v, 0), x)
def pack(x, s, q, c, e, a):
    def b(v):
        return np.ascontiguousarray(v.reshape(N, 128, -1)).astype(np.float32).astype(BF)
    return {"piv": b(x), "safe": b(s), "lem": b(q), "leaf": b(c), "uses": np.ascontiguousarray(e.reshape(N, 128, V)).astype(np.int32), "prem": np.stack([gtable(v) for v in a.reshape(N, 8, 2 * V)])}
def setup_inputs(rng):
    return pack(*parts(rng))
def setup_inputs_turn(rng):
    x, s, q, c, e, a = parts(rng); i = np.arange(16)[:, None]
    j = rng.integers(0, 16, (N, 8, 1, 1)); w = rng.integers(0, 7, (N, 8, 1, V))
    w[..., :7] = np.arange(7)
    one, two = i == j, i == (j + 8) % 16
    m = np.where(w == 0, one, np.where(w == 1, two, np.where(w == 2, one | two, np.where(w == 3, i < 8, np.where(w == 4, i >= 8, w == 5)))))
    n = under(rng, (N, 8, 16, V), TOP); n = n - (n & 1) * (rng.random(n.shape) < 0.5)
    x = np.where(rng.random((N, 8, 1, V)) < 0.3, 0, x)
    return pack(x, s, q, c, np.where(m, n, 2 * V), a)
def setup_inputs_ties(rng):
    x, s, q, c, e, a = parts(rng); v = np.array([0, 1, 127, 128, 129, 254, 255])
    x = rich(rng, x, 1)
    x = np.where(x > 0, rng.choice(np.array([1, 127, 128, 129, 255]), x.shape), 0); nx = np.roll(x, 8, axis=2)
    s, q, c = rng.choice(v, s.shape), rng.choice(v, q.shape), rng.choice(v, c.shape)
    s[..., 0] = x[..., 0]; s[..., 1] = np.maximum(x[..., 1] - 1, 0); s[..., 2] = np.maximum(x[..., 2], nx[..., 2]); s[..., 3] = nx[..., 3]
    return pack(x, s, q, c, e, a)
def setup_inputs_alike(rng):
    x, s, q, c, e, a = parts(rng); on = e < 2 * V
    e[:, 1] = np.where(on[:, 1], under(rng, (N, 1, V), TOP), 2 * V)
    e[:, 2] = np.where(on[:, 2], np.where(rng.random((N, 16, V)) < 0.5, 0, TOP - 1), 2 * V)
    e[:, 3] = 2 * V
    e[:, 4] = np.where(on[:, 4], TOP - 1 - rng.integers(0, 16, (N, 16, V)), 2 * V)
    e[:, 5] = under(rng, (N, 16, V), TOP)
    a[:, 1, 1] = a[:, 1, 0]; a[:, 2] = np.where(rng.random((N, 2, V)) < 0.5, LOW, V + R + F - 1)
    a[:, 4] = V + rng.integers(0, R, (N, 2, V)); a[:, 5] = V + R + rng.integers(0, F, (N, 2, V)); a[:, 6] = LOW
    return pack(x, s, q, c, e, a)
def setup_inputs_late(rng):
    x, s, q, c, e, a = parts(rng); g = int(rng.integers(0, 8)); s[:] = 0
    q2, c2 = rng.integers(200, 256, q.shape), rng.integers(200, 256, c.shape); q2[:, g] = q[:, g]; c2[:, g] = c[:, g]
    e[..., V - R:] = np.where(rng.random((N, 8, 1, R)) < 0.5, 2 * V, e[..., V - R:])
    return pack(x, s, q2, c2, e, a)
def setup_inputs_spread(rng):
    x, s, q, c, e, a = parts(rng)
    def u(n):
        return np.minimum((np.exp2(8 * rng.random((N, 8, 1, n))) * rng.random((N, 8, 16, n))).astype(np.int64), 255)
    x = np.where(x > 0, np.minimum(np.exp2(8 * rng.random(x.shape)).astype(np.int64), 255), 0)
    x = rich(rng, x, np.maximum(u(V), 1))
    m = rng.random((N, 8, 16, V)) < rng.random((N, 8, 1, V)) ** 3
    return pack(x, u(R), u(R), u(F), np.where(m, under(rng, (N, 8, 16, V), TOP), 2 * V), a)
def check_inputs(d):
    bad = []
    for k in ("piv", "safe", "lem", "leaf"):
        v = np.asarray(d[k]).astype(np.float32)
        if not np.all((v >= 0) & (v <= 255) & (v == np.floor(v))): bad.append("whole numbers from 0 to 255 in " + k)
    e = np.asarray(d["uses"]).astype(np.int64)
    if not np.all(((e >= 0) & (e < TOP)) | (e == 2 * V)): bad.append("range of uses")
    a = np.stack([gentries(v) for v in d["prem"]]).astype(np.int64).reshape(N, 8, 2, V)
    if not np.all((a >= LOW) & (a < V + R + F)): bad.append("range of prem")
    return bad
def least(S, e):
    return np.stack([[np.min(np.take(S[q, g], e[q, g], axis=1), axis=1) for g in range(8)] for q in range(N)])
def splice(e, st):
    K = np.zeros((N, 8, 1, 2 * V + 1), bool)
    K[:, :, 0, 2 * R:2 * V:2] = st[..., R:] == 1; K[:, :, 0, 2 * R + 1:2 * V:2] = st[..., R:] == 2
    loose = np.take_along_axis(K, e, 3); has = np.any(loose, axis=2, keepdims=True); j = np.argmax(loose, axis=2)[:, :, None]
    this = (np.arange(16)[:, None] == j) & has
    u = np.take_along_axis(e, j, 2) >> 1
    t = np.roll(np.take_along_axis(e, np.where(has, u - R, 0), 3), 8, axis=2)
    hit = np.any((t != 2 * V) & (e != 2 * V) & ~this, axis=2, keepdims=True)
    return np.where(has & ~hit, np.where(t != 2 * V, t, np.where(this, 2 * V, e)), e)
def reference(piv, safe, lem, leaf, uses, prem):
    def w(v):
        return v.astype(np.float32).astype(np.int64).reshape(N, 8, 16, -1)
    x = w(piv); nx = np.roll(x, 8, axis=2)
    s = np.full((N, 8, 16, V), 255, np.int64); s[..., :R] = w(safe)
    C = np.zeros((N, 8, 16, V + R + F), np.int64); C[..., V:V + R] = w(lem); C[..., V + R:] = w(leaf)
    e = uses.astype(np.int64).reshape(N, 8, 16, V)
    a = np.stack([gentries(v) for v in prem]).astype(np.int64).reshape(N, 8, 2, V)
    st = np.zeros((N, 8, V), np.int64); S = np.full((N, 8, 16, 2 * V + 1), 255, np.int64); gs = None
    for rnd in range(RO):
        old = st[:, :, None] > 0
        if rnd:
            s[..., :R] = np.where(old[..., :R], s[..., :R], np.roll(gs, 1, axis=0))
            C[..., V:V + R] = np.roll(C[..., :R], -1, axis=0)
            e = splice(e, st)
        for l in range(L + 1):
            i, j = AT[l], AT[l + 1]
            if l: s[..., i:j] = np.where(old[..., i:j], s[..., i:j], least(S, e[..., i - R:j - R]))
            y, p, n = s[..., i:j], x[..., i:j], nx[..., i:j]; b = st[..., i:j]
            b = np.where(b > 0, b, np.where(np.all(y >= p, axis=2), 1, np.where(np.all(y >= n, axis=2), 2, 0)))
            st[..., i:j] = b; b = b[:, :, None]
            S[..., 2 * i:2 * j:2] = np.where(b == 0, np.maximum(y, p), np.where(b == 1, y, 255))
            S[..., 2 * i + 1:2 * j:2] = np.where(b == 0, np.maximum(y, n), np.where(b == 2, y, 255))
        gs = least(S, e[..., V - R:])
        for l in range(L, -1, -1):
            i, j = AT[l], AT[l + 1]; p, n = x[..., i:j], nx[..., i:j]; b = st[..., i:j]
            A = np.take_along_axis(C, a[:, :, :1, i:j], 3); B = np.take_along_axis(C, a[:, :, 1:, i:j], 3)
            b = np.where(b > 0, b, np.where(~np.all(A >= p, axis=2), 1, np.where(~np.all(B >= n, axis=2), 2, 0)))
            st[..., i:j] = b; b = b[:, :, None]
            C[..., i:j] = np.where(b == 1, A, np.where(b == 2, B, np.maximum(np.where(p > 0, 0, A), np.where(n > 0, 0, B))))
    return {"yc": np.ascontiguousarray(C[..., :V]).reshape(N, 128, V).astype(np.float32).astype(BF), "ys": np.concatenate([s, gs], axis=3).reshape(N, 128, V + R).astype(np.float32).astype(BF)}

@@ -1,0 +1,554 @@
+from concourse.mybir import AluOpType as A, ActivationFunctionType as AF
+
+PW = 128
+CWM = 256
+CH = {l: [(512 * l, 256), (512 * l + 256, 256)] for l in range(4)}
+SW = 512
+NG, NSO, NFG, NMP = 6, 3, 4, 4
+MAINB, SPLB = 5, 3
+NB16 = 28
+SCRATCH = {
+    "raw": ("sbuf", [128, 2048], "int32"), "rpm": ("sbuf", [128, 256], "int32"), "po": ("sbuf", [128, 256], "uint16"),
+    "off": ("sbuf", [128, 2048], "uint16"), "lt0": ("sbuf", [128, 2056], "float32"), "lt1": ("sbuf", [128, 2056], "float32"),
+    "F": ("sbuf", [128, 4112], "bfloat16"), "Z": ("sbuf", [128, 4112], "bfloat16"),
+    "xm": ("sbuf", [128, 4096], "bfloat16"), "zx": ("sbuf", [128, 4096], "bfloat16"),
+    "o": ("sbuf", [128, 2560], "bfloat16"), "ko": ("sbuf", [128, 2048], "bfloat16"), "st": ("sbuf", [128, 2048], "bfloat16"),
+    "sf": ("sbuf", [128, 512], "bfloat16"), "as1": ("sbuf", [128, 512], "bfloat16"), "as2": ("sbuf", [128, 512], "bfloat16"),
+    "ob": ("sbuf", [128, 128], "bfloat16"), "of": ("sbuf", [128, 128], "float32"), "tb": ("sbuf", [128, 128], "bfloat16"), "tf": ("sbuf", [128, 128], "float32"),
+    "ones": ("sbuf", [128, 512], "bfloat16"), "mb": ("sbuf", [128, 128 * NB16], "bfloat16"), "mf": ("sbuf", [128, 128 * 17], "float32"), "blf": ("sbuf", [128, 128], "float32"),
+    "m1": ("sbuf", [128, 2048], "bfloat16"), "ip": ("sbuf", [128, 16], "int32"), "pw": ("sbuf", [128, 16], "float32"),
+    "yo": ("sbuf", [128, 2560], "bfloat16"),
+}
+for _k in range(3): SCRATCH["cw%d" % _k] = ("sbuf", [128, 3072], "bfloat16")
+for _k in range(NG): SCRATCH["g%d" % _k] = ("sbuf", [128, PW * 16], "bfloat16")
+for _k in range(NFG): SCRATCH["fg%d" % _k] = ("sbuf", [128, PW * 16], "bfloat16")
+for _k in range(NSO): SCRATCH["so%d" % _k] = ("sbuf", [128, CWM * 16], "bfloat16")
+for _k in range(NMP): SCRATCH["mp%d" % _k] = ("sbuf", [128, PW * 16], "bfloat16")
+for _k in range(3):
+    for _n, _w in (("ab", 2 * CWM), ("tt", 2 * CWM), ("vv", CWM), ("mm", CWM), ("bb", CWM), ("ww", CWM)): SCRATCH["%s%d" % (_n, _k)] = ("sbuf", [128, _w], "bfloat16")
+for _k in range(2):
+    for _n in ("X", "L1", "Tg", "dl"): SCRATCH["%s%d" % (_n, _k)] = ("sbuf", [128, SW], "float32")
+    for _n in ("ge", "hm"): SCRATCH["%s%d" % (_n, _k)] = ("sbuf", [128, SW], "bfloat16")
+    SCRATCH["xi%d" % _k] = ("sbuf", [128, SW // 16], "int32")
+    SCRATCH["xu%d" % _k] = ("sbuf", [128, SW // 16], "uint16")
+for _k in range(8): SCRATCH["ps%d" % _k] = ("psum", [128, 512], "float32")
+NDMA = 60
+QS = ("vector", "scalar", "tensor", "pool")
+SEMAPHORES = ["q_" + q for q in QS] + ["d%d" % k for k in range(NDMA)] + ["ra%d" % k for k in range(4)] + ["la%d" % k for k in range(4)]
+
+CY = 0.00083
+OV = {"vector": 0.06, "scalar": 0.07, "tensor": 0.02, "pool": 0.15, "sync": 0.1}
+PEC = 0.00055
+WAKE = 0.12
+SZ = {"float32": 4, "int32": 4, "bfloat16": 2, "uint16": 2}
+GC = 1.5
+ASG = "1000110001010100000111001100000110100011100000010010111000000001001010010000101001100010110000000000101110100101101010000000000000101001001000011011100100100000110000001001010010000011001100000000100000001000000101001001001"
+OFFS = {'1 down2g': -3, '0 up1k': -2, '1 down0t': 19, '1 up0k': 17, '1 up0t': 10, '1 up0v': 20, '0 up0g': 14, '0 ghostsg': -15, '0 ghostsv': -28,
+        '1 splice4g': 4, '2 up2g': 15, '2 up2y': -12, '1 down3t': -10, '1 down3v': -12, '2 ghostsg': -12, '2 splice3t': -4, '2 splice4g': -45,
+        '2 down0v': 9, 'initv': -3, '0 down3v': -16, '1 up1t': -2, '1 up1v': 1, '1 splice2v': 8, '2 up1y': 19, '2 down1t': 2, '0 up2t': 5,
+        '1 down1t': -6, '1 down0v': -1, '1 splice2g': -9, '1 splice3v': -2, '2 up1t': 2, '0 up0v': 1, '1 splice3g': -6, '1 splice3t': -12}
+PLAN = {}
+
+
+def conflict(a, b):
+    if a[1] >= b[2] or b[1] >= a[2]: return False
+    return not (a[3] == 2 and b[3] == 2 and (a[1] - b[1]) % 2)
+
+
+def build(T, rank, topo, core):
+    ops = []
+    last = {}
+    ndma = [0]
+    ph = ["init"]
+
+    def ap(r):
+        t = T[r[0]]
+        return t[:, r[1]:r[2]] if r[3] == 1 else t[:, r[1]:r[2]:r[3]]
+
+    def R(name, lo=0, hi=None, st=1):
+        return (name, lo, SCRATCH[name][1][1] if hi is None else hi, st)
+
+    def n_of(r): return (r[2] - r[1] + r[3] - 1) // r[3]
+
+    def isps(r): return SCRATCH[r[0]][0] == "psum"
+
+    def sz(r): return SZ[SCRATCH[r[0]][2]]
+
+    def op(opts, rd, wr, sem=None, kind="v"):
+        i = len(ops)
+        deps = {}
+        qs = set(o[0] for o in opts)
+        for w, lst in ((0, rd), (1, wr)):
+            for r in lst:
+                for (j, rr, ww) in last.setdefault(r[0], []):
+                    if j == i: continue
+                    if isps(r):
+                        if qs == {"tensor"} and ops[j]["qs"] == {"tensor"}: k = "acc"
+                        else: k = "w" if (w or ww) and conflict(r, rr) else "ord"
+                    else:
+                        if not (w or ww) or not conflict(r, rr): continue
+                        k = "w"
+                    if deps.get(j) != "w": deps[j] = k
+        ops.append(dict(opts=opts, deps=deps, sem=sem, qs=qs, name=ph[0] + kind))
+        for w, lst in ((1, wr), (0, rd)):
+            for r in lst:
+                h = last[r[0]]
+                if w and not isps(r) and r[3] == 1: h[:] = [e for e in h if not (r[1] <= e[1][1] and e[1][2] <= r[2])]
+                h.append((i, r, w))
+        return i
+
+    cut = {}
+    rot = {}
+
+    def bank(pool):
+        n, base = (MAINB, 0) if pool == "m" else (SPLB, MAINB)
+        k = rot.get(pool, 0); rot[pool] = k + 1
+        b = "ps%d" % (base + k % n)
+        h = last.setdefault(b, [])
+        h[:] = h[cut.get(b, 0):]
+        cut[b] = len(h)
+        return b
+
+    def pick(name, n):
+        k = rot.get(name, 0); rot[name] = k + 1
+        return "%s%d" % (name, k % n)
+
+    def cv(n, per): return max(64, n * per) * CY + OV["vector"]
+
+    def tt(out, a, b, f, **k):
+        per = 1 if (isps(a) or isps(b)) else 2
+        return op([("vector", cv(n_of(out), per), lambda e: e.tensor_tensor(ap(out), ap(a), ap(b), f))], [a, b], [out], **k)
+
+    def vts(out, a, s1, s2, f, f2=None):
+        per = 0.5 if (sz(out) == 2 and sz(a) == 2) else 1
+        kw = {} if f2 is None else {"op1": f2}
+        return ("vector", cv(n_of(out), per), lambda e: e.tensor_scalar(ap(out), ap(a), ap(s1) if isinstance(s1, tuple) else s1, s2, op0=f, **kw))
+
+    def act(out, a, f, bias=0.0, scale=1.0):
+        return ("scalar", max(64, n_of(out)) * CY + OV["scalar"], lambda e: e.activation(ap(out), ap(a), f, bias=bias, scale=scale))
+
+    def ts(out, a, s1, s2, f, f2=None, **k):
+        return op([vts(out, a, s1, s2, f, f2)], [a] + ([s1] if isinstance(s1, tuple) else []), [out], **k)
+
+    def flex(out, a, o1, o2, **k): return op([o1, o2], [a], [out], **k)
+
+    def vcopy(out, a):
+        per = 0.5 if (sz(out) == 2 and sz(a) == 2) else 1
+        return ("vector", cv(n_of(out), per), lambda e: e.tensor_copy(ap(out), ap(a)))
+
+    def copy(out, a, **k): return op([vcopy(out, a)], [a], [out], **k)
+
+    def fcopy(out, a, **k): return flex(out, a, act(out, a, AF.Copy), vcopy(out, a), **k)
+
+    def mset(out, c, **k):
+        return op([("vector", cv(n_of(out), 0.5), lambda e: e.memset(ap(out), c))], [], [out], **k)
+
+    def mm(lst, **k):
+        def fn(e):
+            for (o_, l_, r_, s_, t_) in lst: ins = e.matmul(ap(o_), ap(l_), ap(r_), s_, t_)
+            return ins
+        us = sum(max(64, n_of(o_)) * (4 if sz(l_) == 4 else 1) * PEC + OV["tensor"] for (o_, l_, r_, s_, t_) in lst)
+        rd, wr = [], []
+        for (o_, l_, r_, s_, t_) in lst:
+            for z, y in ((l_, rd), (r_, rd), (o_, wr)):
+                if z not in y: y.append(z)
+        return op([("tensor", us, fn)], rd, wr, kind="t", **k)
+
+    def gather(out, win, offs_, relu):
+        n = n_of(out)
+        if relu:
+            fv = lambda e: e.tensor_scalar(ap(out), ap(win).indirect(ap(offs_)), -1.0, 0.0, op0=A.mult, op1=A.max)
+            fs = lambda e: e.activation(ap(out), ap(win).indirect(ap(offs_)), AF.Relu, scale=-1.0)
+        else:
+            fv = lambda e: e.tensor_copy(ap(out), ap(win).indirect(ap(offs_)))
+            fs = lambda e: e.activation(ap(out), ap(win).indirect(ap(offs_)), AF.Copy)
+        return op([("scalar", n * GC * CY + OV["scalar"], fs), ("vector", n * GC * CY + OV["vector"], fv)], [win, offs_], [out], kind="g")
+
+    def scan(out, g_, m_):
+        return op([("vector", cv(n_of(out), 0.5), lambda e: e.tensor_tensor_scan(ap(out), ap(g_), ap(m_), 0.0, A.max, A.mult))], [g_, m_], [out])
+
+    def dma(q, out, in_, rd, wr):
+        s = "d%d" % ndma[0]; ndma[0] += 1
+        return op([(q, OV["sync"], lambda e: e.dma_start(out(), in_()))], rd, wr, sem=(s, 16))
+
+    def load(q, r, src, lo, hi): return dma(q, lambda: ap(r), lambda: T[src][:, lo:hi], [], [r])
+
+    def store(q, dst, lo, hi, r): return dma(q, lambda: T[dst][:, lo:hi], lambda: ap(r), [r], [])
+
+    def local(q, r, s): return dma(q, lambda: ap(r), lambda: ap(s), [s], [r])
+
+    MB = {}
+
+    def mat(nm): return R("mb", MB[nm] * 128, MB[nm] * 128 + 128)
+
+    def newmat(nm):
+        MB[nm] = len(MB)
+        return mat(nm)
+
+    def matf(k): return R("mf", k * 128, k * 128 + 128)
+
+    load("sync", R("raw", 0, 512), "uses", 0, 512)
+    load("scalar", R("yo", 0, 512), "piv", 0, 512)
+    load("sync", R("sf"), "safe", 0, 512)
+    load("scalar", R("rpm"), "prem", 0, 256)
+    for l in range(1, 4):
+        load("sync", R("yo", 512 * l, 512 * l + 512), "piv", 512 * l, 512 * l + 512)
+        load("sync", R("raw", 512 * l, 512 * l + 512), "uses", 512 * l, 512 * l + 512)
+    load("sync", R("cw0", 2560, 3072), "leaf", 0, 512)
+    load("sync", R("cw0", 2048, 2560), "lem", 0, 512)
+
+    def gsel(out, src, pattern, cmp, base, cm):
+        def fn(e): return e.affine_select(ap(out), ap(src), pattern, cmp, 0.0, base, cm)
+        return op([("pool", 0.17 + 256 * CY + 0.05, fn)], [src], [out])
+    mset(R("ob"), 1.0)
+    gsel(newmat("P"), R("ob"), [[-16, 8], [8, 2], [-1, 8]], A.is_equal, -8, 1)
+    gsel(newmat("I"), R("ob"), [[-1, 128]], A.is_equal, 0, 1)
+    gsel(R("tb"), R("ob"), [[-16, 8], [0, 16]], A.is_ge, 0, 1)
+    gsel(newmat("B"), R("tb"), [[16, 8], [0, 16]], A.is_ge, 15, -1)
+    gsel(newmat("sub"), mat("B"), [[-1, 128]], A.is_equal, 1, 1)
+
+    def scaled(nm, src, c):
+        o_ = newmat(nm)
+        return flex(o_, mat(src), act(o_, mat(src), AF.Copy, scale=float(c)), vts(o_, mat(src), float(c), None, A.mult))
+    mset(R("ones"), 1.0)
+    for nm, s_, c in (("B2", "B", 2), ("Bn16", "B", -0.0625), ("I5", "I", 512), ("In5", "I", -512), ("Bn2", "B", -2), ("B16", "B", 0.0625)): scaled(nm, s_, c)
+    mset(R("m1"), 1.0); mset(R("m1", 15, 2048, 16), -1.0)
+    mset(R("F"), 0.0)
+
+    def pair(l):
+        for n0, w in CH[l]:
+            a, b = R("xm", 2 * n0, 2 * n0 + w), R("xm", 2 * n0 + w, 2 * n0 + 2 * w)
+            ts(a, R("yo", n0, n0 + w), -255.0, None, A.add)
+            p = R(bank("m"), 0, w)
+            mm([(p, mat("P"), a, True, True)])
+            fcopy(b, p)
+
+    def zero(l): ts(R("zx", 1024 * l, 1024 * l + 1024), R("xm", 1024 * l, 1024 * l + 1024), -255.0, -255.0, A.is_gt, A.mult)
+
+    def offs(l): copy(R("off", 512 * l - 512, 512 * l), R("raw", 512 * l - 512, 512 * l))
+
+    def late_consts():
+        ts(R("cw0", 2048, 3072), R("cw0", 2048, 3072), -255.0, None, A.add)
+        for k in (1, 2): local("sync", R("cw%d" % k, 2560, 3072), R("cw0", 2560, 3072))
+        for k in range(NMP): local("sync", R("mp%d" % k), R("m1"))
+        mset(R("Z"), 0.0)
+        mset(R("of"), 1.0)
+        gsel(R("tf"), R("of"), [[-16, 8], [0, 16]], A.is_ge, 0, 1)
+        gsel(R("blf"), R("tf"), [[16, 8], [0, 16]], A.is_ge, 15, -1)
+        gsel(matf(16), R("of"), [[-16, 8], [8, 2], [-1, 8]], A.is_equal, -8, 1)
+        for q in range(16): gsel(matf(q), R("blf"), [[0, 8], [1, 16]], A.is_equal, -q, 0)
+        for i in range(16): scaled("D%d" % i, "I", 2.0 ** (15 - i))
+        tt(newmat("S1"), mat("I"), mat("sub"), A.subtract)
+        tt(newmat("Sn"), mat("sub"), mat("I"), A.subtract)
+        op([("pool", 0.2, lambda e: e.iota(T["ip"][:, 0:1], [[0, 1]], 0, 1))], [], [R("ip", 0, 1)])
+        for k, f in ((0, 2), (1, 4), (2, 16), (3, 256)):
+            ts(R("ip", 1 + k, 2 + k), R("ip", 0, 1), 1 << k, None, A.bitwise_and)
+            ts(R("pw", 1 + k, 2 + k), R("ip", 1 + k, 2 + k), -(f - 1) / float(1 << k), float(f), A.mult, A.add)
+        tt(R("pw", 5, 6), R("pw", 1, 2), R("pw", 2, 3), A.mult)
+        tt(R("pw", 6, 7), R("pw", 3, 4), R("pw", 4, 5), A.mult)
+        tt(R("pw", 0, 1), R("pw", 5, 6), R("pw", 6, 7), A.mult)
+        for l in range(1, 5):
+            a = 512 * (l - 1) + (8 if l == 4 else 0)
+            ts(R("lt0", a, a + 512), R("raw", 512 * l - 512, 512 * l), -1.0, 4096.0, A.mult, A.add)
+            if l == 1: ts(R("lt1", a, a + 512), R("raw", 0, 512), -1.0, 4096.0, A.mult, A.add)
+        for z in ("lt0", "lt1"): mset(R(z, 1536, 1544), 0.0)
+
+    def thr(tab, n0, w, sign, both=True):
+        b = bank("m")
+        mm([(R(b, 0, 2 * w), mat("I"), R(tab, 2 * n0, 2 * n0 + 2 * w), True, not both)])
+        if both:
+            s_ = R("st", n0, n0 + w)
+            p, m = (mat("I5"), mat("In5")) if sign > 0 else (mat("In5"), mat("I5"))
+            return b, lambda: mm([(R(b, 0, w), p, s_, False, False), (R(b, w, 2 * w), m, s_, False, True)])
+        return b, None
+
+    def counts(w, first, second, t):
+        b = bank("m")
+        mm([(R(b, 0, w), mat(first), R("ones", 0, w), True, False)])
+        mm([(R(b, 0, w), mat(second), R(t, 0, w), False, True), (R(b, w, 2 * w), mat("B"), R(t, w, 2 * w), True, True)])
+        return b
+
+    def tests(rnd, n0, w, osrc):
+        n1 = n0 + w
+        nb, fin = thr("xm", n0, w, 1, rnd > 0)
+        if fin: fin()
+        t = pick("tt", 3)
+        tt(R(t, 0, w), osrc, R(nb, 0, w), A.is_lt)
+        tt(R(t, w, 2 * w), osrc, R(nb, w, 2 * w), A.is_lt)
+        cb = counts(w, "Bn16", "B2", t)
+        v = R(pick("vv", 3), 0, w)
+        c = R(cb, w, 2 * w)
+        flex(v, c, act(v, c, AF.Relu, bias=1.0, scale=-1.0), vts(v, c, 0.0, None, A.is_equal))
+        n2, fin = thr("xm", n0, w, 1)
+        tt(R("st", n0, n1), v, R(cb, 0, w), A.min)
+        fin()
+        return n2
+
+    def edges(n0, w, n2):
+        n1 = n0 + w
+        tt(R("F", 2 * n0, 2 * n1, 2), R("o", n0, n1), R(n2, 0, w), A.max)
+        tt(R("F", 2 * n0 + 1, 2 * n1, 2), R("o", n0, n1), R(n2, w, 2 * w), A.max)
+
+    def plus(a, b): flex(a, b, act(a, b, AF.Copy, bias=255.0), vts(a, b, 255.0, None, A.add), kind="y")
+
+    def out_s(lo, hi):
+        plus(R("yo", lo, hi), R("o", lo, hi)); store("sync", "ys", lo, hi, R("yo", lo, hi))
+
+    def down0(rnd):
+        ph[0] = "%d down0" % rnd
+        for n0, w in CH[0]:
+            n1 = n0 + w
+            if rnd == 0: ts(R("o", n0, n1), R("sf", n0, n1), -255.0, None, A.add)
+            else:
+                w_, z = R(pick("ww", 3), 0, w), R(pick("bb", 3), 0, w)
+                ts(w_, R("st", n0, n1), 0.0, None, A.is_equal)
+                tt(z, R("as%d" % rnd, n0, n1), w_, A.mult)
+                tt(R("o", n0, n1), z, R("ko", n0, n1), A.add)
+            edges(n0, w, tests(rnd, n0, w, R("o", n0, n1)))
+        if rnd == 2: out_s(0, 512)
+
+    def pieces(rnd, col, n0, w, so):
+        for p in range(0, w, PW):
+            gb = R(pick("g", NG))
+            gather(gb, R("F", 0, 4097), R("off", col + p, col + p + PW), True)
+            if n0 is None or rnd == 0: m_ = R("m1")
+            else:
+                mp = pick("mp", NMP)
+                ts(R(mp, 15, PW * 16, 16), R("st", n0 + p, n0 + p + PW), 0.0, -1.0, A.is_equal, A.mult)
+                m_ = R(mp)
+            scan(R(so, p * 16, (p + PW) * 16), gb, m_)
+
+    def down(rnd, l):
+        ph[0] = "%d down%d" % (rnd, l)
+        todo = []
+        for n0, w in CH[l]:
+            n1 = n0 + w
+            so = pick("so", NSO)
+            pieces(rnd, n0 - 512, n0, w, so)
+            last_ = R(so, 15, w * 16, 16)
+            o_ = R("o", n0, n1)
+            todo.append((n0, w, tests(rnd, n0, w, last_)))
+            if rnd == 0: fcopy(o_, last_)
+            else: tt(o_, last_, R("ko", n0, n1), A.add)
+        for z in todo: edges(*z)
+        if rnd == 2: out_s(512 * l, 512 * l + 512)
+
+    nremote = [0]
+
+    def send(src, dst, to):
+        k = nremote[0]; nremote[0] += 1
+        d = T.cores[to % 4]
+        rid, pid = topo.addr(d)[:2]
+        mask = sum(1 << e for e in topo.engines(core, d)[:8])
+        i = op([("pool", 1.0, lambda e: e.remote_dma(ap(dst), ap(src), T.sem["ra%d" % k], T.sem["la%d" % k], pid, rid, mask))], [src], [], sem=("la%d" % k, 8))
+        j = op([(None, 5.0, None)], [], [dst], sem=("ra%d" % k, 8))
+        ops[j]["after"] = i
+
+    def ghosts(rnd):
+        ph[0] = "%d ghosts" % rnd
+        for c in range(0, 512, CWM):
+            so = pick("so", NSO)
+            pieces(rnd, 1536 + c, None, CWM, so)
+            fcopy(R("o", 2048 + c, 2048 + c + CWM), R(so, 15, CWM * 16, 16))
+        if rnd < 2: send(R("o", 2048, 2560), R("as%d" % (rnd + 1)), rank + 1)
+        else: out_s(2048, 2560)
+
+    def up(rnd, l):
+        ph[0] = "%d up%d" % (rnd, l)
+        cw = "cw%d" % rnd
+        for n0, w in CH[l]:
+            n1, c = n0 + w, n0 // 8
+            ab = pick("ab", 3); a_, b_ = R(ab, 0, w), R(ab, w, 2 * w)
+            gather(R(ab, 0, 2 * w), R(cw, 512 * l + 512, 3072), R("po", c, c + w // 8), False)
+            xb, fin = thr("xm", n0, w, -1)
+            fin()
+            t = pick("tt", 3)
+            tt(R(t, 0, 2 * w), R(ab, 0, 2 * w), R(xb, 0, 2 * w), A.is_lt)
+            fb = counts(w, "B16", "Bn2", t)
+            v = R(pick("vv", 3), 0, w); f_ = R(fb, w, 2 * w)
+            flex(v, f_, act(v, f_, AF.Sign), vts(v, f_, 1.0, None, A.min))
+            tb, fin = thr("zx", n0, w, -1)
+            tt(R("st", n0, n1), v, R(fb, 0, w), A.min)
+            fin()
+            m_ = R(pick("mm", 3), 0, w)
+            tt(R(tb, 0, w), a_, R(tb, 0, w), A.min)
+            tt(m_, b_, R(tb, w, 2 * w), A.min)
+            tt(R(cw, n0, n1), m_, R(tb, 0, w), A.max)
+            if rnd < 2:
+                if l:
+                    ts(R("Z", 2 * n0, 2 * n1, 2), R("st", n0, n1), 0.0, None, A.is_lt, kind="z")
+                    zb = R("Z", 2 * n0 + 1, 2 * n1, 2)
+                    flex(zb, R("st", n0, n1), act(zb, R("st", n0, n1), AF.Relu), vts(zb, R("st", n0, n1), 0.0, None, A.is_gt), kind="z")
+                z = R(pick("bb", 3), 0, w)
+                ts(z, R("st", n0, n1), 0.0, None, A.not_equal, kind="k")
+                tt(R("ko", n0, n1), R("o", n0, n1), z, A.mult, kind="k")
+            else:
+                plus(R("ko", n0, n1), R(cw, n0, n1)); store("sync", "yc", n0, n1, R("ko", n0, n1))
+        if rnd < 2 and l == 0: send(R(cw, 0, 512), R("cw%d" % (rnd + 1), 2048, 2560), rank - 1)
+
+    def splice(k, l):
+        ph[0] = "%d splice%d" % (k + 1, l)
+        src, dst = ("lt0", "lt1") if k == 0 else ("lt1", "lt0")
+        for c in range(0, 512, SW):
+            w = SW
+            col = 512 * (l - 1) + c
+            lc = col + (8 if l == 4 else 0)
+            L = R(src, lc, lc + w)
+            mk = bank("s")
+            for p in range(0, w, PW):
+                fg = pick("fg", NFG)
+                gather(R(fg), R("Z", 0, 4097), R("off", col + p, col + p + PW), False)
+                for h in range(0, 16, 4): mm([(R(mk, p, p + PW), mat("D%d" % i), R(fg, i, PW * 16, 16), i == 0, i == 15) for i in range(h, h + 4)])
+            ge = R(pick("ge", 2))
+            ts(ge, R(mk, 0, w), R("pw", 0, 1), None, A.is_ge)
+            th = R(bank("s"), 0, w)
+            mm([(th, mat("S1"), ge, True, True)])
+            X = pick("X", 2)
+            tt(R(X), L, th, A.mult)
+            wr = R(bank("s"), 0, w // 16)
+            for h in range(0, 16, 4): mm([(wr, matf(q), R(X, q, w, 16), q == 0, q == 15) for q in range(h, h + 4)])
+            xi, xu = R(pick("xi", 2)), R(pick("xu", 2))
+            ts(xi, wr, -0.5, 1535.75, A.mult, A.add)
+            copy(xu, xi)
+            nt = R(bank("s"), 0, w)
+            mm([(nt, mat("B16"), R("ones", 0, w), True, False), (nt, mat("Sn"), ge, False, True)])
+            L1 = R(pick("L1", 2))
+            tt(L1, L, nt, A.mult)
+            tg = pick("Tg", 2)
+            gather(R(tg), R(src, 0, 1544), xu, False)
+            tp = bank("s")
+            for h in range(0, w, 128): mm([(R(tp, h, h + 128), matf(16), R(tg, h, h + 128), True, True)])
+            h = R(pick("hm", 2))
+            tp = R(tp, 0, w)
+            tt(h, L1, tp, A.min)
+            ht = R(bank("s"), 0, w)
+            mm([(ht, mat("B"), h, True, True)])
+            dl = R(pick("dl", 2))
+            tt(dl, tp, R(X), A.subtract)
+            flex(ht, ht, act(ht, ht, AF.Relu, bias=1.0, scale=-1.0), vts(ht, ht, 0.0, None, A.is_equal))
+            tt(ht, dl, ht, A.mult)
+            tt(R(dst, lc, lc + w), L, ht, A.add)
+            ts(R("off", col, col + w), R(dst, lc, lc + w), -1.0, 4096.0, A.mult, A.add)
+
+    pair(0)
+    down0(0)
+    for l in (1, 2, 3):
+        ph[0] = "init"
+        offs(l); pair(l)
+        down(0, l)
+    ph[0] = "init"
+    offs(4)
+    for l in (3, 2, 1, 0): zero(l)
+    for l in range(4):
+        for n0, w in CH[l]:
+            for z in range(2): ts(R("po", n0 // 8 + z * w // 16, n0 // 8 + (z + 1) * w // 16), R("rpm", 128 * z + n0 // 16, 128 * z + (n0 + w) // 16), -512.0 * (l + 1), None, A.add)
+    ph[0] = "late"
+    late_consts()
+    for rnd in range(3):
+        if rnd:
+            for l in (2, 3, 4): splice(rnd - 1, l)
+            down0(rnd)
+            for l in (1, 2, 3): down(rnd, l)
+        ghosts(rnd)
+        for l in (3, 2, 1, 0): up(rnd, l)
+    return ops
+
+
+def flexes(ops): return [i for i, o in enumerate(ops) if len(o["opts"]) == 2]
+
+
+def assign_of(ops, s):
+    fl = flexes(ops)
+    a = [o["opts"][0][0] for o in ops]
+    for k, i in enumerate(fl): a[i] = "vector" if (s[k] == "1" if s else k % 3 == 0) else "scalar"
+    return a
+
+
+def plan(ops, asg, offs):
+    n = len(ops)
+    us = [[x[1] for x in o["opts"] if x[0] == asg[i]][0] for i, o in enumerate(ops)]
+    lat = [2.5 if o["sem"] else 0.0 for o in ops]
+    succ = [[] for _ in range(n)]
+    left = [0] * n
+    for i, o in enumerate(ops):
+        p = set(o["deps"])
+        if "after" in o: p.add(o["after"])
+        left[i] = len(p)
+        for j in p: succ[j].append(i)
+    pr = [0.0] * n
+    for i in range(n - 1, -1, -1): pr[i] = max([pr[s] for s in succ[i]] or [0.0]) + WAKE + us[i] + lat[i]
+    pr = [pr[i] + offs.get(ops[i]["name"], 0.0) for i in range(n)]
+    rt = [0.0] * n
+    fin = [0.0] * n
+    free = {}
+    ready = {}
+    for i in range(n):
+        if not left[i]: ready.setdefault(asg[i], []).append(i)
+    order = []
+    while len(order) < n:
+        bt, bq = None, None
+        for q in (None, "vector", "scalar", "tensor", "pool", "sync"):
+            if ready.get(q):
+                t = max(min(rt[i] for i in ready[q]), free.get(q, 0.0))
+                if bt is None or t < bt: bt, bq = t, q
+        i = min((-pr[i], i) for i in ready[bq] if rt[i] <= bt + 1e-9)[1]
+        ready[bq].remove(i)
+        f = bt + us[i]
+        if bq is not None:
+            free[bq] = f
+            f += lat[i]
+        fin[i] = f
+        order.append(i)
+        for j in succ[i]:
+            rt[j] = max(rt[j], f + WAKE)
+            left[j] -= 1
+            if not left[j]: ready.setdefault(asg[j], []).append(j)
+    return order, max(fin), fin
+
+
+def rank_program(g, core, T, topo):
+    rank = T.rank_of(core)
+    if rank is None:
+        return
+    ops = build(T, rank, topo, core)
+    if "p" not in PLAN:
+        asg = assign_of(ops, ASG)
+        order = plan(ops, asg, OFFS)[0]
+        PLAN["p"] = (order, asg, {j: k for k, j in enumerate(order)})
+    order, asg, pos = PLAN["p"]
+    eng = {"vector": g.vector, "scalar": g.scalar, "tensor": g.tensor, "pool": g, "sync": g.sync}
+    count = {}
+    done = {}
+    clock = {}
+    know = {q: {} for q in eng}
+    for i in order:
+        o, q = ops[i], asg[i]
+        if q is None:
+            done[i] = o["sem"]; clock[i] = {}
+            continue
+        need = {}
+        for j, kind in o["deps"].items():
+            if asg[j] == q and kind != "w" and not ops[j]["sem"] and not o["sem"]: continue
+            s, v = done[j]
+            if need.get(s, (0, 0))[0] < v: need[s] = (v, j)
+        kn = know[q]
+        for s, (v, j) in sorted(need.items(), key=lambda z: -pos[z[1][1]]):
+            if kn.get(s, 0) >= v: continue
+            eng[q].wait_ge(T.sem[s], v)
+            for s2, v2 in clock[j].items():
+                if kn.get(s2, 0) < v2: kn[s2] = v2
+            kn[s] = max(kn.get(s, 0), v)
+        ins = [x[2] for x in o["opts"] if x[0] == q][0](eng[q])
+        clock[i] = dict(kn)
+        if o["sem"]:
+            done[i] = o["sem"]
+            if o["sem"][0][0] == "d": ins.then_inc(T.sem[o["sem"][0]], o["sem"][1])
+        else:
+            s = "q_" + q
+            count[s] = count.get(s, 0) + 1
+            ins.then_inc(T.sem[s], 1)
+            done[i] = (s, count[s])
+    fin = dict(count)
+    for o in ops:
+        if o["sem"]: fin[o["sem"][0]] = o["sem"][1]
+    for s in sorted(fin): g.wait_ge(T.sem[s], fin[s])

@@ -1,52 +1,46 @@
 from concourse.mybir import AluOpType as A, ActivationFunctionType as AF
 
-PW = 128
-CWM = 256
-CH = {l: [(512 * l, 256), (512 * l + 256, 256)] for l in range(4)}
-SW = 512
-NG, NSO, NFG, NMP = 6, 3, 4, 4
-MAINB, SPLB = 5, 3
-NB16 = 28
+BS = 64
+K = 512.0
+KC = 4096
+CFG = {
+    "ch": {0: (256, 256), 1: (256, 256), 2: (256, 256), 3: (256, 256), 4: (256, 256)},
+    "m": {(0, 1): (2, 2), (0, 2): (1, 2), (0, 3): (1, 2), (0, 4): (1, 4),
+          (1, 1): (2, 2), (1, 2): (2, 1), (1, 3): (1, 4), (1, 4): (4, 2),
+          (2, 1): (2, 2), (2, 2): (2, 1), (2, 3): (1, 4), (2, 4): (4, 2)},
+    "gp": 1024, "fp": 1024, "td": "vf", "tu": "vf",
+}
+NB = 4
+NG, NSO, NFG = 6, 3, 4
 SCRATCH = {
     "raw": ("sbuf", [128, 2048], "int32"), "rpm": ("sbuf", [128, 256], "int32"), "po": ("sbuf", [128, 256], "uint16"),
-    "off": ("sbuf", [128, 2048], "uint16"), "lt0": ("sbuf", [128, 2056], "float32"), "lt1": ("sbuf", [128, 2056], "float32"),
+    "off": ("sbuf", [128, 2560], "uint16"), "Lh": ("sbuf", [128, 2048], "float16"), "Lw": ("sbuf", [128, 1536], "float32"),
     "F": ("sbuf", [128, 4112], "bfloat16"), "Z": ("sbuf", [128, 4112], "bfloat16"),
-    "xm": ("sbuf", [128, 4096], "bfloat16"), "zx": ("sbuf", [128, 4096], "bfloat16"),
-    "o": ("sbuf", [128, 2560], "bfloat16"), "ko": ("sbuf", [128, 2048], "bfloat16"), "st": ("sbuf", [128, 2048], "bfloat16"),
-    "sf": ("sbuf", [128, 512], "bfloat16"), "as1": ("sbuf", [128, 512], "bfloat16"), "as2": ("sbuf", [128, 512], "bfloat16"),
-    "ob": ("sbuf", [128, 128], "bfloat16"), "of": ("sbuf", [128, 128], "float32"), "tb": ("sbuf", [128, 128], "bfloat16"), "tf": ("sbuf", [128, 128], "float32"),
-    "ones": ("sbuf", [128, 512], "bfloat16"), "mb": ("sbuf", [128, 128 * NB16], "bfloat16"), "mf": ("sbuf", [128, 128 * 17], "float32"), "blf": ("sbuf", [128, 128], "float32"),
-    "m1": ("sbuf", [128, 2048], "bfloat16"), "ip": ("sbuf", [128, 16], "int32"), "pw": ("sbuf", [128, 16], "float32"),
-    "yo": ("sbuf", [128, 2560], "bfloat16"),
+    "x": ("sbuf", [128, 2048], "bfloat16"), "zk": ("sbuf", [128, 2048], "bfloat16"),
+    "o": ("sbuf", [128, 2560], "bfloat16"), "kx": ("sbuf", [128, 2048], "bfloat16"),
+    "as1": ("sbuf", [128, 512], "bfloat16"), "as2": ("sbuf", [128, 512], "bfloat16"),
+    "ob": ("sbuf", [128, 128], "bfloat16"), "kb": ("sbuf", [128, 1024], "bfloat16"), "mb": ("sbuf", [128, 128 * 6], "bfloat16"),
+    "iw": ("sbuf", [128, 152 * 7], "bfloat16"), "W": ("sbuf", [128, 288], "bfloat16"), "tri": ("sbuf", [128, 2048], "bfloat16"),
+    "S": ("sbuf", [128, 1024], "bfloat16"), "Sn": ("sbuf", [128, 1024], "bfloat16"), "U": ("sbuf", [128, 1024], "bfloat16"),
+    "mo": ("sbuf", [128, 256], "bfloat16"), "tl": ("sbuf", [128, 4096], "bfloat16"),
+    "ip": ("sbuf", [128, 8], "int32"), "col": ("sbuf", [128, 8], "float32"),
 }
+for _k in (4, 8, 16): SCRATCH["mk%d" % _k] = ("sbuf", [128, 2048], "bfloat16")
 for _k in range(3): SCRATCH["cw%d" % _k] = ("sbuf", [128, 3072], "bfloat16")
-for _k in range(NG): SCRATCH["g%d" % _k] = ("sbuf", [128, PW * 16], "bfloat16")
-for _k in range(NFG): SCRATCH["fg%d" % _k] = ("sbuf", [128, PW * 16], "bfloat16")
-for _k in range(NSO): SCRATCH["so%d" % _k] = ("sbuf", [128, CWM * 16], "bfloat16")
-for _k in range(NMP): SCRATCH["mp%d" % _k] = ("sbuf", [128, PW * 16], "bfloat16")
+for _k in range(NG): SCRATCH["g%d" % _k] = ("sbuf", [128, 2048], "bfloat16")
+for _k in range(NFG): SCRATCH["fg%d" % _k] = ("sbuf", [128, 2048], "bfloat16")
+for _k in range(NSO): SCRATCH["so%d" % _k] = ("sbuf", [128, 4096], "bfloat16")
 for _k in range(3):
-    for _n, _w in (("ab", 2 * CWM), ("tt", 2 * CWM), ("vv", CWM), ("mm", CWM), ("bb", CWM), ("ww", CWM)): SCRATCH["%s%d" % (_n, _k)] = ("sbuf", [128, _w], "bfloat16")
-for _k in range(2):
-    for _n in ("X", "L1", "Tg", "dl"): SCRATCH["%s%d" % (_n, _k)] = ("sbuf", [128, SW], "float32")
-    for _n in ("ge", "hm"): SCRATCH["%s%d" % (_n, _k)] = ("sbuf", [128, SW], "bfloat16")
-    SCRATCH["xi%d" % _k] = ("sbuf", [128, SW // 16], "int32")
-    SCRATCH["xu%d" % _k] = ("sbuf", [128, SW // 16], "uint16")
+    for _n in ("ga", "gb", "ta", "tb", "qq", "th", "ot"): SCRATCH["%s%d" % (_n, _k)] = ("sbuf", [128, 512], "bfloat16")
+    for _n in ("X", "Tg", "hm", "Tk", "Lk"): SCRATCH["%s%d" % (_n, _k)] = ("sbuf", [128, 512], "float16")
+    SCRATCH["xi%d" % _k] = ("sbuf", [128, 32], "int32")
+    SCRATCH["xu%d" % _k] = ("sbuf", [128, 32], "uint16")
 for _k in range(8): SCRATCH["ps%d" % _k] = ("psum", [128, 512], "float32")
-NDMA = 60
+NDMA = 50
 QS = ("vector", "scalar", "tensor", "pool")
 SEMAPHORES = ["q_" + q for q in QS] + ["d%d" % k for k in range(NDMA)] + ["ra%d" % k for k in range(4)] + ["la%d" % k for k in range(4)]
 
-CY = 0.00083
-OV = {"vector": 0.06, "scalar": 0.07, "tensor": 0.02, "pool": 0.15, "sync": 0.1}
-PEC = 0.00055
-WAKE = 0.12
-SZ = {"float32": 4, "int32": 4, "bfloat16": 2, "uint16": 2}
-GC = 1.5
-ASG = "1000110001010100000111001100000110100011100000010010111000000001001010010000101001100010110000000000101110100101101010000000000000101001001000011011100100100000110000001001010010000011001100000000100000001000000101001001001"
-OFFS = {'1 down2g': -3, '0 up1k': -2, '1 down0t': 19, '1 up0k': 17, '1 up0t': 10, '1 up0v': 20, '0 up0g': 14, '0 ghostsg': -15, '0 ghostsv': -28,
-        '1 splice4g': 4, '2 up2g': 15, '2 up2y': -12, '1 down3t': -10, '1 down3v': -12, '2 ghostsg': -12, '2 splice3t': -4, '2 splice4g': -45,
-        '2 down0v': 9, 'initv': -3, '0 down3v': -16, '1 up1t': -2, '1 up1v': 1, '1 splice2v': 8, '2 up1y': 19, '2 down1t': 2, '0 up2t': 5,
-        '1 down1t': -6, '1 down0v': -1, '1 splice2g': -9, '1 splice3v': -2, '2 up1t': 2, '0 up0v': 1, '1 splice3g': -6, '1 splice3t': -12}
+SZ = {"float32": 4, "int32": 4, "bfloat16": 2, "uint16": 2, "float16": 2}
 PLAN = {}
 
 
@@ -55,31 +49,37 @@ def conflict(a, b):
     return not (a[3] == 2 and b[3] == 2 and (a[1] - b[1]) % 2)
 
 
-def build(T, rank, topo, core):
+def build(T, rank, topo, core, phys, cfg):
     ops = []
     last = {}
     ndma = [0]
     ph = ["init"]
+    rot = {}
+
+    def isps(r): return r[0][0] == "#"
 
     def ap(r):
-        t = T[r[0]]
+        t = T["ps%d" % phys[r[0]]] if isps(r) else T[r[0]]
         return t[:, r[1]:r[2]] if r[3] == 1 else t[:, r[1]:r[2]:r[3]]
 
     def R(name, lo=0, hi=None, st=1):
         return (name, lo, SCRATCH[name][1][1] if hi is None else hi, st)
 
+    def sub(r, a, b, st=1):
+        return (r[0], r[1] + a * r[3], r[1] + (b - 1) * r[3] + 1, r[3] * st)
+
     def n_of(r): return (r[2] - r[1] + r[3] - 1) // r[3]
 
-    def isps(r): return SCRATCH[r[0]][0] == "psum"
+    def sz(r): return 4 if isps(r) else SZ[SCRATCH[r[0]][2]]
 
-    def sz(r): return SZ[SCRATCH[r[0]][2]]
-
-    def op(opts, rd, wr, sem=None, kind="v"):
+    def op(opts, rd, wr, sem=None, kind="v", after=()):
         i = len(ops)
         deps = {}
         qs = set(o[0] for o in opts)
+        banks = set()
         for w, lst in ((0, rd), (1, wr)):
             for r in lst:
+                if isps(r): banks.add(r[0])
                 for (j, rr, ww) in last.setdefault(r[0], []):
                     if j == i: continue
                     if isps(r):
@@ -89,7 +89,7 @@ def build(T, rank, topo, core):
                         if not (w or ww) or not conflict(r, rr): continue
                         k = "w"
                     if deps.get(j) != "w": deps[j] = k
-        ops.append(dict(opts=opts, deps=deps, sem=sem, qs=qs, name=ph[0] + kind))
+        ops.append(dict(opts=opts, deps=deps, sem=sem, qs=qs, name=ph[0] + kind, after=[a for a in after if a is not None], banks=banks))
         for w, lst in ((1, wr), (0, rd)):
             for r in lst:
                 h = last[r[0]]
@@ -97,241 +97,244 @@ def build(T, rank, topo, core):
                 h.append((i, r, w))
         return i
 
-    cut = {}
-    rot = {}
+    def bank(w):
+        rot["#"] = rot.get("#", 0) + 1
+        return ("#%d" % rot["#"], 0, w, 1)
 
-    def bank(pool):
-        n, base = (MAINB, 0) if pool == "m" else (SPLB, MAINB)
-        k = rot.get(pool, 0); rot[pool] = k + 1
-        b = "ps%d" % (base + k % n)
-        h = last.setdefault(b, [])
-        h[:] = h[cut.get(b, 0):]
-        cut[b] = len(h)
-        return b
-
-    def pick(name, n):
+    def pick(name, n, w=None):
         k = rot.get(name, 0); rot[name] = k + 1
-        return "%s%d" % (name, k % n)
+        return R("%s%d" % (name, k % n), 0, w)
 
-    def cv(n, per): return max(64, n * per) * CY + OV["vector"]
+    def half(*rs): return 0.5 if all(sz(r) == 2 for r in rs) else 1
 
     def tt(out, a, b, f, **k):
         per = 1 if (isps(a) or isps(b)) else 2
-        return op([("vector", cv(n_of(out), per), lambda e: e.tensor_tensor(ap(out), ap(a), ap(b), f))], [a, b], [out], **k)
+        return op([("vector", (n_of(out) * per, 0, 1, 0), lambda e: e.tensor_tensor(ap(out), ap(a), ap(b), f))], [a, b], [out], **k)
+
+    def sc(s): return ap(s) if isinstance(s, tuple) else s
 
     def vts(out, a, s1, s2, f, f2=None):
-        per = 0.5 if (sz(out) == 2 and sz(a) == 2) else 1
         kw = {} if f2 is None else {"op1": f2}
-        return ("vector", cv(n_of(out), per), lambda e: e.tensor_scalar(ap(out), ap(a), ap(s1) if isinstance(s1, tuple) else s1, s2, op0=f, **kw))
+        return ("vector", (n_of(out) * half(out, a), 0, 1, 0), lambda e: e.tensor_scalar(ap(out), ap(a), sc(s1), sc(s2), op0=f, **kw))
 
     def act(out, a, f, bias=0.0, scale=1.0):
-        return ("scalar", max(64, n_of(out)) * CY + OV["scalar"], lambda e: e.activation(ap(out), ap(a), f, bias=bias, scale=scale))
+        return ("scalar", (n_of(out), 0, 1, 0), lambda e: e.activation(ap(out), ap(a), f, bias=bias, scale=scale))
 
     def ts(out, a, s1, s2, f, f2=None, **k):
-        return op([vts(out, a, s1, s2, f, f2)], [a] + ([s1] if isinstance(s1, tuple) else []), [out], **k)
+        return op([vts(out, a, s1, s2, f, f2)], [a] + [s for s in (s1, s2) if isinstance(s, tuple)], [out], **k)
 
     def flex(out, a, o1, o2, **k): return op([o1, o2], [a], [out], **k)
 
-    def vcopy(out, a):
-        per = 0.5 if (sz(out) == 2 and sz(a) == 2) else 1
-        return ("vector", cv(n_of(out), per), lambda e: e.tensor_copy(ap(out), ap(a)))
+    def vcopy(out, a): return ("vector", (n_of(out) * half(out, a), 0, 1, 0), lambda e: e.tensor_copy(ap(out), ap(a)))
 
     def copy(out, a, **k): return op([vcopy(out, a)], [a], [out], **k)
 
     def fcopy(out, a, **k): return flex(out, a, act(out, a, AF.Copy), vcopy(out, a), **k)
 
-    def mset(out, c, **k):
-        return op([("vector", cv(n_of(out), 0.5), lambda e: e.memset(ap(out), c))], [], [out], **k)
+    def relu(out, a, **k): return flex(out, a, act(out, a, AF.Relu), vts(out, a, 0.0, None, A.max), **k)
 
-    def mm(lst, **k):
+    def lin(out, a, m, c, **k): return flex(out, a, act(out, a, AF.Copy, bias=float(c), scale=float(m)), vts(out, a, float(m), float(c), A.mult, A.add), **k)
+
+    def mset(out, c, **k): return op([("vector", (n_of(out) * 0.5, 0, 1, 0), lambda e: e.memset(ap(out), c))], [], [out], **k)
+
+    def mm(lst, start=True, stop=True, **k):
         def fn(e):
-            for (o_, l_, r_, s_, t_) in lst: ins = e.matmul(ap(o_), ap(l_), ap(r_), s_, t_)
+            for j, (o_, l_, r_) in enumerate(lst): ins = e.matmul(ap(o_), ap(l_), ap(r_), start and j == 0, stop and j == len(lst) - 1)
             return ins
-        us = sum(max(64, n_of(o_)) * (4 if sz(l_) == 4 else 1) * PEC + OV["tensor"] for (o_, l_, r_, s_, t_) in lst)
         rd, wr = [], []
-        for (o_, l_, r_, s_, t_) in lst:
+        for (o_, l_, r_) in lst:
             for z, y in ((l_, rd), (r_, rd), (o_, wr)):
                 if z not in y: y.append(z)
-        return op([("tensor", us, fn)], rd, wr, kind="t", **k)
+        return op([("tensor", (sum(max(64, n_of(z[0])) for z in lst), 0, len(lst), 0), fn)], rd, wr, kind="t", **k)
 
-    def gather(out, win, offs_, relu):
-        n = n_of(out)
-        if relu:
-            fv = lambda e: e.tensor_scalar(ap(out), ap(win).indirect(ap(offs_)), -1.0, 0.0, op0=A.mult, op1=A.max)
-            fs = lambda e: e.activation(ap(out), ap(win).indirect(ap(offs_)), AF.Relu, scale=-1.0)
-        else:
-            fv = lambda e: e.tensor_copy(ap(out), ap(win).indirect(ap(offs_)))
-            fs = lambda e: e.activation(ap(out), ap(win).indirect(ap(offs_)), AF.Copy)
-        return op([("scalar", n * GC * CY + OV["scalar"], fs), ("vector", n * GC * CY + OV["vector"], fv)], [win, offs_], [out], kind="g")
+    def gather(out, win, offs_, **k):
+        c = (0, n_of(out), 1, 0)
+        return op([("scalar", c, lambda e: e.activation(ap(out), ap(win).indirect(ap(offs_)), AF.Copy)),
+                   ("vector", c, lambda e: e.tensor_copy(ap(out), ap(win).indirect(ap(offs_))))], [win, offs_], [out], kind="g", **k)
 
-    def scan(out, g_, m_):
-        return op([("vector", cv(n_of(out), 0.5), lambda e: e.tensor_tensor_scan(ap(out), ap(g_), ap(m_), 0.0, A.max, A.mult))], [g_, m_], [out])
+    def gmin(out, win, offs_):
+        return op([("vector", (0, n_of(out), 1, 0), lambda e: e.tensor_tensor(ap(out), ap(win).indirect(ap(offs_)), ap(out), A.min))], [win, offs_, out], [out], kind="f")
+
+    def scan(out, m_, g_):
+        return op([("vector", (n_of(out) * 0.5, 0, 1, 0), lambda e: e.tensor_tensor_scan(ap(out), ap(m_), ap(g_), 0.0, A.max, A.min))], [g_, m_], [out], kind="s")
 
     def dma(q, out, in_, rd, wr):
         s = "d%d" % ndma[0]; ndma[0] += 1
-        return op([(q, OV["sync"], lambda e: e.dma_start(out(), in_()))], rd, wr, sem=(s, 16))
+        return op([(q, (0, 0, 0, 0.1), lambda e: e.dma_start(out(), in_()))], rd, wr, sem=(s, 16), kind="d")
 
     def load(q, r, src, lo, hi): return dma(q, lambda: ap(r), lambda: T[src][:, lo:hi], [], [r])
 
-    def store(q, dst, lo, hi, r): return dma(q, lambda: T[dst][:, lo:hi], lambda: ap(r), [r], [])
+    def store(dst, lo, hi, r): return dma("sync", lambda: T[dst][:, lo:hi], lambda: ap(r), [r], [])
 
-    def local(q, r, s): return dma(q, lambda: ap(r), lambda: ap(s), [s], [r])
+    def gsel(out, src, pattern, cmp, base, cm, fill=0.0):
+        return op([("pool", (2 * n_of(out), 0, 0, 0.22), lambda e: e.affine_select(ap(out), ap(src), pattern, cmp, fill, base, cm))], [src], [out], kind="p")
 
-    MB = {}
+    def iota(out, pattern, base, cm):
+        kw = {} if SCRATCH[out[0]][2] == "int32" else {"allow_small_or_imprecise_dtypes": True}
+        return op([("pool", (2 * n_of(out), 0, 0, 0.18), lambda e: e.iota(ap(out), pattern, base, cm, **kw))], [], [out], kind="p")
 
-    def mat(nm): return R("mb", MB[nm] * 128, MB[nm] * 128 + 128)
+    I = R("iw", 12, 140)
+    P, In, Pn, P2, I4 = (R("mb", 128 * k, 128 * k + 128) for k in range(5))
+    Mo, Mc = R("mo", 0, 128), R("mo", 128, 256)
 
-    def newmat(nm):
-        MB[nm] = len(MB)
-        return mat(nm)
+    def row(j, neg=False): return R("W", 144 * neg + 15 - j, 144 * neg + 143 - j)
 
-    def matf(k): return R("mf", k * 128, k * 128 + 128)
+    def blk(nm, k): return R(nm, 128 * k, 128 * k + 128)
 
+    def move(m, t, s):
+        a = 152 * (1 + t + (2 if m == 4 else 0)) + 12 - (s - t) * (16 // m)
+        return R("iw", a, a + 128)
+
+    def chunks(l):
+        a, out = 0, []
+        for k, w in enumerate(cfg["ch"][l]):
+            out.append((k, a, w)); a += w
+        return out
+
+    def tile(l, k, kind): return R("tl", BS * (3 * (4 * l + k) + kind), BS * (3 * (4 * l + k) + kind + 1))
+
+    def spread(b, nm, t): return [(sub(b, j * BS, j * BS + BS), blk(nm, j), t) for j in range(n_of(b) // BS)]
+
+    def ocol(rnd, l): return 2048 if (l == 1 and rnd and cfg["m"][0, 1] != cfg["m"][1, 1]) else 512 * (l - 1)
+
+    load("sync", R("o", 0, 512), "safe", 0, 512)
+    load("scalar", R("x", 0, 512), "piv", 0, 512)
     load("sync", R("raw", 0, 512), "uses", 0, 512)
-    load("scalar", R("yo", 0, 512), "piv", 0, 512)
-    load("sync", R("sf"), "safe", 0, 512)
-    load("scalar", R("rpm"), "prem", 0, 256)
-    for l in range(1, 4):
-        load("sync", R("yo", 512 * l, 512 * l + 512), "piv", 512 * l, 512 * l + 512)
-        load("sync", R("raw", 512 * l, 512 * l + 512), "uses", 512 * l, 512 * l + 512)
-    load("sync", R("cw0", 2560, 3072), "leaf", 0, 512)
+    load("scalar", R("x", 512, 2048), "piv", 512, 2048)
+    for l in range(1, 4): load("sync", R("raw", 512 * l, 512 * l + 512), "uses", 512 * l, 512 * l + 512)
+    load("sync", R("rpm"), "prem", 0, 256)
     load("sync", R("cw0", 2048, 2560), "lem", 0, 512)
+    for k in range(3): load("sync", R("cw%d" % k, 2560, 3072), "leaf", 0, 512)
+    nb = max(max(c) for c in cfg["ch"].values()) // BS
+    mset(R("ob"), 1.0); mset(R("iw"), 0.0); mset(R("W", 0, 144), 0.0); mset(R("kb", 0, 128 * nb), K)
+    gsel(I, R("ob"), [[-1, 128]], A.is_equal, 0, 1)
+    gsel(P, R("ob"), [[-16, 8], [8, 2], [-1, 8]], A.is_equal, -8, 1)
+    w8 = R("W", 15, 143, 16)
+    gsel(w8, R("ob", 0, 8), [[-16, 8]], A.is_ge, 0, 1)
+    gsel(w8, w8, [[16, 8]], A.is_ge, 15, -1)
+    lin(R("W", 144, 288), R("W", 0, 144), -1, 0)
+    lin(In, I, -1, 0)
+    made = set()
 
-    def gsel(out, src, pattern, cmp, base, cm):
-        def fn(e): return e.affine_select(ap(out), ap(src), pattern, cmp, 0.0, base, cm)
-        return op([("pool", 0.17 + 256 * CY + 0.05, fn)], [src], [out])
-    mset(R("ob"), 1.0)
-    gsel(newmat("P"), R("ob"), [[-16, 8], [8, 2], [-1, 8]], A.is_equal, -8, 1)
-    gsel(newmat("I"), R("ob"), [[-1, 128]], A.is_equal, 0, 1)
-    gsel(R("tb"), R("ob"), [[-16, 8], [0, 16]], A.is_ge, 0, 1)
-    gsel(newmat("B"), R("tb"), [[16, 8], [0, 16]], A.is_ge, 15, -1)
-    gsel(newmat("sub"), mat("B"), [[-1, 128]], A.is_equal, 1, 1)
-
-    def scaled(nm, src, c):
-        o_ = newmat(nm)
-        return flex(o_, mat(src), act(o_, mat(src), AF.Copy, scale=float(c)), vts(o_, mat(src), float(c), None, A.mult))
-    mset(R("ones"), 1.0)
-    for nm, s_, c in (("B2", "B", 2), ("Bn16", "B", -0.0625), ("I5", "I", 512), ("In5", "I", -512), ("Bn2", "B", -2), ("B16", "B", 0.0625)): scaled(nm, s_, c)
-    mset(R("m1"), 1.0); mset(R("m1", 15, 2048, 16), -1.0)
-    mset(R("F"), 0.0)
-
-    def pair(l):
-        for n0, w in CH[l]:
-            a, b = R("xm", 2 * n0, 2 * n0 + w), R("xm", 2 * n0 + w, 2 * n0 + 2 * w)
-            ts(a, R("yo", n0, n0 + w), -255.0, None, A.add)
-            p = R(bank("m"), 0, w)
-            mm([(p, mat("P"), a, True, True)])
-            fcopy(b, p)
-
-    def zero(l): ts(R("zx", 1024 * l, 1024 * l + 1024), R("xm", 1024 * l, 1024 * l + 1024), -255.0, -255.0, A.is_gt, A.mult)
-
-    def offs(l): copy(R("off", 512 * l - 512, 512 * l), R("raw", 512 * l - 512, 512 * l))
+    def parts(m):
+        if m > 1 and m not in made:
+            made.add(m)
+            for t in range(m): gsel(move(m, t, t), I, [[0, 8], [1, m], [0, 16 // m]], A.is_equal, -t, 0)
+    pk = [[-2, nb], [-16, 8], [0, 16]]
+    s_, kb = R("S", 0, 128 * nb), R("kb", 0, 128 * nb)
+    gsel(s_, kb, pk, A.is_equal, -1, 1)
+    gsel(s_, s_, pk, A.not_equal, 0, 1, fill=-2 * K)
+    lin(R("Sn", 0, 128 * nb), s_, -1, 0)
+    mset(R("F", 1024, 4112), 255.0)
+    for h in (16, 8, 4):
+        mset(R("mk%d" % h, 0, cfg["gp"]), 0.0); mset(R("mk%d" % h, 0, cfg["gp"], h), 255.0)
 
     def late_consts():
-        ts(R("cw0", 2048, 3072), R("cw0", 2048, 3072), -255.0, None, A.add)
-        for k in (1, 2): local("sync", R("cw%d" % k, 2560, 3072), R("cw0", 2560, 3072))
-        for k in range(NMP): local("sync", R("mp%d" % k), R("m1"))
-        mset(R("Z"), 0.0)
-        mset(R("of"), 1.0)
-        gsel(R("tf"), R("of"), [[-16, 8], [0, 16]], A.is_ge, 0, 1)
-        gsel(R("blf"), R("tf"), [[16, 8], [0, 16]], A.is_ge, 15, -1)
-        gsel(matf(16), R("of"), [[-16, 8], [8, 2], [-1, 8]], A.is_equal, -8, 1)
-        for q in range(16): gsel(matf(q), R("blf"), [[0, 8], [1, 16]], A.is_equal, -q, 0)
-        for i in range(16): scaled("D%d" % i, "I", 2.0 ** (15 - i))
-        tt(newmat("S1"), mat("I"), mat("sub"), A.subtract)
-        tt(newmat("Sn"), mat("sub"), mat("I"), A.subtract)
-        op([("pool", 0.2, lambda e: e.iota(T["ip"][:, 0:1], [[0, 1]], 0, 1))], [], [R("ip", 0, 1)])
-        for k, f in ((0, 2), (1, 4), (2, 16), (3, 256)):
-            ts(R("ip", 1 + k, 2 + k), R("ip", 0, 1), 1 << k, None, A.bitwise_and)
-            ts(R("pw", 1 + k, 2 + k), R("ip", 1 + k, 2 + k), -(f - 1) / float(1 << k), float(f), A.mult, A.add)
-        tt(R("pw", 5, 6), R("pw", 1, 2), R("pw", 2, 3), A.mult)
-        tt(R("pw", 6, 7), R("pw", 3, 4), R("pw", 4, 5), A.mult)
-        tt(R("pw", 0, 1), R("pw", 5, 6), R("pw", 6, 7), A.mult)
-        for l in range(1, 5):
-            a = 512 * (l - 1) + (8 if l == 4 else 0)
-            ts(R("lt0", a, a + 512), R("raw", 512 * l - 512, 512 * l), -1.0, 4096.0, A.mult, A.add)
-            if l == 1: ts(R("lt1", a, a + 512), R("raw", 0, 512), -1.0, 4096.0, A.mult, A.add)
-        for z in ("lt0", "lt1"): mset(R(z, 1536, 1544), 0.0)
+        u_ = R("U", 0, 128 * nb)
+        gsel(u_, kb, pk, A.is_ge, 0, 1)
+        gsel(u_, u_, [[2, nb], [16, 8], [0, 16]], A.is_ge, 1, -1)
+        iota(R("mo", 0, 128, 2), [[6 * KC, 64]], 2 * KC, -3 * KC)
+        iota(R("mo", 1, 128, 2), [[-6 * KC, 64]], -2 * KC, 3 * KC)
+        iota(R("mo", 128, 256, 2), [[2, 64]], 1, -1)
+        iota(R("mo", 129, 256, 2), [[-4, 64]], -1, 2)
+        gsel(R("mo"), R("mo"), [[0, 2], [-2, 64], [0, 2]], A.is_ge, 0, 1)
+        gsel(R("mo"), R("mo"), [[0, 2], [2, 64], [0, 2]], A.is_ge, 1, -1)
+        iota(R("tri"), [[2, 16], [0, 8], [-2, 16]], 1, 0)
+        gsel(R("tri"), R("tri"), [[-1, 16], [0, 8], [1, 16]], A.is_ge, 0, 0)
+        gsel(R("tri"), R("tri"), [[0, 16], [-16, 8], [0, 16]], A.is_equal, 0, 1)
+        iota(R("ip", 0, 1), [[0, 1]], 0, 1)
+        ts(R("ip", 4, 5), R("ip", 0, 1), 1, None, A.bitwise_and)
+        for k, (a, b) in enumerate(((6.0, 2.0), (2.0, 6.0), (32769.0, 0.0))): ts(R("col", k, k + 1), R("ip", 4, 5), a, b, A.mult, A.add)
+        lin(Pn, P, -1, 0); lin(P2, P, 2048, 0); lin(I4, I, 4096, 0)
+        mset(R("Z", 0, 1024), 0.0); mset(R("Z", 4096, 4112), 0.0)
+        ts(R("Lw", 0, 512), R("raw", 0, 512), -2048.0, None, A.add)
+        for l in (3, 2, 1, 0):
+            ts(R("zk", 512 * l, 512 * l + 512), R("x", 512 * l, 512 * l + 512), 0.0, K, A.is_equal, A.mult)
+            for z in range(2): ts(R("po", 128 * z + 32 * l, 128 * z + 32 * l + 32), R("rpm", 128 * z + 32 * l, 128 * z + 32 * l + 32), -512.0 * (l + 1), None, A.add)
 
-    def thr(tab, n0, w, sign, both=True):
-        b = bank("m")
-        mm([(R(b, 0, 2 * w), mat("I"), R(tab, 2 * n0, 2 * n0 + 2 * w), True, not both)])
-        if both:
-            s_ = R("st", n0, n0 + w)
-            p, m = (mat("I5"), mat("In5")) if sign > 0 else (mat("In5"), mat("I5"))
-            return b, lambda: mm([(R(b, 0, w), p, s_, False, False), (R(b, w, 2 * w), m, s_, False, True)])
-        return b, None
-
-    def counts(w, first, second, t):
-        b = bank("m")
-        mm([(R(b, 0, w), mat(first), R("ones", 0, w), True, False)])
-        mm([(R(b, 0, w), mat(second), R(t, 0, w), False, True), (R(b, w, 2 * w), mat("B"), R(t, w, 2 * w), True, True)])
-        return b
-
-    def tests(rnd, n0, w, osrc):
-        n1 = n0 + w
-        nb, fin = thr("xm", n0, w, 1, rnd > 0)
-        if fin: fin()
-        t = pick("tt", 3)
-        tt(R(t, 0, w), osrc, R(nb, 0, w), A.is_lt)
-        tt(R(t, w, 2 * w), osrc, R(nb, w, 2 * w), A.is_lt)
-        cb = counts(w, "Bn16", "B2", t)
-        v = R(pick("vv", 3), 0, w)
-        c = R(cb, w, 2 * w)
-        flex(v, c, act(v, c, AF.Relu, bias=1.0, scale=-1.0), vts(v, c, 0.0, None, A.is_equal))
-        n2, fin = thr("xm", n0, w, 1)
-        tt(R("st", n0, n1), v, R(cb, 0, w), A.min)
-        fin()
-        return n2
-
-    def edges(n0, w, n2):
-        n1 = n0 + w
-        tt(R("F", 2 * n0, 2 * n1, 2), R("o", n0, n1), R(n2, 0, w), A.max)
-        tt(R("F", 2 * n0 + 1, 2 * n1, 2), R("o", n0, n1), R(n2, w, 2 * w), A.max)
-
-    def plus(a, b): flex(a, b, act(a, b, AF.Copy, bias=255.0), vts(a, b, 255.0, None, A.add), kind="y")
-
-    def out_s(lo, hi):
-        plus(R("yo", lo, hi), R("o", lo, hi)); store("sync", "ys", lo, hi, R("yo", lo, hi))
-
-    def down0(rnd):
-        ph[0] = "%d down0" % rnd
-        for n0, w in CH[0]:
-            n1 = n0 + w
-            if rnd == 0: ts(R("o", n0, n1), R("sf", n0, n1), -255.0, None, A.add)
+    def lay(m, col, w, L, Tn, c):
+        parts(m)
+        b = bank(w)
+        n = w // m
+        for t in range(m):
+            o_ = sub(b, t * n, t * n + n)
+            if m == 1: lst = [(o_, I, L)] + ([(o_, P, Tn)] if Tn else [])
             else:
-                w_, z = R(pick("ww", 3), 0, w), R(pick("bb", 3), 0, w)
-                ts(w_, R("st", n0, n1), 0.0, None, A.is_equal)
-                tt(z, R("as%d" % rnd, n0, n1), w_, A.mult)
-                tt(R("o", n0, n1), z, R("ko", n0, n1), A.add)
-            edges(n0, w, tests(rnd, n0, w, R("o", n0, n1)))
-        if rnd == 2: out_s(0, 512)
+                lst = [(o_, move(m, t, s), sub(L, s, w, m)) for s in range(m)]
+                if Tn: lst += [(o_, move(m, (t + m // 2) % m, s), sub(Tn, s, w, m)) for s in range(m)]
+            mm(lst)
+        ts(R("off", col, col + w), b, c, None, A.add)
 
-    def pieces(rnd, col, n0, w, so):
-        for p in range(0, w, PW):
-            gb = R(pick("g", NG))
-            gather(gb, R("F", 0, 4097), R("off", col + p, col + p + PW), True)
-            if n0 is None or rnd == 0: m_ = R("m1")
+    def first_lists(l, rnd):
+        a = 512 * (l - 1)
+        if rnd == 0: ts(R("Lh", a, a + 512), R("raw", a, a + 512), -2048.0, None, A.add)
+        for k, c, w in chunks(l):
+            m = cfg["m"][rnd, l][k]
+            if m == 1: copy(R("off", ocol(rnd, l) + c, ocol(rnd, l) + c + w), R("raw", a + c, a + c + w))
+            else: lay(m, ocol(rnd, l) + c, w, R("Lh", a + c, a + c + w), None, 2048.0)
+
+    def state(forms, n0, w, srcs, neg, old, new, cmp, after):
+        cb = bank(BS)
+        x_ = R("x", n0, n0 + w)
+        first = True
+        if old:
+            mm([(cb, Mo, old)], stop=False, after=[after]); first = False
+        for z in range(2):
+            b, t = bank(w), pick("ta" if z == 0 else "tb", 3, w)
+            if forms[z] == "v":
+                mm([(b, (I, P)[z], x_)], after=[after])
+                tt(t, srcs[z], b, A.is_lt)
             else:
-                mp = pick("mp", NMP)
-                ts(R(mp, 15, PW * 16, 16), R("st", n0 + p, n0 + p + PW), 0.0, -1.0, A.is_equal, A.mult)
-                m_ = R(mp)
-            scan(R(so, p * 16, (p + PW) * 16), gb, m_)
+                mm([(b, (I, P)[z], x_)], stop=False, after=[after])
+                mm([(b, In, srcs[z])], start=False)
+                relu(t, b)
+            mm([(cb, row(2 * j + z, neg), sub(t, j * BS, j * BS + BS)) for j in range(w // BS)], start=first, stop=z == 1)
+            first = False
+        return ts(new, cb, 0.0, None, cmp, kind="i")
+
+    def sides(tab, n0, w, t, names, after=None):
+        out = []
+        for z in range(2):
+            b = bank(w)
+            mm([(b, (I, P)[z], R(tab, n0, n0 + w))] + spread(b, names[z], t), after=[after])
+            out.append(b)
+        return out
+
+    def least(rnd, l, k, c, w):
+        m = cfg["m"][rnd, l][k]
+        h, so = 16 // m, pick("so", NSO)
+        wp = min(w, cfg["gp"] * m // 16)
+        for j in range(0, w, wp):
+            v = min(wp, w - j)
+            gb = pick("g", NG, v * h)
+            for t in range(m):
+                a = ocol(rnd, l) + c + (t * w + j) // m
+                i = (gmin if t else gather)(gb, R("F", 0, 4097), R("off", a, a + v // m))
+                if t == 0: g0 = i
+            scan(sub(so, j * h, (j + v) * h), R("mk%d" % h, 0, v * h), gb)
+        return sub(so, h - 1, w * h, h), g0, i
 
     def down(rnd, l):
-        ph[0] = "%d down%d" % (rnd, l)
+        ph[0] = "%dD%d" % (rnd, l)
         todo = []
-        for n0, w in CH[l]:
-            n1 = n0 + w
-            so = pick("so", NSO)
-            pieces(rnd, n0 - 512, n0, w, so)
-            last_ = R(so, 15, w * 16, 16)
-            o_ = R("o", n0, n1)
-            todo.append((n0, w, tests(rnd, n0, w, last_)))
-            if rnd == 0: fcopy(o_, last_)
-            else: tt(o_, last_, R("ko", n0, n1), A.add)
-        for z in todo: edges(*z)
-        if rnd == 2: out_s(512 * l, 512 * l + 512)
+        for k, c, w in chunks(l):
+            n0 = 512 * l + c
+            o_ = R("o", n0, n0 + w)
+            g0 = gl = None
+            if l: src, g0, gl = least(rnd, l, k, c, w)
+            else: src = R("as%d" % rnd, c, c + w) if rnd else o_
+            if l == 0 and rnd: g0 = lastup[k]
+            state(cfg["td"], n0, w, (src, src), True, tile(l, k, 2) if rnd else None, tile(l, k, 0), A.is_ge, g0)
+            if rnd:
+                b = bank(w)
+                mm([(b, I, src)] + spread(b, "U", tile(l, k, 2)))
+                tt(o_, b, R("kx", n0, n0 + w), A.min)
+            elif l: fcopy(o_, src, kind="c")
+            todo.append((k, n0, w, o_ if rnd else src))
+        for k, n0, w, src in todo:
+            for z, b in enumerate(sides("x", n0, w, tile(l, k, 0), ("S", "Sn"), gl)):
+                tt(R("F", 2 * n0 + z, 2 * n0 + 2 * w, 2), src, b, A.max, kind="e")
+        if rnd == 2: store("ys", 512 * l, 512 * l + 512, R("o", 512 * l, 512 * l + 512))
 
     nremote = [0]
 
@@ -340,182 +343,225 @@ def build(T, rank, topo, core):
         d = T.cores[to % 4]
         rid, pid = topo.addr(d)[:2]
         mask = sum(1 << e for e in topo.engines(core, d)[:8])
-        i = op([("pool", 1.0, lambda e: e.remote_dma(ap(dst), ap(src), T.sem["ra%d" % k], T.sem["la%d" % k], pid, rid, mask))], [src], [], sem=("la%d" % k, 8))
-        j = op([(None, 5.0, None)], [], [dst], sem=("ra%d" % k, 8))
-        ops[j]["after"] = i
+        i = op([("pool", (0, 0, 0, 1.0), lambda e: e.remote_dma(ap(dst), ap(src), T.sem["ra%d" % k], T.sem["la%d" % k], pid, rid, mask))], [src], [], sem=("la%d" % k, 8), kind="r")
+        op([(None, (0, 0, 0, 4.0), None)], [], [dst], sem=("ra%d" % k, 8), after=[i], kind="a")
 
     def ghosts(rnd):
-        ph[0] = "%d ghosts" % rnd
-        for c in range(0, 512, CWM):
-            so = pick("so", NSO)
-            pieces(rnd, 1536 + c, None, CWM, so)
-            fcopy(R("o", 2048 + c, 2048 + c + CWM), R(so, 15, CWM * 16, 16))
+        ph[0] = "%dG" % rnd
+        for k, c, w in chunks(4):
+            fcopy(R("o", 2048 + c, 2048 + c + w), least(rnd, 4, k, c, w)[0], kind="c")
         if rnd < 2: send(R("o", 2048, 2560), R("as%d" % (rnd + 1)), rank + 1)
-        else: out_s(2048, 2560)
+        else: store("ys", 2048, 2560, R("o", 2048, 2560))
+
+    lastup = {}
 
     def up(rnd, l):
-        ph[0] = "%d up%d" % (rnd, l)
+        ph[0] = "%dU%d" % (rnd, l)
         cw = "cw%d" % rnd
-        for n0, w in CH[l]:
-            n1, c = n0 + w, n0 // 8
-            ab = pick("ab", 3); a_, b_ = R(ab, 0, w), R(ab, w, 2 * w)
-            gather(R(ab, 0, 2 * w), R(cw, 512 * l + 512, 3072), R("po", c, c + w // 8), False)
-            xb, fin = thr("xm", n0, w, -1)
-            fin()
-            t = pick("tt", 3)
-            tt(R(t, 0, 2 * w), R(ab, 0, 2 * w), R(xb, 0, 2 * w), A.is_lt)
-            fb = counts(w, "B16", "Bn2", t)
-            v = R(pick("vv", 3), 0, w); f_ = R(fb, w, 2 * w)
-            flex(v, f_, act(v, f_, AF.Sign), vts(v, f_, 1.0, None, A.min))
-            tb, fin = thr("zx", n0, w, -1)
-            tt(R("st", n0, n1), v, R(fb, 0, w), A.min)
-            fin()
-            m_ = R(pick("mm", 3), 0, w)
-            tt(R(tb, 0, w), a_, R(tb, 0, w), A.min)
-            tt(m_, b_, R(tb, w, 2 * w), A.min)
-            tt(R(cw, n0, n1), m_, R(tb, 0, w), A.max)
-            if rnd < 2:
-                if l:
-                    ts(R("Z", 2 * n0, 2 * n1, 2), R("st", n0, n1), 0.0, None, A.is_lt, kind="z")
-                    zb = R("Z", 2 * n0 + 1, 2 * n1, 2)
-                    flex(zb, R("st", n0, n1), act(zb, R("st", n0, n1), AF.Relu), vts(zb, R("st", n0, n1), 0.0, None, A.is_gt), kind="z")
-                z = R(pick("bb", 3), 0, w)
-                ts(z, R("st", n0, n1), 0.0, None, A.not_equal, kind="k")
-                tt(R("ko", n0, n1), R("o", n0, n1), z, A.mult, kind="k")
-            else:
-                plus(R("ko", n0, n1), R(cw, n0, n1)); store("sync", "yc", n0, n1, R("ko", n0, n1))
+        for k, c, w in chunks(l):
+            n0 = 512 * l + c
+            ab = (pick("ga", 3, w), pick("gb", 3, w))
+            gs = [gather(ab[z], R(cw, 512 * l + 512, 3072), R("po", 128 * z + n0 // 16, 128 * z + (n0 + w) // 16)) for z in range(2)]
+            lastup[k] = state(cfg["tu"], n0, w, ab, False, tile(l, k, 0), tile(l, k, 1), A.is_gt, gs[0])
+            ba, bb = sides("zk", n0, w, tile(l, k, 1), ("Sn", "S"))
+            q = pick("qq", 3, w)
+            tt(ba, ab[0], ba, A.min)
+            tt(q, ab[1], bb, A.min)
+            tt(R(cw, n0, n0 + w), q, ba, A.max)
+            if rnd == 2:
+                store("yc", n0, n0 + w, R(cw, n0, n0 + w))
+                continue
+            b, cl = bank(BS), tile(l, k, 2)
+            mm([(b, Mc, tile(l, k, 1))])
+            relu(cl, b, kind="z")
+            if l:
+                b = bank(w)
+                for z in spread(b, "S", cl): mm([z])
+                za, zb = R("Z", 2 * n0, 2 * n0 + 2 * w, 2), R("Z", 2 * n0 + 1, 2 * n0 + 2 * w, 2)
+                flex(za, b, act(za, b, AF.Relu, scale=-0.5 / K), vts(za, b, 0.0, None, A.is_lt), kind="z")
+                flex(zb, b, act(zb, b, AF.Relu, scale=1 / K), vts(zb, b, 0.0, None, A.is_gt), kind="z")
+            b = bank(w)
+            mm([(b, In, R("o", n0, n0 + w))] + spread(b, "U", cl))
+            lin(R("kx", n0, n0 + w), b, -1, K, kind="k")
         if rnd < 2 and l == 0: send(R(cw, 0, 512), R("cw%d" % (rnd + 1), 2048, 2560), rank - 1)
 
-    def splice(k, l):
-        ph[0] = "%d splice%d" % (k + 1, l)
-        src, dst = ("lt0", "lt1") if k == 0 else ("lt1", "lt0")
-        for c in range(0, 512, SW):
-            w = SW
+    def splice(rnd, l):
+        ph[0] = "%dS%d" % (rnd, l)
+        for k, c, w in chunks(l):
             col = 512 * (l - 1) + c
-            lc = col + (8 if l == 4 else 0)
-            L = R(src, lc, lc + w)
-            mk = bank("s")
-            for p in range(0, w, PW):
-                fg = pick("fg", NFG)
-                gather(R(fg), R("Z", 0, 4097), R("off", col + p, col + p + PW), False)
-                for h in range(0, 16, 4): mm([(R(mk, p, p + PW), mat("D%d" % i), R(fg, i, PW * 16, 16), i == 0, i == 15) for i in range(h, h + 4)])
-            ge = R(pick("ge", 2))
-            ts(ge, R(mk, 0, w), R("pw", 0, 1), None, A.is_ge)
-            th = R(bank("s"), 0, w)
-            mm([(th, mat("S1"), ge, True, True)])
-            X = pick("X", 2)
-            tt(R(X), L, th, A.mult)
-            wr = R(bank("s"), 0, w // 16)
-            for h in range(0, 16, 4): mm([(wr, matf(q), R(X, q, w, 16), q == 0, q == 15) for q in range(h, h + 4)])
-            xi, xu = R(pick("xi", 2)), R(pick("xu", 2))
-            ts(xi, wr, -0.5, 1535.75, A.mult, A.add)
-            copy(xu, xi)
-            nt = R(bank("s"), 0, w)
-            mm([(nt, mat("B16"), R("ones", 0, w), True, False), (nt, mat("Sn"), ge, False, True)])
-            L1 = R(pick("L1", 2))
-            tt(L1, L, nt, A.mult)
-            tg = pick("Tg", 2)
-            gather(R(tg), R(src, 0, 1544), xu, False)
-            tp = bank("s")
-            for h in range(0, w, 128): mm([(R(tp, h, h + 128), matf(16), R(tg, h, h + 128), True, True)])
-            h = R(pick("hm", 2))
-            tp = R(tp, 0, w)
-            tt(h, L1, tp, A.min)
-            ht = R(bank("s"), 0, w)
-            mm([(ht, mat("B"), h, True, True)])
-            dl = R(pick("dl", 2))
-            tt(dl, tp, R(X), A.subtract)
-            flex(ht, ht, act(ht, ht, AF.Relu, bias=1.0, scale=-1.0), vts(ht, ht, 0.0, None, A.is_equal))
-            tt(ht, dl, ht, A.mult)
-            tt(R(dst, lc, lc + w), L, ht, A.add)
-            ts(R("off", col, col + w), R(dst, lc, lc + w), -1.0, 4096.0, A.mult, A.add)
+            L = R("Lh", col, col + w)
+            m = cfg["m"][rnd - 1, l][k]
+            h, fl = 16 // m, bank(w)
+            wp = min(w, cfg["fp"] * m // 16)
+            for j in range(0, w, wp):
+                v = min(wp, w - j)
+                for t in range(m):
+                    fg = pick("fg", NFG, v * h)
+                    a = col + (t * w + j) // m
+                    gather(fg, R("Z", 0, 4097), R("off", a, a + v // m))
+                    mm([(sub(fl, j, j + v), blk("tri", t * h + r), sub(fg, r, v * h, h)) for r in range(h)], start=t == 0, stop=t == m - 1)
+            th = pick("th", 3, w)
+            i = relu(th, fl)
+            X, b = pick("X", 3, w), bank(w)
+            mm([(b, I, L)], after=[i])
+            tt(X, th, b, A.mult)
+            b = bank(w // 16)
+            mm([(b, row(q), sub(X, q, w, 16)) for q in range(16)])
+            xi, xu = pick("xi", 3, w // 16), pick("xu", 3, w // 16)
+            ts(xi, b, 0.5, 511.75, A.mult, A.add, kind="i")
+            i = copy(xu, xi, kind="i")
+            tg = pick("Tg", 3, w)
+            win, add = (R("raw", 0, 1536), -2048.0) if rnd == 1 else (R("Lw"), 0.0)
+            op([("vector", (0, w, 1, 0), lambda e, tg=tg, xu=xu, win=win, add=add: e.tensor_scalar(ap(tg), ap(win).indirect(ap(xu)), add, None, op0=A.add))], [win, xu], [tg])
+            b, hm = bank(w), pick("hm", 3, w)
+            mm([(b, P, L), (b, Pn, X), (b, P2, th)], after=[i])
+            tt(hm, tg, b, A.max)
+            b = bank(BS)
+            mm([(b, row(2 * j + 1), sub(z, j * BS, j * BS + BS)) for z in (th, hm) for j in range(w // BS)])
+            ot = pick("ot", 3, 2 * BS)
+            ts(sub(ot, 0, BS), b, R("col", 2, 3), R("col", 0, 1), A.is_ge, A.mult, kind="i")
+            ts(sub(ot, BS, 2 * BS), b, R("col", 2, 3), R("col", 1, 2), A.is_ge, A.mult, kind="i")
+            tk, lk, b = pick("Tk", 3, w), pick("Lk", 3, w), bank(w)
+            for z in spread(b, "Sn", sub(ot, 0, BS)): mm([z])
+            tt(tk, tg, b, A.max)
+            b = bank(w)
+            mm([(b, I4, th)] + spread(b, "S", sub(ot, BS, 2 * BS)))
+            tt(lk, L, b, A.max)
+            lay(cfg["m"][rnd, l][k], col, w, lk, tk, 0.0)
+            if rnd == 1:
+                b = bank(w)
+                mm([(b, I, lk), (b, P, tk)])
+                ts(L, b, -2048.0, None, A.add, kind="l")
+                if l < 4: lin(R("Lw", col, col + w), b, 1, -2048, kind="l")
 
-    pair(0)
-    down0(0)
+    down(0, 0)
     for l in (1, 2, 3):
         ph[0] = "init"
-        offs(l); pair(l)
+        first_lists(l, 0)
         down(0, l)
-    ph[0] = "init"
-    offs(4)
-    for l in (3, 2, 1, 0): zero(l)
-    for l in range(4):
-        for n0, w in CH[l]:
-            for z in range(2): ts(R("po", n0 // 8 + z * w // 16, n0 // 8 + (z + 1) * w // 16), R("rpm", 128 * z + n0 // 16, 128 * z + (n0 + w) // 16), -512.0 * (l + 1), None, A.add)
     ph[0] = "late"
+    first_lists(4, 0)
     late_consts()
+    if ocol(1, 1): first_lists(1, 1)
     for rnd in range(3):
         if rnd:
-            for l in (2, 3, 4): splice(rnd - 1, l)
-            down0(rnd)
-            for l in (1, 2, 3): down(rnd, l)
+            for l in (2, 3, 4): splice(rnd, l)
+            for l in range(4): down(rnd, l)
         ghosts(rnd)
         for l in (3, 2, 1, 0): up(rnd, l)
     return ops
 
 
-def flexes(ops): return [i for i, o in enumerate(ops) if len(o["opts"]) == 2]
+MODELS = ((1.0, 1.1, 0.03, 0.1), (1.1, 1.55, 0.05, 0.12), (1.3, 2.0, 0.06, 0.15))
+QALL = (None, "vector", "scalar", "tensor", "pool", "sync")
 
 
-def assign_of(ops, s):
-    fl = flexes(ops)
-    a = [o["opts"][0][0] for o in ops]
-    for k, i in enumerate(fl): a[i] = "vector" if (s[k] == "1" if s else k % 3 == 0) else "scalar"
-    return a
+def cost(q, c, md):
+    if q == "tensor": return c[0] * 0.00045 * md[0] + c[2] * 0.015
+    return ((max(64, c[0]) if c[0] else 0) + c[1] * md[1]) * 0.00083 * md[0] + c[2] * md[2] + c[3]
 
 
-def plan(ops, asg, offs):
+def plan(ops, md, offs, look=0.5, vb=0.0):
     n = len(ops)
-    us = [[x[1] for x in o["opts"] if x[0] == asg[i]][0] for i, o in enumerate(ops)]
-    lat = [2.5 if o["sem"] else 0.0 for o in ops]
+    us = [{x[0]: cost(x[0], x[1], md) for x in o["opts"]} for o in ops]
+    lat = [(2.2 if o["sem"] and None not in o["qs"] else 0.0) + md[3] for o in ops]
     succ = [[] for _ in range(n)]
     left = [0] * n
+    users = {}
     for i, o in enumerate(ops):
-        p = set(o["deps"])
-        if "after" in o: p.add(o["after"])
+        p = set(o["deps"]) | set(o["after"])
         left[i] = len(p)
         for j in p: succ[j].append(i)
+        for b in o["banks"]: users.setdefault(b, []).append(i)
     pr = [0.0] * n
-    for i in range(n - 1, -1, -1): pr[i] = max([pr[s] for s in succ[i]] or [0.0]) + WAKE + us[i] + lat[i]
+    for i in range(n - 1, -1, -1): pr[i] = max([pr[s] for s in succ[i]] or [0.0]) + lat[i] + min(us[i].values())
     pr = [pr[i] + offs.get(ops[i]["name"], 0.0) for i in range(n)]
-    rt = [0.0] * n
-    fin = [0.0] * n
-    free = {}
-    ready = {}
+    rt, fin, asg = [0.0] * n, [0.0] * n, [None] * n
+    free = {q: 0.0 for q in QALL}
+    ready = {q: [] for q in QALL}
     for i in range(n):
-        if not left[i]: ready.setdefault(asg[i], []).append(i)
+        if not left[i]:
+            for q in us[i]: ready[q].append(i)
+    phys, prev, held = {}, {}, [None] * 8
+    bfree = [0.0] * 8
+    togo = {b: len(u) for b, u in users.items()}
     order = []
     while len(order) < n:
-        bt, bq = None, None
-        for q in (None, "vector", "scalar", "tensor", "pool", "sync"):
-            if ready.get(q):
-                t = max(min(rt[i] for i in ready[q]), free.get(q, 0.0))
-                if bt is None or t < bt: bt, bq = t, q
-        i = min((-pr[i], i) for i in ready[bq] if rt[i] <= bt + 1e-9)[1]
-        ready[bq].remove(i)
-        f = bt + us[i]
-        if bq is not None:
-            free[bq] = f
-            f += lat[i]
-        fin[i] = f
+        bt, bq, bc = None, None, None
+        fb = [k for k in range(8) if held[k] is None or not togo[held[k]]]
+        tb = min([bfree[k] for k in fb] or [1e9])
+        for q in QALL:
+            c = ready[q]
+            if q == "tensor": c = [(max(rt[i], tb) if any(b not in phys for b in ops[i]["banks"]) else rt[i], i) for i in c]
+            else: c = [(rt[i], i) for i in c]
+            if c:
+                t = max(min(c)[0], free[q])
+                if bt is None or t < bt: bt, bq, bc = t, q, c
+        if bt is None or bt >= 1e9: return None
+        bias = vb if bq == "vector" else 0.0
+        key = lambda z: pr[z[1]] - (bias if len(us[z[1]]) > 1 else 0.0)
+        now = [z for z in bc if z[0] <= bt + 1e-9]
+        best = max(now, key=key)
+        soon = [z for z in bc if z[0] > bt + 1e-9 and key(z) > key(best) and z[0] < bt + look * us[best[1]][bq] and len(us[z[1]]) == 1]
+        if soon:
+            u = min(soon)
+            fit = [z for z in now if bt + us[z[1]][bq] <= u[0] + 0.1]
+            best = max(fit, key=key) if fit else u
+        t, i = max(bt, best[0]), best[1]
+        for q in us[i]: ready[q].remove(i)
+        for b in ops[i]["banks"]:
+            if b not in phys:
+                k = min((k for k in fb if bfree[k] <= t + 1e-9), key=lambda k: bfree[k])
+                if held[k] is not None: prev[i] = users[held[k]]
+                phys[b], held[k] = k, b
+        f = t + us[i][bq]
+        if bq is not None: free[bq] = f
+        asg[i], fin[i] = bq, f + lat[i] - md[3]
         order.append(i)
+        for b in ops[i]["banks"]:
+            togo[b] -= 1
+            bfree[phys[b]] = max(bfree[phys[b]], f + md[3])
         for j in succ[i]:
-            rt[j] = max(rt[j], f + WAKE)
+            hard = j in range(n) and i in ops[j]["deps"]
+            d = f + lat[i] if (hard or ops[j]["qs"] == {None}) else t
+            if hard and ops[j]["deps"][i] == "acc": d = f
+            rt[j] = max(rt[j], d)
             left[j] -= 1
-            if not left[j]: ready.setdefault(asg[j], []).append(j)
-    return order, max(fin), fin
+            if not left[j]:
+                for q in us[j]: ready[q].append(j)
+    return order, asg, phys, prev, max(fin), fin
+
+
+def replay(ops, pl, md):
+    order, asg, phys, prev = pl[:4]
+    fin, free = {}, {}
+    for i in order:
+        o, q = ops[i], asg[i]
+        t = free.get(q, 0.0) if q is not None else 0.0
+        for j, k in o["deps"].items():
+            t = max(t, fin[j] + (0.0 if asg[j] == q and k != "w" and not ops[j]["sem"] else md[3]))
+        for j in prev.get(i, ()): t = max(t, fin[j] + (0.0 if asg[j] == q else md[3]))
+        if q is None: t = max([t] + [fin[j] - 2.2 for j in o["after"]])
+        f = t + [cost(q, x[1], md) for x in o["opts"] if x[0] == q][0]
+        free[q] = f
+        fin[i] = f + (2.2 if o["sem"] and q is not None else 0.0)
+    return max(fin.values())
+
+
+OFFS = {}
+LOOK, VB = 0.5, 10.0
 
 
 def rank_program(g, core, T, topo):
     rank = T.rank_of(core)
     if rank is None:
         return
-    ops = build(T, rank, topo, core)
-    if "p" not in PLAN:
-        asg = assign_of(ops, ASG)
-        order = plan(ops, asg, OFFS)[0]
-        PLAN["p"] = (order, asg, {j: k for k, j in enumerate(order)})
-    order, asg, pos = PLAN["p"]
+    phys = {}
+    ops = build(T, rank, topo, core, phys, CFG)
+    if "p" not in PLAN: PLAN["p"] = plan(ops, MODELS[1], OFFS, LOOK, VB)
+    order, asg, ph, prev = PLAN["p"][:4]
+    phys.update(ph)
+    pos = {j: k for k, j in enumerate(order)}
     eng = {"vector": g.vector, "scalar": g.scalar, "tensor": g.tensor, "pool": g, "sync": g.sync}
     count = {}
     done = {}
@@ -527,7 +573,9 @@ def rank_program(g, core, T, topo):
             done[i] = o["sem"]; clock[i] = {}
             continue
         need = {}
-        for j, kind in o["deps"].items():
+        deps = dict(o["deps"])
+        for j in prev.get(i, ()): deps.setdefault(j, "ord")
+        for j, kind in deps.items():
             if asg[j] == q and kind != "w" and not ops[j]["sem"] and not o["sem"]: continue
             s, v = done[j]
             if need.get(s, (0, 0))[0] < v: need[s] = (v, j)

@@ -1,44 +1,49 @@
 from concourse.mybir import AluOpType as A, ActivationFunctionType as AF
 
-BS = 64
 K = 512.0
 KC = 4096
 CFG = {
-    "ch": {0: (256, 256), 1: (256, 256), 2: (256, 256), 3: (256, 256), 4: (256, 256)},
-    "m": {(0, 1): (2, 2), (0, 2): (1, 2), (0, 3): (1, 2), (0, 4): (1, 4),
-          (1, 1): (2, 2), (1, 2): (2, 1), (1, 3): (1, 4), (1, 4): (4, 2),
-          (2, 1): (2, 2), (2, 2): (2, 1), (2, 3): (1, 4), (2, 4): (4, 2)},
-    "gp": 1024, "fp": 1024, "td": "vf", "tu": "vf",
+    "bs": 128,
+    "dch": {0: (256, 256), 1: (256, 256), 2: (256, 256), 3: (256, 256), 4: (256, 256)},
+    "uch": {0: (256, 256), 1: (512,), 2: (512,), 3: (512,)},
+    "sw": {2: 1, 3: 1, 4: 1},
+    "m": {(0, 1): (2, 1), (0, 2): (1, 2), (0, 3): (1, 2), (0, 4): (1, 2),
+          (1, 1): (2, 2), (1, 2): (2, 2), (1, 3): (1, 2), (1, 4): (1, 2),
+          (2, 1): (2, 2), (2, 2): (2, 2), (2, 3): (1, 2), (2, 4): (1, 2)},
+    "gp": 1024, "fp": 1024, "td": ("ff", "ff", "ff"), "tu": ("ff", "ff", "ff"), "sig": 0, "sp": 1024, "gg": 1024, "back": 0.0, "cp": 1, "ew": ("cccc", "cccc", "cccc"), "pre": 1, "keep": 4, "far": 3.0, "tries": 5000, "cu": ("vvvv", "vvvv", "vvvv"),
+    "pin": {"1S3g": "s", "1S4g": "s", "2S3g": "s", "2S4g": "s"}, "offs": {}, "look": 0.3, "vb": 10.0, "it": 2, "gap": 3.0,
 }
-NB = 4
-NG, NSO, NFG = 6, 3, 4
+NG, NSO, NFG = 6, 3, 3
 SCRATCH = {
-    "raw": ("sbuf", [128, 2048], "int32"), "rpm": ("sbuf", [128, 256], "int32"), "po": ("sbuf", [128, 256], "uint16"),
-    "off": ("sbuf", [128, 2560], "uint16"), "Lh": ("sbuf", [128, 2048], "float16"), "Lw": ("sbuf", [128, 1536], "float32"),
+    "raw": ("sbuf", [128, 2056], "int32"), "rpm": ("sbuf", [128, 256], "int32"), "po": ("sbuf", [128, 256], "uint16"),
+    "off": ("sbuf", [128, 2560], "uint16"), "Lh": ("sbuf", [128, 2048], "float16"), "Lw": ("sbuf", [128, 1544], "float32"),
     "F": ("sbuf", [128, 4112], "bfloat16"), "Z": ("sbuf", [128, 4112], "bfloat16"),
     "x": ("sbuf", [128, 2048], "bfloat16"), "zk": ("sbuf", [128, 2048], "bfloat16"),
     "o": ("sbuf", [128, 2560], "bfloat16"), "kx": ("sbuf", [128, 2048], "bfloat16"),
     "as1": ("sbuf", [128, 512], "bfloat16"), "as2": ("sbuf", [128, 512], "bfloat16"),
-    "ob": ("sbuf", [128, 128], "bfloat16"), "kb": ("sbuf", [128, 1024], "bfloat16"), "mb": ("sbuf", [128, 128 * 6], "bfloat16"),
-    "iw": ("sbuf", [128, 152 * 7], "bfloat16"), "W": ("sbuf", [128, 288], "bfloat16"), "tri": ("sbuf", [128, 2048], "bfloat16"),
+    "ob": ("sbuf", [128, 128], "bfloat16"), "kb": ("sbuf", [128, 512], "bfloat16"), "mb": ("sbuf", [128, 128 * 5], "bfloat16"),
+    "iw": ("sbuf", [128, 152 * 7], "bfloat16"), "W": ("sbuf", [128, 720], "bfloat16"), "tri": ("sbuf", [128, 2048], "bfloat16"),
     "S": ("sbuf", [128, 1024], "bfloat16"), "Sn": ("sbuf", [128, 1024], "bfloat16"), "U": ("sbuf", [128, 1024], "bfloat16"),
-    "mo": ("sbuf", [128, 256], "bfloat16"), "tl": ("sbuf", [128, 4096], "bfloat16"),
+    "Ra": ("sbuf", [128, 1024], "bfloat16"), "Rb": ("sbuf", [128, 1024], "bfloat16"), "rp2": ("sbuf", [128, 512], "int32"),
+    "mo": ("sbuf", [128, 256 + 128 * 10], "bfloat16"), "tl": ("sbuf", [128, 4608], "bfloat16"),
     "ip": ("sbuf", [128, 8], "int32"), "col": ("sbuf", [128, 8], "float32"),
 }
 for _k in (4, 8, 16): SCRATCH["mk%d" % _k] = ("sbuf", [128, 2048], "bfloat16")
 for _k in range(3): SCRATCH["cw%d" % _k] = ("sbuf", [128, 3072], "bfloat16")
 for _k in range(NG): SCRATCH["g%d" % _k] = ("sbuf", [128, 2048], "bfloat16")
-for _k in range(NFG): SCRATCH["fg%d" % _k] = ("sbuf", [128, 2048], "bfloat16")
+for _k in range(NFG): SCRATCH["fg%d" % _k] = ("sbuf", [128, 4096], "bfloat16")
 for _k in range(NSO): SCRATCH["so%d" % _k] = ("sbuf", [128, 4096], "bfloat16")
 for _k in range(3):
-    for _n in ("ga", "gb", "ta", "tb", "qq", "th", "ot"): SCRATCH["%s%d" % (_n, _k)] = ("sbuf", [128, 512], "bfloat16")
+    for _n in ("ga", "gb", "ta", "tb"): SCRATCH["%s%d" % (_n, _k)] = ("sbuf", [128, 512], "bfloat16")
+for _k in range(2):
+    for _n in ("qq", "th", "ot"): SCRATCH["%s%d" % (_n, _k)] = ("sbuf", [128, 512], "bfloat16")
     for _n in ("X", "Tg", "hm", "Tk", "Lk"): SCRATCH["%s%d" % (_n, _k)] = ("sbuf", [128, 512], "float16")
     SCRATCH["xi%d" % _k] = ("sbuf", [128, 32], "int32")
     SCRATCH["xu%d" % _k] = ("sbuf", [128, 32], "uint16")
 for _k in range(8): SCRATCH["ps%d" % _k] = ("psum", [128, 512], "float32")
 NDMA = 50
 QS = ("vector", "scalar", "tensor", "pool")
-SEMAPHORES = ["q_" + q for q in QS] + ["d%d" % k for k in range(NDMA)] + ["ra%d" % k for k in range(4)] + ["la%d" % k for k in range(4)]
+SEMAPHORES = ["q_" + q for q in QS] + ["d%d" % k for k in range(NDMA)] + ["ra%d" % k for k in range(8)] + ["la%d" % k for k in range(8)]
 
 SZ = {"float32": 4, "int32": 4, "bfloat16": 2, "uint16": 2, "float16": 2}
 PLAN = {}
@@ -55,6 +60,8 @@ def build(T, rank, topo, core, phys, cfg):
     ndma = [0]
     ph = ["init"]
     rot = {}
+    BS = cfg["bs"]
+    nb = 512 // BS
 
     def isps(r): return r[0][0] == "#"
 
@@ -75,6 +82,8 @@ def build(T, rank, topo, core, phys, cfg):
     def op(opts, rd, wr, sem=None, kind="v", after=()):
         i = len(ops)
         deps = {}
+        pin = cfg["pin"].get(ph[0] + kind)
+        if pin and len(opts) > 1: opts = [o for o in opts if o[0][0] == pin]
         qs = set(o[0] for o in opts)
         banks = set()
         for w, lst in ((0, rd), (1, wr)):
@@ -103,6 +112,7 @@ def build(T, rank, topo, core, phys, cfg):
 
     def pick(name, n, w=None):
         k = rot.get(name, 0); rot[name] = k + 1
+        assert w is None or w <= SCRATCH[name + "0"][1][1]
         return R("%s%d" % (name, k % n), 0, w)
 
     def half(*rs): return 0.5 if all(sz(r) == 2 for r in rs) else 1
@@ -147,6 +157,12 @@ def build(T, rank, topo, core, phys, cfg):
                 if z not in y: y.append(z)
         return op([("tensor", (sum(max(64, n_of(z[0])) for z in lst), 0, len(lst), 0), fn)], rd, wr, kind="t", **k)
 
+    def mms(lst, **k):
+        def fn(e):
+            for (o_, l_, r_) in lst: ins = e.matmul(ap(o_), ap(l_), ap(r_), True, True)
+            return ins
+        return op([("tensor", (sum(max(64, n_of(z[0])) for z in lst), 0, len(lst), 0), fn)], [z[1] for z in lst] + [z[2] for z in lst], [z[0] for z in lst], kind="t", **k)
+
     def gather(out, win, offs_, **k):
         c = (0, n_of(out), 1, 0)
         return op([("scalar", c, lambda e: e.activation(ap(out), ap(win).indirect(ap(offs_)), AF.Copy)),
@@ -173,11 +189,18 @@ def build(T, rank, topo, core, phys, cfg):
         kw = {} if SCRATCH[out[0]][2] == "int32" else {"allow_small_or_imprecise_dtypes": True}
         return op([("pool", (2 * n_of(out), 0, 0, 0.18), lambda e: e.iota(ap(out), pattern, base, cm, **kw))], [], [out], kind="p")
 
-    I = R("iw", 12, 140)
-    P, In, Pn, P2, I4 = (R("mb", 128 * k, 128 * k + 128) for k in range(5))
-    Mo, Mc = R("mo", 0, 128), R("mo", 128, 256)
+    def pcopy(out, a): return gsel(out, a, [[0, n_of(out)]], A.is_ge, 0, 0) if cfg["cp"] else fcopy(out, a, kind="c")
 
-    def row(j, neg=False): return R("W", 144 * neg + 15 - j, 144 * neg + 143 - j)
+    def fill(out, c): return iota(out, [[0, n_of(out)]], int(c), 0)
+
+    I = R("iw", 12, 140)
+    P, In, In4, I8, Pn = (R("mb", 128 * k, 128 * k + 128) for k in range(5))
+    kb = R("kb", 0, 256)
+    Mo = R("mo", 0, 128)
+
+    WT = ((1, 0), (-1, 1), (-KC, 0), (1, -KC))
+
+    def row(j, v=0): return R("W", 144 * v + 15 - j, 144 * v + 143 - j)
 
     def blk(nm, k): return R(nm, 128 * k, 128 * k + 128)
 
@@ -185,15 +208,37 @@ def build(T, rank, topo, core, phys, cfg):
         a = 152 * (1 + t + (2 if m == 4 else 0)) + 12 - (s - t) * (16 // m)
         return R("iw", a, a + 128)
 
-    def chunks(l):
+    def chunks(l, which="dch"):
         a, out = 0, []
-        for k, w in enumerate(cfg["ch"][l]):
+        for k, w in enumerate(cfg[which][l]):
             out.append((k, a, w)); a += w
         return out
 
-    def tile(l, k, kind): return R("tl", BS * (3 * (4 * l + k) + kind), BS * (3 * (4 * l + k) + kind + 1))
+    cur = {}
 
-    def spread(b, nm, t): return [(sub(b, j * BS, j * BS + BS), blk(nm, j), t) for j in range(n_of(b) // BS)]
+    def tile(l, k, kind, c, w):
+        a = BS * (3 * (3 * l + kind) + k)
+        if k == 0: cur[l, kind] = []
+        cur[l, kind].append((R("tl", a, a + BS), c, w))
+        return cur[l, kind][-1][0]
+
+    def spread(b, nm, tiles, c=0):
+        return [(sub(b, j - c, j - c + BS), blk(nm, j // BS), [t for t, a, w in tiles if a <= j < a + w][0]) for j in range(c, c + n_of(b), BS)]
+
+    masked = {}
+
+    def olds(b, tiles, c, w):
+        cover = [z for z in tiles if z[1] < c + w and c < z[1] + z[2]]
+        if len(cover) == 1: return [(b, Mo, cover[0][0])]
+        out = []
+        for t, a, v in cover:
+            if (a, v) not in masked:
+                z = masked[a, v] = R("mo", 256 + 128 * len(masked), 384 + 128 * len(masked))
+                assert len(masked) <= 10
+                gsel(z, Mo, [[0, 8], [1, 16]], A.is_ge, -2 * (a // BS), 0)
+                gsel(z, z, [[0, 8], [-1, 16]], A.is_ge, 2 * ((a + v) // BS) - 1, 0)
+            out.append((b, masked[a, v], t))
+        return out
 
     def ocol(rnd, l): return 2048 if (l == 1 and rnd and cfg["m"][0, 1] != cfg["m"][1, 1]) else 512 * (l - 1)
 
@@ -201,84 +246,105 @@ def build(T, rank, topo, core, phys, cfg):
     load("scalar", R("x", 0, 512), "piv", 0, 512)
     load("sync", R("raw", 0, 512), "uses", 0, 512)
     load("scalar", R("x", 512, 2048), "piv", 512, 2048)
-    for l in range(1, 4): load("sync", R("raw", 512 * l, 512 * l + 512), "uses", 512 * l, 512 * l + 512)
+    def raw(a, w): return R("raw", a + 8 * (a >= 1536), a + 8 * (a >= 1536) + w)
+    for l in range(1, 4): load("sync", raw(512 * l, 512), "uses", 512 * l, 512 * l + 512)
     load("sync", R("rpm"), "prem", 0, 256)
     load("sync", R("cw0", 2048, 2560), "lem", 0, 512)
     for k in range(3): load("sync", R("cw%d" % k, 2560, 3072), "leaf", 0, 512)
-    nb = max(max(c) for c in cfg["ch"].values()) // BS
-    mset(R("ob"), 1.0); mset(R("iw"), 0.0); mset(R("W", 0, 144), 0.0); mset(R("kb", 0, 128 * nb), K)
+    mset(R("ob"), 1.0); mset(R("iw", 0, 152), 0.0); mset(R("W"), 0.0); mset(kb, K)
+    mset(R("iw", 152, 456), 0.0); mset(R("iw", 456, 1064), 0.0)
     gsel(I, R("ob"), [[-1, 128]], A.is_equal, 0, 1)
     gsel(P, R("ob"), [[-16, 8], [8, 2], [-1, 8]], A.is_equal, -8, 1)
     w8 = R("W", 15, 143, 16)
     gsel(w8, R("ob", 0, 8), [[-16, 8]], A.is_ge, 0, 1)
     gsel(w8, w8, [[16, 8]], A.is_ge, 15, -1)
-    lin(R("W", 144, 288), R("W", 0, 144), -1, 0)
+    for v in (1, 2, 3):
+        for z in range(2):
+            if WT[v][z]: lin(R("W", 144 * v + 15 + z, 144 * v + 143, 16), w8, WT[v][z], 0)
     lin(In, I, -1, 0)
+    iota(R("ip", 0, 1), [[0, 1]], 0, 1)
+    ts(R("ip", 4, 5), R("ip", 0, 1), 1, None, A.bitwise_and)
+    COLS = ((6, 2), (2, 6), (32769, 0), (0, 1), (1, 0), (0, -128), (-256, 128))
+
+    def column(k): ts(R("col", k, k + 1), R("ip", 4, 5), float(COLS[k][0]), float(COLS[k][1]), A.mult, A.add)
+    column(4)
     made = set()
 
     def parts(m):
         if m > 1 and m not in made:
             made.add(m)
             for t in range(m): gsel(move(m, t, t), I, [[0, 8], [1, m], [0, 16 // m]], A.is_equal, -t, 0)
-    pk = [[-2, nb], [-16, 8], [0, 16]]
-    s_, kb = R("S", 0, 128 * nb), R("kb", 0, 128 * nb)
-    gsel(s_, kb, pk, A.is_equal, -1, 1)
-    gsel(s_, s_, pk, A.not_equal, 0, 1, fill=-2 * K)
-    lin(R("Sn", 0, 128 * nb), s_, -1, 0)
+    p2 = [[-2, 2], [-16, 8], [0, 16]]
+    for a in range(0, nb, 2):
+        s_ = R("S", 128 * a, 128 * a + 256)
+        gsel(s_, kb, p2, A.is_equal, -1 - 2 * a, 1)
+        gsel(s_, s_, p2, A.not_equal, -2 * a, 1, fill=-2 * K)
+        lin(R("Sn", 128 * a, 128 * a + 256), s_, -1, 0)
     mset(R("F", 1024, 4112), 255.0)
-    for h in (16, 8, 4):
-        mset(R("mk%d" % h, 0, cfg["gp"]), 0.0); mset(R("mk%d" % h, 0, cfg["gp"], h), 255.0)
 
     def late_consts():
-        u_ = R("U", 0, 128 * nb)
-        gsel(u_, kb, pk, A.is_ge, 0, 1)
-        gsel(u_, u_, [[2, nb], [16, 8], [0, 16]], A.is_ge, 1, -1)
-        iota(R("mo", 0, 128, 2), [[6 * KC, 64]], 2 * KC, -3 * KC)
-        iota(R("mo", 1, 128, 2), [[-6 * KC, 64]], -2 * KC, 3 * KC)
-        iota(R("mo", 128, 256, 2), [[2, 64]], 1, -1)
+        if "f" in "".join(cfg["cu"]):
+            iota(R("th1", 0, 256), [[0, 256]], -int(K), 0)
+            lin(Pn, P, -1, 0)
+        for a in range(0, nb, 2):
+            u_ = R("U", 128 * a, 128 * a + 256)
+            gsel(u_, kb, p2, A.is_ge, -2 * a, 1)
+            gsel(u_, u_, [[2, 2], [16, 8], [0, 16]], A.is_ge, 1 + 2 * a, -1)
+            if "f" in "".join(cfg["cu"]):
+                for z, nm in enumerate(("Ra", "Rb")): gsel(R(nm, 128 * a, 128 * a + 256), R("th1", 0, 256), p2, A.is_equal, -2 * a - z, 1)
+        iota(R("mo", 128, 256, 2), [[4, 64]], 1, -2)
         iota(R("mo", 129, 256, 2), [[-4, 64]], -1, 2)
-        gsel(R("mo"), R("mo"), [[0, 2], [-2, 64], [0, 2]], A.is_ge, 0, 1)
-        gsel(R("mo"), R("mo"), [[0, 2], [2, 64], [0, 2]], A.is_ge, 1, -1)
-        iota(R("tri"), [[2, 16], [0, 8], [-2, 16]], 1, 0)
+        gsel(R("mo", 128, 256), R("mo", 128, 256), [[-2, 64], [0, 2]], A.is_ge, 0, 1)
+        gsel(R("mo", 128, 256), R("mo", 128, 256), [[2, 64], [0, 2]], A.is_ge, 1, -1)
+        lin(Mo, R("mo", 128, 256), 2 ** 25, 0)
+        iota(R("tri"), [[2 * KC, 16], [0, 8], [-2 * KC, 16]], KC, 0)
         gsel(R("tri"), R("tri"), [[-1, 16], [0, 8], [1, 16]], A.is_ge, 0, 0)
         gsel(R("tri"), R("tri"), [[0, 16], [-16, 8], [0, 16]], A.is_equal, 0, 1)
-        iota(R("ip", 0, 1), [[0, 1]], 0, 1)
-        ts(R("ip", 4, 5), R("ip", 0, 1), 1, None, A.bitwise_and)
-        for k, (a, b) in enumerate(((6.0, 2.0), (2.0, 6.0), (32769.0, 0.0))): ts(R("col", k, k + 1), R("ip", 4, 5), a, b, A.mult, A.add)
-        lin(Pn, P, -1, 0); lin(P2, P, 2048, 0); lin(I4, I, 4096, 0)
-        mset(R("Z", 0, 1024), 0.0); mset(R("Z", 4096, 4112), 0.0)
-        ts(R("Lw", 0, 512), R("raw", 0, 512), -2048.0, None, A.add)
+        for k in (3,) + ((5, 6) if cfg["sig"] else ()): column(k)
+        lin(In4, I, -4, 0); lin(I8, I, 8, 0)
+        lin(R("W", 144 * 4 + 15, 144 * 4 + 143, 16), w8, -1, 0)
+        fill(R("kb", 256, 512), K); fill(R("raw", 1536, 1544), 4096); fill(R("Lw", 1536, 1544), 2048)
+        fill(R("Z", 0, 1024), 0); fill(R("Z", 4096, 4112), 0)
+        wide(0, 512)
         for l in (3, 2, 1, 0):
-            ts(R("zk", 512 * l, 512 * l + 512), R("x", 512 * l, 512 * l + 512), 0.0, K, A.is_equal, A.mult)
-            for z in range(2): ts(R("po", 128 * z + 32 * l, 128 * z + 32 * l + 32), R("rpm", 128 * z + 32 * l, 128 * z + 32 * l + 32), -512.0 * (l + 1), None, A.add)
+            z, x_ = R("zk", 512 * l, 512 * l + 512), R("x", 512 * l, 512 * l + 512)
+            flex(z, x_, act(z, x_, AF.Relu, bias=K, scale=-K), vts(z, x_, 0.0, K, A.is_equal, A.mult))
+        iota(R("rp2", 0, 256), [[0, 2], [512, 4], [0, 32]], 512, 0)
+        tt(R("rp2", 256, 512), R("rpm"), R("rp2", 0, 256), A.subtract)
+        copy(R("po"), R("rp2", 256, 512))
 
-    def lay(m, col, w, L, Tn, c):
-        parts(m)
+    def lay(grp, col, L):
+        for m, a, w in grp:
+            if m == 1: ts(R("off", col + a, col + a + w), sub(L, a, a + w), 2048.0, None, A.add)
+        grp = [z for z in grp if z[0] > 1]
+        if not grp: return
+        b = bank(n_of(L))
+        for m, a, w in grp:
+            parts(m)
+            n = w // m
+            for t in range(m): mm([(sub(b, a + t * n, a + t * n + n), move(m, t, s), sub(L, a + s, a + w, m)) for s in range(m)])
+        runs = []
+        for m, a, w in grp:
+            if runs and runs[-1][1] == a: runs[-1][1] = a + w
+            else: runs.append([a, a + w])
+        for a, e_ in runs: ts(R("off", col + a, col + e_), sub(b, a, e_), 2048.0, None, A.add)
+
+    def wide(col, w):
         b = bank(w)
-        n = w // m
-        for t in range(m):
-            o_ = sub(b, t * n, t * n + n)
-            if m == 1: lst = [(o_, I, L)] + ([(o_, P, Tn)] if Tn else [])
-            else:
-                lst = [(o_, move(m, t, s), sub(L, s, w, m)) for s in range(m)]
-                if Tn: lst += [(o_, move(m, (t + m // 2) % m, s), sub(Tn, s, w, m)) for s in range(m)]
-            mm(lst)
-        ts(R("off", col, col + w), b, c, None, A.add)
+        mm([(b, I, R("Lh", col, col + w))])
+        fcopy(R("Lw", col, col + w), b, kind="l")
 
     def first_lists(l, rnd):
         a = 512 * (l - 1)
-        if rnd == 0: ts(R("Lh", a, a + 512), R("raw", a, a + 512), -2048.0, None, A.add)
-        for k, c, w in chunks(l):
-            m = cfg["m"][rnd, l][k]
-            if m == 1: copy(R("off", ocol(rnd, l) + c, ocol(rnd, l) + c + w), R("raw", a + c, a + c + w))
-            else: lay(m, ocol(rnd, l) + c, w, R("Lh", a + c, a + c + w), None, 2048.0)
+        if rnd == 0: ts(R("Lh", a, a + 512), raw(a, 512), -2048.0, None, A.add)
+        lay([(cfg["m"][rnd, l][k], c, w) for k, c, w in chunks(l)], ocol(rnd, l), R("Lh", a, a + 512))
 
-    def state(forms, n0, w, srcs, neg, old, new, cmp, after):
+    def state(forms, n0, w, srcs, neg, old, new, after, sig):
         cb = bank(BS)
         x_ = R("x", n0, n0 + w)
         first = True
         if old:
-            mm([(cb, Mo, old)], stop=False, after=[after]); first = False
+            mm(olds(cb, old, n0 % 512, w), stop=False, after=[after]); first = False
         for z in range(2):
             b, t = bank(w), pick("ta" if z == 0 else "tb", 3, w)
             if forms[z] == "v":
@@ -288,31 +354,45 @@ def build(T, rank, topo, core, phys, cfg):
                 mm([(b, (I, P)[z], x_)], stop=False, after=[after])
                 mm([(b, In, srcs[z])], start=False)
                 relu(t, b)
-            mm([(cb, row(2 * j + z, neg), sub(t, j * BS, j * BS + BS)) for j in range(w // BS)], start=first, stop=z == 1)
+            mm([(cb, row(2 * (j + n0 % 512 // BS) + z, ((3, 0), (1, 2))[neg][z]), sub(t, j * BS, j * BS + BS)) for j in range(w // BS)], start=first, stop=z == 1)
             first = False
-        return ts(new, cb, 0.0, None, cmp, kind="i")
+        c_, d_ = R("col", 3 + neg, 4 + neg), R("col", 5 + neg, 6 + neg)
+        v = vts(new, cb, c_, None, A.is_ge)
+        if not sig: return op([v], [cb, c_], [new], kind="i")
+        return op([("scalar", (BS, 0, 1, 0), lambda e: e.activation(ap(new), ap(cb), AF.Sigmoid, bias=ap(d_), scale=256.0)), v], [cb, c_, d_], [new], kind="i")
 
     def sides(tab, n0, w, t, names, after=None):
         out = []
         for z in range(2):
             b = bank(w)
-            mm([(b, (I, P)[z], R(tab, n0, n0 + w))] + spread(b, names[z], t), after=[after])
+            mm([(b, (I, P)[z], R(tab, n0, n0 + w))] + spread(b, names[z], t, n0 % 512), after=[after])
             out.append(b)
         return out
 
     def least(rnd, l, k, c, w):
         m = cfg["m"][rnd, l][k]
-        h, so = 16 // m, pick("so", NSO)
-        wp = min(w, cfg["gp"] * m // 16)
-        for j in range(0, w, wp):
-            v = min(wp, w - j)
-            gb = pick("g", NG, v * h)
-            for t in range(m):
-                a = ocol(rnd, l) + c + (t * w + j) // m
-                i = (gmin if t else gather)(gb, R("F", 0, 4097), R("off", a, a + v // m))
-                if t == 0: g0 = i
-            scan(sub(so, j * h, (j + v) * h), R("mk%d" % h, 0, v * h), gb)
-        return sub(so, h - 1, w * h, h), g0, i
+        h = 16 // m
+        so = pick("so", NSO, w * h)
+        gp = cfg["gg"] if l == 4 else cfg["gp"]
+        wp, ws = min(w, gp // h), min(w, max(gp, cfg["sp"]) // h)
+        for j0 in range(0, w, ws):
+            v0 = min(ws, w - j0)
+            gb = pick("g", NG, v0 * h)
+            for j in range(j0, j0 + v0, wp):
+                v = min(wp, j0 + v0 - j)
+                for t in range(m):
+                    a = ocol(rnd, l) + c + (t * w + j) // m
+                    i = (gmin if t else gather)(sub(gb, (j - j0) * h, (j - j0 + v) * h), R("F", 0, 4097), R("off", a, a + v // m))
+                    if t == 0: g0 = i
+            if (h, v0) not in made:
+                made.add((h, v0))
+                have = max([0] + [z[1] for z in made if isinstance(z, tuple) and z[0] == h and z[1] != v0])
+                if have < v0:
+                    fill(R("mk%d" % h, have * h, v0 * h), 0); fill(R("mk%d" % h, have * h, v0 * h, h), 255)
+            g0 = scan(sub(so, j0 * h, (j0 + v0) * h), R("mk%d" % h, 0, v0 * h), gb)
+        return sub(so, h - 1, w * h, h), (g0 if cfg["pre"] else i), i
+
+    lastup = {}
 
     def down(rnd, l):
         ph[0] = "%dD%d" % (rnd, l)
@@ -323,16 +403,17 @@ def build(T, rank, topo, core, phys, cfg):
             g0 = gl = None
             if l: src, g0, gl = least(rnd, l, k, c, w)
             else: src = R("as%d" % rnd, c, c + w) if rnd else o_
-            if l == 0 and rnd: g0 = lastup[k]
-            state(cfg["td"], n0, w, (src, src), True, tile(l, k, 2) if rnd else None, tile(l, k, 0), A.is_ge, g0)
+            if l == 0 and rnd: g0 = lastup[0]
+            state(cfg["td"][rnd], n0, w, (src, src), True, cur[l, 1] if rnd else None, tile(l, k, 0, c, w), g0, cfg["sig"] and rnd)
             if rnd:
                 b = bank(w)
-                mm([(b, I, src)] + spread(b, "U", tile(l, k, 2)))
+                mm([(b, I, src)] + spread(b, "U", cur[l, 1], c))
                 tt(o_, b, R("kx", n0, n0 + w), A.min)
-            elif l: fcopy(o_, src, kind="c")
+            elif l: pcopy(o_, src)
             todo.append((k, n0, w, o_ if rnd else src))
+        if cfg["ew"][rnd][l] == "w": todo = [(0, 512 * l, 512, R("o", 512 * l, 512 * l + 512))]
         for k, n0, w, src in todo:
-            for z, b in enumerate(sides("x", n0, w, tile(l, k, 0), ("S", "Sn"), gl)):
+            for z, b in enumerate(sides("x", n0, w, cur[l, 0], ("S", "Sn"), gl)):
                 tt(R("F", 2 * n0 + z, 2 * n0 + 2 * w, 2), src, b, A.max, kind="e")
         if rnd == 2: store("ys", 512 * l, 512 * l + 512, R("o", 512 * l, 512 * l + 512))
 
@@ -344,95 +425,99 @@ def build(T, rank, topo, core, phys, cfg):
         rid, pid = topo.addr(d)[:2]
         mask = sum(1 << e for e in topo.engines(core, d)[:8])
         i = op([("pool", (0, 0, 0, 1.0), lambda e: e.remote_dma(ap(dst), ap(src), T.sem["ra%d" % k], T.sem["la%d" % k], pid, rid, mask))], [src], [], sem=("la%d" % k, 8), kind="r")
-        op([(None, (0, 0, 0, 4.0), None)], [], [dst], sem=("ra%d" % k, 8), after=[i], kind="a")
+        op([(None, (0, 0, 0, 4.0 if k else 7.0), None)], [], [dst], sem=("ra%d" % k, 8), after=[i], kind="a")
 
     def ghosts(rnd):
         ph[0] = "%dG" % rnd
         for k, c, w in chunks(4):
-            fcopy(R("o", 2048 + c, 2048 + c + w), least(rnd, 4, k, c, w)[0], kind="c")
-        if rnd < 2: send(R("o", 2048, 2560), R("as%d" % (rnd + 1)), rank + 1)
-        else: store("ys", 2048, 2560, R("o", 2048, 2560))
-
-    lastup = {}
+            o_ = R("o", 2048 + c, 2048 + c + w)
+            pcopy(o_, least(rnd, 4, k, c, w)[0])
+            if rnd < 2: send(o_, R("as%d" % (rnd + 1), c, c + w), rank + 1)
+            else: store("ys", 2048 + c, 2048 + c + w, o_)
 
     def up(rnd, l):
         ph[0] = "%dU%d" % (rnd, l)
         cw = "cw%d" % rnd
-        for k, c, w in chunks(l):
+        for k, c, w in chunks(l, "uch"):
             n0 = 512 * l + c
             ab = (pick("ga", 3, w), pick("gb", 3, w))
             gs = [gather(ab[z], R(cw, 512 * l + 512, 3072), R("po", 128 * z + n0 // 16, 128 * z + (n0 + w) // 16)) for z in range(2)]
-            lastup[k] = state(cfg["tu"], n0, w, ab, False, tile(l, k, 0), tile(l, k, 1), A.is_gt, gs[0])
-            ba, bb = sides("zk", n0, w, tile(l, k, 1), ("Sn", "S"))
-            q = pick("qq", 3, w)
-            tt(ba, ab[0], ba, A.min)
-            tt(q, ab[1], bb, A.min)
+            new = tile(l, k, 1, c, w)
+            lastup[0] = state(cfg["tu"][rnd], n0, w, ab, False, cur[l, 0], new, gs[0], cfg["sig"])
+            q = pick("qq", 2, w)
+            if cfg["cu"][rnd][l] == "v":
+                ba, bb = sides("zk", n0, w, cur[l, 1], ("Sn", "S"))
+                tt(ba, ab[0], ba, A.min)
+                tt(q, ab[1], bb, A.min)
+            else:
+                b, y = bank(w), pick("th", 2, w)
+                mm([(b, I, R("zk", n0, n0 + w))] + spread(b, "U", cur[l, 1], c))
+                flex(y, b, act(y, b, AF.Relu, bias=K, scale=-1.0), vts(y, b, 0.0, K, A.is_equal, A.mult))
+                bb, ba = bank(w), bank(w)
+                mm([(bb, I, ab[1])] + spread(bb, "Ra", cur[l, 1], c), stop=False)
+                mm([(bb, Pn, y)], start=False)
+                relu(q, bb)
+                mm([(ba, I, ab[0])] + spread(ba, "Rb", cur[l, 1], c), stop=False)
+                mm([(ba, In, y)], start=False)
             tt(R(cw, n0, n0 + w), q, ba, A.max)
             if rnd == 2:
                 store("yc", n0, n0 + w, R(cw, n0, n0 + w))
                 continue
-            b, cl = bank(BS), tile(l, k, 2)
-            mm([(b, Mc, tile(l, k, 1))])
-            relu(cl, b, kind="z")
             if l:
                 b = bank(w)
-                for z in spread(b, "S", cl): mm([z])
+                mms(spread(b, "S", cur[l, 1], c))
                 za, zb = R("Z", 2 * n0, 2 * n0 + 2 * w, 2), R("Z", 2 * n0 + 1, 2 * n0 + 2 * w, 2)
                 flex(za, b, act(za, b, AF.Relu, scale=-0.5 / K), vts(za, b, 0.0, None, A.is_lt), kind="z")
                 flex(zb, b, act(zb, b, AF.Relu, scale=1 / K), vts(zb, b, 0.0, None, A.is_gt), kind="z")
             b = bank(w)
-            mm([(b, In, R("o", n0, n0 + w))] + spread(b, "U", cl))
+            mm([(b, In, R("o", n0, n0 + w))] + spread(b, "U", cur[l, 1], c))
             lin(R("kx", n0, n0 + w), b, -1, K, kind="k")
         if rnd < 2 and l == 0: send(R(cw, 0, 512), R("cw%d" % (rnd + 1), 2048, 2560), rank - 1)
 
     def splice(rnd, l):
         ph[0] = "%dS%d" % (rnd, l)
-        for k, c, w in chunks(l):
+        for grp in ([chunks(l)] if cfg["sw"][l] else [[z] for z in chunks(l)]):
+            c, w = grp[0][1], sum(z[2] for z in grp)
             col = 512 * (l - 1) + c
-            L = R("Lh", col, col + w)
-            m = cfg["m"][rnd - 1, l][k]
-            h, fl = 16 // m, bank(w)
-            wp = min(w, cfg["fp"] * m // 16)
-            for j in range(0, w, wp):
-                v = min(wp, w - j)
+            L, fl = R("Lh", col, col + w), bank(w)
+            for k, c1, w1 in grp:
+                m = cfg["m"][rnd - 1, l][k]
+                h, n = 16 // m, w1 // m
                 for t in range(m):
-                    fg = pick("fg", NFG, v * h)
-                    a = col + (t * w + j) // m
-                    gather(fg, R("Z", 0, 4097), R("off", a, a + v // m))
-                    mm([(sub(fl, j, j + v), blk("tri", t * h + r), sub(fg, r, v * h, h)) for r in range(h)], start=t == 0, stop=t == m - 1)
-            th = pick("th", 3, w)
-            i = relu(th, fl)
-            X, b = pick("X", 3, w), bank(w)
-            mm([(b, I, L)], after=[i])
-            tt(X, th, b, A.mult)
+                    fg, a = pick("fg", NFG, w1 * h), col + c1 - c + t * n
+                    for j in range(0, n, cfg["fp"] // 16):
+                        v = min(cfg["fp"] // 16, n - j)
+                        gather(sub(fg, 16 * j, 16 * (j + v)), R("Z", 0, 4097), R("off", a + j, a + j + v))
+                    for r0 in range(0, h, 4):
+                        o_ = sub(fl, c1 - c, c1 - c + w1)
+                        last_mm = mm([(o_, blk("tri", t * h + r), sub(fg, r, w1 * h, h)) for r in range(r0, r0 + 4)] + ([] if t + r0 else [(o_, In4, R("kb", 0, w1))]),
+                                     start=t + r0 == 0, stop=t * h + r0 == 12)
+            L1 = pick("X", 2, w)
+            i = tt(L1, L, fl, A.max)
             b = bank(w // 16)
-            mm([(b, row(q), sub(X, q, w, 16)) for q in range(16)])
-            xi, xu = pick("xi", 3, w // 16), pick("xu", 3, w // 16)
-            ts(xi, b, 0.5, 511.75, A.mult, A.add, kind="i")
+            mm([(b, row(q, 4), sub(L, q, w, 16)) for q in range(16)], stop=False, after=[last_mm])
+            mm([(b, row(q), sub(L1, q, w, 16)) for q in range(16)], start=False)
+            xi, xu = pick("xi", 2, w // 16), pick("xu", 2, w // 16)
+            ts(xi, b, -0.5, 1535.75, A.mult, A.add, kind="i")
             i = copy(xu, xi, kind="i")
-            tg = pick("Tg", 3, w)
-            win, add = (R("raw", 0, 1536), -2048.0) if rnd == 1 else (R("Lw"), 0.0)
+            tg = pick("Tg", 2, w)
+            win, add = (R("raw", 0, 1537), -2048.0) if rnd == 1 else (R("Lw", 0, 1537), 0.0)
             op([("vector", (0, w, 1, 0), lambda e, tg=tg, xu=xu, win=win, add=add: e.tensor_scalar(ap(tg), ap(win).indirect(ap(xu)), add, None, op0=A.add))], [win, xu], [tg])
-            b, hm = bank(w), pick("hm", 3, w)
-            mm([(b, P, L), (b, Pn, X), (b, P2, th)], after=[i])
+            b, hm = bank(w), pick("hm", 2, w)
+            mm([(b, P, L1)], after=[i])
             tt(hm, tg, b, A.max)
             b = bank(BS)
-            mm([(b, row(2 * j + 1), sub(z, j * BS, j * BS + BS)) for z in (th, hm) for j in range(w // BS)])
-            ot = pick("ot", 3, 2 * BS)
-            ts(sub(ot, 0, BS), b, R("col", 2, 3), R("col", 0, 1), A.is_ge, A.mult, kind="i")
-            ts(sub(ot, BS, 2 * BS), b, R("col", 2, 3), R("col", 1, 2), A.is_ge, A.mult, kind="i")
-            tk, lk, b = pick("Tk", 3, w), pick("Lk", 3, w), bank(w)
-            for z in spread(b, "Sn", sub(ot, 0, BS)): mm([z])
-            tt(tk, tg, b, A.max)
+            mm([(b, row(2 * j + 1), sub(hm, j * BS, j * BS + BS)) for j in range(w // BS)])
+            ot = pick("ot", 2, BS)
+            ts(ot, b, 32768.0, 8.0, A.is_ge, A.mult, kind="i")
+            lk, b = pick("Lk", 2, w), bank(w)
+            mm([(b, I, L)] + spread(b, "S", [(ot, 0, w)]))
+            tt(lk, L1, b, A.min)
             b = bank(w)
-            mm([(b, I4, th)] + spread(b, "S", sub(ot, BS, 2 * BS)))
-            tt(lk, L, b, A.max)
-            lay(cfg["m"][rnd, l][k], col, w, lk, tk, 0.0)
-            if rnd == 1:
-                b = bank(w)
-                mm([(b, I, lk), (b, P, tk)])
-                ts(L, b, -2048.0, None, A.add, kind="l")
-                if l < 4: lin(R("Lw", col, col + w), b, 1, -2048, kind="l")
+            mm([(b, P, tg), (b, I8, R("kb", 0, w))] + spread(b, "Sn", [(ot, 0, w)]))
+            tt(L, lk, b, A.min)
+            lay([(cfg["m"][rnd, l][k], c1 - c, w1) for k, c1, w1 in grp], col, L)
+            if rnd == 1 and l < 4: wide(col, w)
 
     down(0, 0)
     for l in (1, 2, 3):
@@ -452,16 +537,49 @@ def build(T, rank, topo, core, phys, cfg):
     return ops
 
 
-MODELS = ((1.0, 1.1, 0.03, 0.1), (1.1, 1.55, 0.05, 0.12), (1.3, 2.0, 0.06, 0.15))
+MODELS = ((1.0, 1.1, 0.05, 0.1), (1.0, 1.55, 0.05, 0.08), (1.4, 2.0, 0.05, 0.12), (1.2, 1.3, 0.06, 0.25))
 QALL = (None, "vector", "scalar", "tensor", "pool", "sync")
 
 
 def cost(q, c, md):
-    if q == "tensor": return c[0] * 0.00045 * md[0] + c[2] * 0.015
+    if q == "tensor": return c[0] * 0.00045 * md[0] + c[2] * 0.006
     return ((max(64, c[0]) if c[0] else 0) + c[1] * md[1]) * 0.00083 * md[0] + c[2] * md[2] + c[3]
 
 
-def plan(ops, md, offs, look=0.5, vb=0.0):
+def backward(ops, us, lat, succ, ends, asg):
+    n = len(ops)
+    left = [len(s) for s in succ]
+    rt, pr, free = [0.0] * n, [0.0] * n, {}
+    ready = {q: [] for q in QALL}
+    for i in range(n):
+        if not left[i]: ready[asg[i]].append(i)
+    for _ in range(n):
+        t, q = min((max(min(rt[i] for i in c), free.get(q, 0.0)), k) for k, (q, c) in enumerate(ready.items()) if c)
+        q = QALL[q]
+        i = max((i for i in ready[q] if rt[i] <= t + 1e-9), key=lambda i: ends[i])
+        ready[q].remove(i)
+        pr[i] = t + us[i][q]
+        if q is not None: free[q] = pr[i]
+        for j in set(ops[i]["deps"]) | set(ops[i]["after"]):
+            hard = ops[i]["deps"].get(j)
+            rt[j] = max(rt[j], pr[i] + (lat[j] if hard and hard != "acc" else 0.0 if hard or q is None else -us[j][asg[j]]))
+            left[j] -= 1
+            if not left[j]: ready[asg[j]].append(j)
+    return pr
+
+
+def plan(ops, md, cfg):
+    best = pl = None
+    for _ in range(cfg["it"] + 1):
+        pl = forward(ops, md, cfg, *((pl[5], pl[1]) if pl else ()))
+        if pl is None: break
+        v = sum(replay(ops, pl, m) / (m[0] * (1 + m[1])) for m in MODELS)
+        if best is None or v < best[0]: best = (v, pl)
+    return best and best[1]
+
+
+def forward(ops, md, cfg, ends=None, asg0=None):
+    offs, look, vb = cfg["offs"], cfg["look"], cfg["vb"]
     n = len(ops)
     us = [{x[0]: cost(x[0], x[1], md) for x in o["opts"]} for o in ops]
     lat = [(2.2 if o["sem"] and None not in o["qs"] else 0.0) + md[3] for o in ops]
@@ -475,7 +593,9 @@ def plan(ops, md, offs, look=0.5, vb=0.0):
         for b in o["banks"]: users.setdefault(b, []).append(i)
     pr = [0.0] * n
     for i in range(n - 1, -1, -1): pr[i] = max([pr[s] for s in succ[i]] or [0.0]) + lat[i] + min(us[i].values())
-    pr = [pr[i] + offs.get(ops[i]["name"], 0.0) for i in range(n)]
+    if ends: pr = backward(ops, us, lat, succ, ends, asg0)
+    pr = [pr[i] + offs.get(ops[i]["name"], 0.0) + offs.get(ops[i]["name"][:-1], 0.0) for i in range(n)]
+    opens = [any(users[b][0] == i for b in o["banks"]) for i, o in enumerate(ops)]
     rt, fin, asg = [0.0] * n, [0.0] * n, [None] * n
     free = {q: 0.0 for q in QALL}
     ready = {q: [] for q in QALL}
@@ -492,20 +612,48 @@ def plan(ops, md, offs, look=0.5, vb=0.0):
         tb = min([bfree[k] for k in fb] or [1e9])
         for q in QALL:
             c = ready[q]
-            if q == "tensor": c = [(max(rt[i], tb) if any(b not in phys for b in ops[i]["banks"]) else rt[i], i) for i in c]
+            if not c: continue
+            if q == "tensor":
+                top = max(pr[i] for z in ready.values() for i in z) - cfg["far"] if len(fb) <= cfg["keep"] else -1e9
+                c = [(max(rt[i], tb) if opens[i] else rt[i], i) for i in c if not opens[i] or pr[i] >= top]
+                if not c: continue
             else: c = [(rt[i], i) for i in c]
-            if c:
-                t = max(min(c)[0], free[q])
-                if bt is None or t < bt: bt, bq, bc = t, q, c
+            t = max(min(c)[0], free[q])
+            if bt is None or t < bt: bt, bq, bc = t, q, c
         if bt is None or bt >= 1e9: return None
         bias = vb if bq == "vector" else 0.0
         key = lambda z: pr[z[1]] - (bias if len(us[z[1]]) > 1 else 0.0)
         now = [z for z in bc if z[0] <= bt + 1e-9]
+        if bq == "vector":
+            now = [z for z in now if len(us[z[1]]) == 1 or free["scalar"] - bt + sum(us[j]["scalar"] for j in ready["scalar"] if pr[j] > pr[z[1]]) >= cfg["back"] * us[z[1]][bq]]
+            if not now:
+                free[bq] = bt + 0.1
+                continue
         best = max(now, key=key)
-        soon = [z for z in bc if z[0] > bt + 1e-9 and key(z) > key(best) and z[0] < bt + look * us[best[1]][bq] and len(us[z[1]]) == 1]
+        ahead = []
+        if bq in ("vector", "scalar") and us[best[1]][bq] > 0.3:
+            other = "vector" if bq == "scalar" else "scalar"
+            tq, lf, at = {"tensor": free["tensor"], other: max(free[other], bt)}, {}, {}
+            todo = [(j, "tensor") for j in ready["tensor"]] + [(j, other) for j in ready[other] if len(us[j]) == 1]
+            while todo:
+                t, _, j, q = min((max(rt[j], at.get(j, 0.0), tq[q]), -pr[j], j, q) for j, q in todo)
+                if t > bt + look * us[best[1]][bq]: break
+                todo.remove((j, q))
+                t = tq[q] = t + us[j][q]
+                for k in succ[j]:
+                    lf[k] = lf.get(k, left[k]) - 1
+                    at[k] = max(at.get(k, 0.0), t + md[3])
+                    if lf[k]: continue
+                    if bq in us[k]: ahead.append((max(rt[k], at[k]), k))
+                    elif "tensor" in us[k] or other in us[k]: todo.append((k, "tensor" if "tensor" in us[k] else other))
+        soon = [z for z in bc + ahead if z[0] > bt + 1e-9 and key(z) > key(best) + cfg["gap"] and z[0] < bt + look * us[best[1]][bq]
+                and (len(us[z[1]]) == 1 or bq == "scalar")]
         if soon:
             u = min(soon)
             fit = [z for z in now if bt + us[z[1]][bq] <= u[0] + 0.1]
+            if not fit and u in ahead:
+                free[bq] = u[0]
+                continue
             best = max(fit, key=key) if fit else u
         t, i = max(bt, best[0]), best[1]
         for q in us[i]: ready[q].remove(i)
@@ -522,9 +670,8 @@ def plan(ops, md, offs, look=0.5, vb=0.0):
             togo[b] -= 1
             bfree[phys[b]] = max(bfree[phys[b]], f + md[3])
         for j in succ[i]:
-            hard = j in range(n) and i in ops[j]["deps"]
-            d = f + lat[i] if (hard or ops[j]["qs"] == {None}) else t
-            if hard and ops[j]["deps"][i] == "acc": d = f
+            hard = ops[j]["deps"].get(i)
+            d = f if hard == "acc" else f + lat[i] if (hard or ops[j]["qs"] == {None}) else t
             rt[j] = max(rt[j], d)
             left[j] -= 1
             if not left[j]:
@@ -548,8 +695,73 @@ def replay(ops, pl, md):
     return max(fin.values())
 
 
-OFFS = {}
-LOOK, VB = 0.5, 10.0
+def polish(ops, pl, tries, temp=0.05):
+    order, asg, phys, prev = list(pl[0]), list(pl[1]), pl[2], pl[3]
+    n = len(ops)
+    pre = []
+    for i, o in enumerate(ops):
+        d = {j: k != "w" and not ops[j]["sem"] for j, k in o["deps"].items()}
+        for j in prev.get(i, ()): d.setdefault(j, True)
+        if None in o["qs"]:
+            for j in o["after"]: d[j] = None
+        pre.append(list(d.items()))
+    succ = [[] for _ in range(n)]
+    for i in range(n):
+        for j, _ in pre[i]: succ[j].append(i)
+    us = [[{x[0]: cost(x[0], x[1], md) for x in o["opts"]} for o in ops] for md in MODELS]
+    tail = [2.2 if o["sem"] and None not in o["qs"] else 0.0 for o in ops]
+    wt = [1 / (m[0] * (1 + m[1])) for m in MODELS]
+
+    def run(k):
+        wake, u, fin, free, why, lastq = MODELS[k][3], us[k], [0.0] * n, {q: 0.0 for q in QALL}, [-1] * n, {}
+        st = [0.0] * n
+        for i in order:
+            q = asg[i]
+            t, y = (free[q], lastq.get(q, -1)) if q else (0.0, -1)
+            for j, soft in pre[i]:
+                v = fin[j] - 2.2 if soft is None else fin[j] if soft and asg[j] == q else fin[j] + wake
+                if v > t: t, y = v, j
+            st[i] = t
+            t += u[i][q]
+            free[q], lastq[q], why[i], fin[i] = t, i, y, t + tail[i]
+        e_ = max(fin)
+        return e_, why, fin.index(e_), st
+    seed = [12345]
+
+    def rnd(m):
+        seed[0] = (seed[0] * 1103515245 + 12345) % 2 ** 31
+        return (seed[0] >> 8) % m
+    res = [run(k) for k in range(len(MODELS))]
+    now = sum(r[0] * w for r, w in zip(res, wt))
+    best = (now, list(order), list(asg))
+    for it in range(tries):
+        why, i = res[rnd(len(res))][1:3]
+        chain = []
+        while i >= 0: chain.append(i); i = why[i]
+        i = chain[rnd(len(chain))]
+        q, p = asg[i], order.index(i)
+        if q is None: continue
+        kind = rnd(5)
+        if kind == 0 and len(us[0][i]) < 2: kind = 1
+        if kind == 0: asg[i] = "vector" if q == "scalar" else "scalar"
+        step, hops, stop = (-1, 1 + rnd(3), set(j for j, _ in pre[i])) if kind < 3 else (1, 1 + rnd(3), set(succ[i]))
+        if kind == 0: hops -= 1
+        a = b = p
+        while hops and 0 <= a + step < n and order[a + step] not in stop:
+            a += step
+            if asg[order[a]] == asg[i]: hops -= 1; b = a
+        if b == p and kind: continue
+        order.insert(b, order.pop(p))
+        new = [run(k) for k in range(len(MODELS))]
+        v = sum(r[0] * w for r, w in zip(new, wt))
+        if v <= now + temp * (1 - it / tries) * rnd(1000) / 1000:
+            now, res = v, new
+            st = new[1][3]
+            order.sort(key=lambda j: st[j])
+            if v < best[0]: best = (v, list(order), list(asg))
+        else:
+            order.insert(p, order.pop(b)); asg[i] = q
+    return best[1], best[2], phys, prev
 
 
 def rank_program(g, core, T, topo):
@@ -558,7 +770,7 @@ def rank_program(g, core, T, topo):
         return
     phys = {}
     ops = build(T, rank, topo, core, phys, CFG)
-    if "p" not in PLAN: PLAN["p"] = plan(ops, MODELS[1], OFFS, LOOK, VB)
+    if "p" not in PLAN: PLAN["p"] = polish(ops, plan(ops, MODELS[1], CFG), CFG["tries"], 0.02)
     order, asg, ph, prev = PLAN["p"][:4]
     phys.update(ph)
     pos = {j: k for k, j in enumerate(order)}

@@ -2,51 +2,63 @@ from concourse.mybir import AluOpType as A, ActivationFunctionType as AF
 
 K = 512.0
 KC = 4096
+BIG = 2.0 ** 43
+H = (256, 256)
 CFG = {
-    "bs": 128,
-    "dch": {0: (256, 256), 1: (256, 256), 2: (256, 256), 3: (256, 256), 4: (256, 256)},
-    "uch": {0: (256, 256), 1: (512,), 2: (512,), 3: (512,)},
-    "sw": {2: 1, 3: 1, 4: 1},
-    "m": {(0, 1): (2, 1), (0, 2): (1, 2), (0, 3): (1, 2), (0, 4): (1, 2),
-          (1, 1): (2, 2), (1, 2): (2, 2), (1, 3): (1, 2), (1, 4): (1, 2),
-          (2, 1): (2, 2), (2, 2): (2, 2), (2, 3): (1, 2), (2, 4): (1, 2)},
-    "gp": 1024, "fp": 1024, "td": ("ff", "ff", "ff"), "tu": ("ff", "ff", "ff"), "sig": 0, "sp": 1024, "gg": 1024, "back": 0.0, "cp": 1, "ew": ("cccc", "cccc", "cccc"), "pre": 1, "keep": 4, "far": 3.0, "tries": 5000, "cu": ("vvvv", "vvvv", "vvvv"),
-    "pin": {"1S3g": "s", "1S4g": "s", "2S3g": "s", "2S4g": "s"}, "offs": {}, "look": 0.3, "vb": 10.0, "it": 2, "gap": 3.0,
+    "dch": {(r, l): (512,) if r and not l else H for r in range(3) for l in range(5)},
+    "m": {(r, l): (4, 4) if r and l < 3 else (1, 2) for r in range(3) for l in range(1, 5)},
+    "uch": {(r, l): (H if (r, l) == (2, 0) else (512,)) for r in range(3) for l in range(4)},
+    "cu": ("vddv", "vddv", "dddd"),
+    "pf": ("pp", "qp", "qp", "qp"),
+    "zd": (2, 3), "ka": (1, 2, 3),
+    "gp": 1024, "fp": (1024, 2048, 2048),
+    "pin": {}, "look": 0.3, "vb": 10.0, "it": 2, "gap": 3.0, "keep": 4, "far": 3.0,
+    "wt": (1.5, 1, 0.8), "ns": 3, "stay": 50, "wide": 100, "zone": 100, "swap": 10, "seed": 1,
+    "lag": {"S4l": 5, "S3l": 2, "S2l": 2}, "cycles": ((50000, .6), (45000, .5), (45000, .45), (45000, .4), (60000, .45), (40000, .35)),
 }
-NG, NSO, NFG = 6, 3, 3
+for _r in range(3):
+    for _p in ("D0", "D1", "D2", "D3", "G", "U0", "U1", "U2", "U3", "S2", "S3", "S4"):
+        for _k in "gaveulkzcyi": CFG["pin"]["%d%s%s" % (_r, _p, _k)] = "s"
+    CFG["pin"]["%dS2g" % _r] = "svsvsvs"
+    CFG["pin"]["0D%dg" % (_r + 1)] = "vs"
+NT = 4
 SCRATCH = {
     "raw": ("sbuf", [128, 2056], "int32"), "rpm": ("sbuf", [128, 256], "int32"), "po": ("sbuf", [128, 256], "uint16"),
-    "off": ("sbuf", [128, 2560], "uint16"), "Lh": ("sbuf", [128, 2048], "float16"), "Lw": ("sbuf", [128, 1544], "float32"),
+    "off": ("sbuf", [128, 3072], "uint16"), "Lh": ("sbuf", [128, 2048], "float16"), "Lw": ("sbuf", [128, 1544], "float32"),
     "F": ("sbuf", [128, 4112], "bfloat16"), "Z": ("sbuf", [128, 4112], "bfloat16"),
-    "x": ("sbuf", [128, 2048], "bfloat16"), "zk": ("sbuf", [128, 2048], "bfloat16"),
-    "o": ("sbuf", [128, 2560], "bfloat16"), "kx": ("sbuf", [128, 2048], "bfloat16"),
+    "x": ("sbuf", [128, 2048], "bfloat16"), "o": ("sbuf", [128, 2560], "bfloat16"), "kx": ("sbuf", [128, 2048], "bfloat16"),
     "as1": ("sbuf", [128, 512], "bfloat16"), "as2": ("sbuf", [128, 512], "bfloat16"),
-    "ob": ("sbuf", [128, 128], "bfloat16"), "kb": ("sbuf", [128, 512], "bfloat16"), "mb": ("sbuf", [128, 128 * 5], "bfloat16"),
-    "iw": ("sbuf", [128, 152 * 7], "bfloat16"), "W": ("sbuf", [128, 720], "bfloat16"), "tri": ("sbuf", [128, 2048], "bfloat16"),
-    "S": ("sbuf", [128, 1024], "bfloat16"), "Sn": ("sbuf", [128, 1024], "bfloat16"), "U": ("sbuf", [128, 1024], "bfloat16"),
-    "Ra": ("sbuf", [128, 1024], "bfloat16"), "Rb": ("sbuf", [128, 1024], "bfloat16"), "rp2": ("sbuf", [128, 512], "int32"),
-    "mo": ("sbuf", [128, 256 + 128 * 10], "bfloat16"), "tl": ("sbuf", [128, 4608], "bfloat16"),
-    "ip": ("sbuf", [128, 8], "int32"), "col": ("sbuf", [128, 8], "float32"),
+    "ob": ("sbuf", [128, 128], "bfloat16"), "kb": ("sbuf", [128, 512], "bfloat16"), "zb": ("sbuf", [128, 512], "bfloat16"),
+    "mb": ("sbuf", [128, 128 * 9], "bfloat16"), "iw": ("sbuf", [128, 152 * 7], "bfloat16"), "W": ("sbuf", [128, 720], "bfloat16"),
+    "tri": ("sbuf", [128, 2048], "bfloat16"), "ez": ("sbuf", [128, 272], "bfloat16"), "rp2": ("sbuf", [128, 512], "int32"),
+    "mo": ("sbuf", [128, 128 * 13], "bfloat16"), "tl": ("sbuf", [128, 128 * 36], "bfloat16"), "g0": ("sbuf", [128, 512], "bfloat16"),
+    "b4": ("sbuf", [128, 512], "bfloat16"), "nw": ("sbuf", [128, 2048], "bfloat16"), "ip": ("sbuf", [128, 8], "int32"),
+    "col": ("sbuf", [128, 16], "float32"),
 }
-for _k in (4, 8, 16): SCRATCH["mk%d" % _k] = ("sbuf", [128, 2048], "bfloat16")
+SPREAD = {"SA": (0, 2048, -1024, 0), "SB": (2048, 0, -1024, 0), "TA": (BIG, -BIG, 0, 256), "TB": (-BIG, BIG, 0, 256),
+          "UK": (K, K, -K, -K), "UN": (-K, -K, 0, 0)}
+for _k in SPREAD: SCRATCH[_k] = ("sbuf", [128, 512], "bfloat16")
+for _k in (4, 8, 16): SCRATCH["mk%d" % _k] = ("sbuf", [128, 1024], "bfloat16")
 for _k in range(3): SCRATCH["cw%d" % _k] = ("sbuf", [128, 3072], "bfloat16")
-for _k in range(NG): SCRATCH["g%d" % _k] = ("sbuf", [128, 2048], "bfloat16")
-for _k in range(NFG): SCRATCH["fg%d" % _k] = ("sbuf", [128, 4096], "bfloat16")
-for _k in range(NSO): SCRATCH["so%d" % _k] = ("sbuf", [128, 4096], "bfloat16")
+for _n, _k in (("gr", 10240), ("fg", 16384), ("so", 10240)): SCRATCH[_n] = ("sbuf", [128, _k], "bfloat16")
+for _k in range(NT):
+    for _n in ("ta", "tb"): SCRATCH["%s%d" % (_n, _k)] = ("sbuf", [128, 512], "bfloat16")
 for _k in range(3):
-    for _n in ("ga", "gb", "ta", "tb"): SCRATCH["%s%d" % (_n, _k)] = ("sbuf", [128, 512], "bfloat16")
+    for _n in ("ga", "gb"): SCRATCH["%s%d" % (_n, _k)] = ("sbuf", [128, 512], "bfloat16")
+    SCRATCH["zf%d" % _k] = ("sbuf", [128, 64], "bfloat16")
 for _k in range(2):
-    for _n in ("qq", "th", "ot"): SCRATCH["%s%d" % (_n, _k)] = ("sbuf", [128, 512], "bfloat16")
-    for _n in ("X", "Tg", "hm", "Tk", "Lk"): SCRATCH["%s%d" % (_n, _k)] = ("sbuf", [128, 512], "float16")
-    SCRATCH["xi%d" % _k] = ("sbuf", [128, 32], "int32")
+    for _n in ("qq", "yo"): SCRATCH["%s%d" % (_n, _k)] = ("sbuf", [128, 512], "bfloat16")
+    SCRATCH["ot%d" % _k] = ("sbuf", [128, 128], "bfloat16")
+    for _n in ("X", "Tg", "hm", "Lk"): SCRATCH["%s%d" % (_n, _k)] = ("sbuf", [128, 512], "float16")
     SCRATCH["xu%d" % _k] = ("sbuf", [128, 32], "uint16")
 for _k in range(8): SCRATCH["ps%d" % _k] = ("psum", [128, 512], "float32")
-NDMA = 50
+NDMA = 60
 QS = ("vector", "scalar", "tensor", "pool")
-SEMAPHORES = ["q_" + q for q in QS] + ["d%d" % k for k in range(NDMA)] + ["ra%d" % k for k in range(8)] + ["la%d" % k for k in range(8)]
+SEMAPHORES = ["q_" + q for q in QS] + ["d%d" % k for k in range(NDMA)] + ["ra%d" % k for k in range(6)] + ["la%d" % k for k in range(6)]
 
 SZ = {"float32": 4, "int32": 4, "bfloat16": 2, "uint16": 2, "float16": 2}
 PLAN = {}
+BS = 128
 
 
 def conflict(a, b):
@@ -60,8 +72,6 @@ def build(T, rank, topo, core, phys, cfg):
     ndma = [0]
     ph = ["init"]
     rot = {}
-    BS = cfg["bs"]
-    nb = 512 // BS
 
     def isps(r): return r[0][0] == "#"
 
@@ -83,7 +93,9 @@ def build(T, rank, topo, core, phys, cfg):
         i = len(ops)
         deps = {}
         pin = cfg["pin"].get(ph[0] + kind)
-        if pin and len(opts) > 1: opts = [o for o in opts if o[0][0] == pin]
+        if pin and len(opts) > 1:
+            c = rot[ph[0] + kind] = rot.get(ph[0] + kind, -1) + 1
+            opts = [o for o in opts if o[0][0] == pin[min(c, len(pin) - 1)]]
         qs = set(o[0] for o in opts)
         banks = set()
         for w, lst in ((0, rd), (1, wr)):
@@ -112,8 +124,13 @@ def build(T, rank, topo, core, phys, cfg):
 
     def pick(name, n, w=None):
         k = rot.get(name, 0); rot[name] = k + 1
-        assert w is None or w <= SCRATCH[name + "0"][1][1]
         return R("%s%d" % (name, k % n), 0, w)
+
+    def ring(name, w):
+        a = rot.get(name, 0)
+        if a + w > SCRATCH[name][1][1]: a = 0
+        rot[name] = a + w
+        return R(name, a, a + w)
 
     def half(*rs): return 0.5 if all(sz(r) == 2 for r in rs) else 1
 
@@ -128,45 +145,38 @@ def build(T, rank, topo, core, phys, cfg):
         return ("vector", (n_of(out) * half(out, a), 0, 1, 0), lambda e: e.tensor_scalar(ap(out), ap(a), sc(s1), sc(s2), op0=f, **kw))
 
     def act(out, a, f, bias=0.0, scale=1.0):
-        return ("scalar", (n_of(out), 0, 1, 0), lambda e: e.activation(ap(out), ap(a), f, bias=bias, scale=scale))
+        return ("scalar", (n_of(out), 0, 1, 0), lambda e: e.activation(ap(out), ap(a), f, bias=bias, scale=sc(scale)))
 
     def ts(out, a, s1, s2, f, f2=None, **k):
         return op([vts(out, a, s1, s2, f, f2)], [a] + [s for s in (s1, s2) if isinstance(s, tuple)], [out], **k)
 
     def flex(out, a, o1, o2, **k): return op([o1, o2], [a], [out], **k)
 
-    def vcopy(out, a): return ("vector", (n_of(out) * half(out, a), 0, 1, 0), lambda e: e.tensor_copy(ap(out), ap(a)))
-
-    def copy(out, a, **k): return op([vcopy(out, a)], [a], [out], **k)
-
-    def fcopy(out, a, **k): return flex(out, a, act(out, a, AF.Copy), vcopy(out, a), **k)
+    def fcopy(out, a, **k):
+        return flex(out, a, act(out, a, AF.Copy), ("vector", (n_of(out) * half(out, a), 0, 1, 0), lambda e: e.tensor_copy(ap(out), ap(a))), **k)
 
     def relu(out, a, **k): return flex(out, a, act(out, a, AF.Relu), vts(out, a, 0.0, None, A.max), **k)
 
     def lin(out, a, m, c, **k): return flex(out, a, act(out, a, AF.Copy, bias=float(c), scale=float(m)), vts(out, a, float(m), float(c), A.mult, A.add), **k)
 
-    def mset(out, c, **k): return op([("vector", (n_of(out) * 0.5, 0, 1, 0), lambda e: e.memset(ap(out), c))], [], [out], **k)
+    def mset(out, c): return op([("vector", (n_of(out) * 0.5, 0, 1, 0), lambda e: e.memset(ap(out), c))], [], [out])
 
-    def mm(lst, start=True, stop=True, **k):
+    def mm(lst, start=True, stop=True, each=False, kind="t", after=()):
         def fn(e):
-            for j, (o_, l_, r_) in enumerate(lst): ins = e.matmul(ap(o_), ap(l_), ap(r_), start and j == 0, stop and j == len(lst) - 1)
+            for j, (o_, l_, r_) in enumerate(lst): ins = e.matmul(ap(o_), ap(l_), ap(r_), each or (start and j == 0), each or (stop and j == len(lst) - 1))
             return ins
         rd, wr = [], []
         for (o_, l_, r_) in lst:
             for z, y in ((l_, rd), (r_, rd), (o_, wr)):
                 if z not in y: y.append(z)
-        return op([("tensor", (sum(max(64, n_of(z[0])) for z in lst), 0, len(lst), 0), fn)], rd, wr, kind="t", **k)
+        return op([("tensor", (sum(max(64, n_of(z[0])) for z in lst), 0, len(lst), 0), fn)], rd, wr, kind=kind, after=after)
 
-    def mms(lst, **k):
-        def fn(e):
-            for (o_, l_, r_) in lst: ins = e.matmul(ap(o_), ap(l_), ap(r_), True, True)
-            return ins
-        return op([("tensor", (sum(max(64, n_of(z[0])) for z in lst), 0, len(lst), 0), fn)], [z[1] for z in lst] + [z[2] for z in lst], [z[0] for z in lst], kind="t", **k)
-
-    def gather(out, win, offs_, **k):
+    def gather(out, win, offs_, add=None, clip=False, kind="g"):
         c = (0, n_of(out), 1, 0)
-        return op([("scalar", c, lambda e: e.activation(ap(out), ap(win).indirect(ap(offs_)), AF.Copy)),
-                   ("vector", c, lambda e: e.tensor_copy(ap(out), ap(win).indirect(ap(offs_))))], [win, offs_], [out], kind="g", **k)
+        if add is None and not clip: v = lambda e: e.tensor_copy(ap(out), ap(win).indirect(ap(offs_)))
+        else: v = lambda e: e.tensor_scalar(ap(out), ap(win).indirect(ap(offs_)), add or 0.0, None, op0=A.max if clip else A.add)
+        return op([("scalar", c, lambda e: e.activation(ap(out), ap(win).indirect(ap(offs_)), AF.Relu if clip else AF.Copy, bias=add or 0.0)),
+                   ("vector", c, v)], [win, offs_], [out], kind=kind)
 
     def gmin(out, win, offs_):
         return op([("vector", (0, n_of(out), 1, 0), lambda e: e.tensor_tensor(ap(out), ap(win).indirect(ap(offs_)), ap(out), A.min))], [win, offs_, out], [out], kind="f")
@@ -177,6 +187,10 @@ def build(T, rank, topo, core, phys, cfg):
     def dma(q, out, in_, rd, wr):
         s = "d%d" % ndma[0]; ndma[0] += 1
         return op([(q, (0, 0, 0, 0.1), lambda e: e.dma_start(out(), in_()))], rd, wr, sem=(s, 16), kind="d")
+
+    def add(out, r, wr):
+        s = "d%d" % ndma[0]; ndma[0] += 1
+        return op([("pool", (0, 0, 0, 1.0), lambda e: e.dma_start(out(), ap(r), accum_op=A.add))], [r] + wr, wr, sem=(s, 16), kind="d")
 
     def load(q, r, src, lo, hi): return dma(q, lambda: ap(r), lambda: T[src][:, lo:hi], [], [r])
 
@@ -189,14 +203,19 @@ def build(T, rank, topo, core, phys, cfg):
         kw = {} if SCRATCH[out[0]][2] == "int32" else {"allow_small_or_imprecise_dtypes": True}
         return op([("pool", (2 * n_of(out), 0, 0, 0.18), lambda e: e.iota(ap(out), pattern, base, cm, **kw))], [], [out], kind="p")
 
-    def pcopy(out, a): return gsel(out, a, [[0, n_of(out)]], A.is_ge, 0, 0) if cfg["cp"] else fcopy(out, a, kind="c")
+    def pcopy(out, a): return gsel(out, a, [[0, n_of(out)]], A.is_ge, 0, 0)
 
     def fill(out, c): return iota(out, [[0, n_of(out)]], int(c), 0)
 
+    def zero(out):
+        for a in range(0, n_of(out), 512):
+            r, z = sub(out, a, min(a + 512, n_of(out))), R("zb", 0, min(512, n_of(out) - a))
+            dma("sync", lambda r=r: ap(r), lambda z=z: ap(z), [z], [r])
+
     I = R("iw", 12, 140)
-    P, In, In4, I8, Pn = (R("mb", 128 * k, 128 * k + 128) for k in range(5))
-    kb = R("kb", 0, 256)
-    Mo = R("mo", 0, 128)
+    P, In, In4, I256, P256 = (R("mb", 128 * k, 128 * k + 128) for k in range(5))
+    GS = [R("mb", 128 * k, 128 * k + 128) for k in range(5, 9)]
+    MO = (R("mo", 0, 128), R("mo", 128, 256))
 
     WT = ((1, 0), (-1, 1), (-KC, 0), (1, -KC))
 
@@ -208,16 +227,27 @@ def build(T, rank, topo, core, phys, cfg):
         a = 152 * (1 + t + (2 if m == 4 else 0)) + 12 - (s - t) * (16 // m)
         return R("iw", a, a + 128)
 
-    def chunks(l, which="dch"):
+    def chunks(rnd, l, which="dch"):
         a, out = 0, []
-        for k, w in enumerate(cfg[which][l]):
+        for k, w in enumerate(cfg[which][rnd, l]):
             out.append((k, a, w)); a += w
         return out
+
+    made = set()
+
+    def weights(nm, a=0, b=4, zs=range(4)):
+        s_ = R(nm, 128 * a, 128 * b)
+        for z in zs:
+            w = SPREAD[nm][z]
+            if not w or (nm, a, z) in made: continue
+            src = s_ if (nm, a) in made else R("zb", 0, 128 * (b - a))
+            made.add((nm, a)); made.add((nm, a, z))
+            gsel(s_, src, [[-4, b - a], [-16, 8], [0, 16]], A.not_equal, -4 * a - z, 1, fill=float(w))
 
     cur = {}
 
     def tile(l, k, kind, c, w):
-        a = BS * (3 * (3 * l + kind) + k)
+        a = BS * (3 * (3 * l + kind + (kind and ph[0][0] == "1")) + k)
         if k == 0: cur[l, kind] = []
         cur[l, kind].append((R("tl", a, a + BS), c, w))
         return cur[l, kind][-1][0]
@@ -227,20 +257,27 @@ def build(T, rank, topo, core, phys, cfg):
 
     masked = {}
 
-    def olds(b, tiles, c, w):
+    def olds(b, tiles, c, w, kind):
         cover = [z for z in tiles if z[1] < c + w and c < z[1] + z[2]]
-        if len(cover) == 1: return [(b, Mo, cover[0][0])]
+        if len(cover) == 1: return [(b, MO[kind], cover[0][0])]
         out = []
         for t, a, v in cover:
-            if (a, v) not in masked:
-                z = masked[a, v] = R("mo", 256 + 128 * len(masked), 384 + 128 * len(masked))
-                assert len(masked) <= 10
-                gsel(z, Mo, [[0, 8], [1, 16]], A.is_ge, -2 * (a // BS), 0)
-                gsel(z, z, [[0, 8], [-1, 16]], A.is_ge, 2 * ((a + v) // BS) - 1, 0)
-            out.append((b, masked[a, v], t))
+            lo, hi = max(a, c), min(a + v, c + w)
+            if (kind, lo, hi) not in masked:
+                z = masked[kind, lo, hi] = R("mo", 256 + 128 * len(masked), 384 + 128 * len(masked))
+                if lo: gsel(z, MO[kind], [[0, 8], [1, 16]], A.is_ge, -4 * (lo // BS), 0)
+                if hi < 512: gsel(z, z if lo else MO[kind], [[0, 8], [-1, 16]], A.is_ge, 4 * (hi // BS) - 1, 0)
+            out.append((b, masked[kind, lo, hi], t))
         return out
 
-    def ocol(rnd, l): return 2048 if (l == 1 and rnd and cfg["m"][0, 1] != cfg["m"][1, 1]) else 512 * (l - 1)
+    forms1 = []
+
+    def ocol(rnd, l):
+        if l > 1: return 512 * (l - 1)
+        f = (cfg["dch"][rnd, 1], cfg["m"][rnd, 1])
+        if f not in forms1: forms1.append(f)
+        k = forms1.index(f)
+        return 1536 + 512 * k if k else 0
 
     load("sync", R("o", 0, 512), "safe", 0, 512)
     load("scalar", R("x", 0, 512), "piv", 0, 512)
@@ -251,7 +288,7 @@ def build(T, rank, topo, core, phys, cfg):
     load("sync", R("rpm"), "prem", 0, 256)
     load("sync", R("cw0", 2048, 2560), "lem", 0, 512)
     for k in range(3): load("sync", R("cw%d" % k, 2560, 3072), "leaf", 0, 512)
-    mset(R("ob"), 1.0); mset(R("iw", 0, 152), 0.0); mset(R("W"), 0.0); mset(kb, K)
+    mset(R("ob"), 1.0); mset(R("iw", 0, 152), 0.0); mset(R("zb"), 0.0); mset(R("W"), 0.0)
     mset(R("iw", 152, 456), 0.0); mset(R("iw", 456, 1064), 0.0)
     gsel(I, R("ob"), [[-1, 128]], A.is_equal, 0, 1)
     gsel(P, R("ob"), [[-16, 8], [8, 2], [-1, 8]], A.is_equal, -8, 1)
@@ -263,59 +300,63 @@ def build(T, rank, topo, core, phys, cfg):
             if WT[v][z]: lin(R("W", 144 * v + 15 + z, 144 * v + 143, 16), w8, WT[v][z], 0)
     lin(In, I, -1, 0)
     iota(R("ip", 0, 1), [[0, 1]], 0, 1)
-    ts(R("ip", 4, 5), R("ip", 0, 1), 1, None, A.bitwise_and)
-    COLS = ((6, 2), (2, 6), (32769, 0), (0, 1), (1, 0), (0, -128), (-256, 128))
-
-    def column(k): ts(R("col", k, k + 1), R("ip", 4, 5), float(COLS[k][0]), float(COLS[k][1]), A.mult, A.add)
-    column(4)
-    made = set()
+    r4 = R("ip", 4, 5)
+    ts(r4, R("ip", 0, 1), 3, None, A.bitwise_and)
+    cD, cU, cH, c3 = (R("col", k, k + 1) for k in range(4))
+    ts(c3, r4, -1.0, 3.0, A.mult, A.add)
+    ts(cD, r4, c3, None, A.min)
 
     def parts(m):
         if m > 1 and m not in made:
             made.add(m)
             for t in range(m): gsel(move(m, t, t), I, [[0, 8], [1, m], [0, 16 // m]], A.is_equal, -t, 0)
-    p2 = [[-2, 2], [-16, 8], [0, 16]]
-    for a in range(0, nb, 2):
-        s_ = R("S", 128 * a, 128 * a + 256)
-        gsel(s_, kb, p2, A.is_equal, -1 - 2 * a, 1)
-        gsel(s_, s_, p2, A.not_equal, -2 * a, 1, fill=-2 * K)
-        lin(R("Sn", 128 * a, 128 * a + 256), s_, -1, 0)
+    for a in (0, 2):
+        weights("SA", a, a + 2, (1,)); weights("SB", a, a + 2, (0,))
     mset(R("F", 1024, 4112), 255.0)
 
     def late_consts():
-        if "f" in "".join(cfg["cu"]):
-            iota(R("th1", 0, 256), [[0, 256]], -int(K), 0)
-            lin(Pn, P, -1, 0)
-        for a in range(0, nb, 2):
-            u_ = R("U", 128 * a, 128 * a + 256)
-            gsel(u_, kb, p2, A.is_ge, -2 * a, 1)
-            gsel(u_, u_, [[2, 2], [16, 8], [0, 16]], A.is_ge, 1 + 2 * a, -1)
-            if "f" in "".join(cfg["cu"]):
-                for z, nm in enumerate(("Ra", "Rb")): gsel(R(nm, 128 * a, 128 * a + 256), R("th1", 0, 256), p2, A.is_equal, -2 * a - z, 1)
-        iota(R("mo", 128, 256, 2), [[4, 64]], 1, -2)
-        iota(R("mo", 129, 256, 2), [[-4, 64]], -1, 2)
-        gsel(R("mo", 128, 256), R("mo", 128, 256), [[-2, 64], [0, 2]], A.is_ge, 0, 1)
-        gsel(R("mo", 128, 256), R("mo", 128, 256), [[2, 64], [0, 2]], A.is_ge, 1, -1)
-        lin(Mo, R("mo", 128, 256), 2 ** 25, 0)
-        iota(R("tri"), [[2 * KC, 16], [0, 8], [-2 * KC, 16]], KC, 0)
-        gsel(R("tri"), R("tri"), [[-1, 16], [0, 8], [1, 16]], A.is_ge, 0, 0)
-        gsel(R("tri"), R("tri"), [[0, 16], [-16, 8], [0, 16]], A.is_equal, 0, 1)
-        for k in (3,) + ((5, 6) if cfg["sig"] else ()): column(k)
-        lin(In4, I, -4, 0); lin(I8, I, 8, 0)
-        lin(R("W", 144 * 4 + 15, 144 * 4 + 143, 16), w8, -1, 0)
-        fill(R("kb", 256, 512), K); fill(R("raw", 1536, 1544), 4096); fill(R("Lw", 1536, 1544), 2048)
-        fill(R("Z", 0, 1024), 0); fill(R("Z", 4096, 4112), 0)
-        wide(0, 512)
-        for l in (3, 2, 1, 0):
-            z, x_ = R("zk", 512 * l, 512 * l + 512), R("x", 512 * l, 512 * l + 512)
-            flex(z, x_, act(z, x_, AF.Relu, bias=K, scale=-K), vts(z, x_, 0.0, K, A.is_equal, A.mult))
+        for a in (0, 2): weights("SA", a, a + 2); weights("SB", a, a + 2)
+        b4, p4 = R("b4"), [[-4, 4], [-16, 8], [0, 16]]
+        gsel(b4, R("zb"), p4, A.is_gt, -3, 1, fill=1.0)
+        gsel(b4, b4, p4, A.is_ge, 0, 1)
+        cn, ck, ca, cb, c1, c2 = (R("col", k, k + 1) for k in range(6, 12))
+        ts(cn, r4, 2.0, -K, A.is_lt, A.mult); ts(ck, cn, -2.0, -K, A.mult, A.add)
+        ts(c1, r4, 2 * BIG / K, -BIG / K, A.mult, A.add); ts(c2, r4, 3.0, 256.0, A.is_equal, A.mult)
+        ts(ca, c1, cn, c2, A.mult, A.add); ts(c1, c1, -1.0, None, A.mult); ts(cb, c1, cn, c2, A.mult, A.add)
+        weights("UN")
+        for nm, c in (("TA", ca), ("TB", cb), ("UK", ck)): op([act(R(nm), b4, AF.Copy, scale=c), vts(R(nm), b4, c, None, A.mult)], [b4, c], [R(nm)])
+        z1 = R("zb", 0, 128)
+        for z, v in ((I256, -256.0), (In4, -4.0)): gsel(z, z1, [[-1, 128]], A.not_equal, 0, 1, fill=v)
+        gsel(P256, z1, [[-16, 8], [8, 2], [-1, 8]], A.not_equal, -8, 1, fill=-256.0)
+        for z, v in zip(GS, (2 ** 30, -2 ** 17, -2 ** 30, 2 ** 17)):
+            gsel(z, z1, [[-16, 8], [0, 16]], A.is_gt, -15, 1, fill=float(v)); gsel(z, z, [[-16, 8], [0, 16]], A.is_ge, 0, 1)
+        for kind in (1, 0):
+            zero(MO[kind])
+            for a, b, v in ((0, 0, 1), (1, 0, -1), (0, 1, -1), (1, 1, 1)) + (((2, 2, 1),) if kind else ((0, 2, 1), (1, 2, 1))):
+                gsel(sub(MO[kind], b, 128, 4), sub(MO[kind], b, 128, 4), [[-4, 32]], A.not_equal, -a, 1, fill=v * 2.0 ** 25)
+        gsel(R("g0"), R("zb"), [[0, 4], [-16, 8], [0, 16]], A.not_equal, 0, 1, fill=-2.0 * KC)
+        for a in range(0, 16, 4):
+            t_ = R("tri", 128 * a, 128 * a + 512)
+            gsel(t_, R("g0"), [[-1, 4], [0, 8], [1, 16]], A.is_gt, -a, 0)
+            gsel(t_, t_, [[-1, 4], [-256, 8], [1, 16]], A.not_equal, -a, 16, fill=float(KC))
+        ts(cU, r4, 3.0, None, A.is_lt)
+        ts(cH, r4, 65535.0, -32767.5, A.mult, A.add)
+        w4 = R("W", 144 * 4 + 15, 144 * 4 + 143, 16)
+        gsel(w4, R("zb", 0, 8), [[-16, 8]], A.is_gt, -15, 1, fill=-1.0); gsel(w4, w4, [[-16, 8]], A.is_ge, 0, 1)
+        fill(R("kb"), K); fill(R("raw", 1536, 1544), 4096); fill(R("Lw", 1536, 1544), 2048)
+        fill(R("Z", 4096, 4112), 0)
+        for l in range(4):
+            if l == 0 or l in cfg["zd"]: zero(R("Z", 1024 * l, 1024 * l + 1024))
+        fill(R("ez"), 0)
+        for z in range(2): gsel(R("ez", 136 * z + 4, 136 * z + 132), I, [[0, 32], [1, 4]], A.is_equal, -z, 0)
+        pcopy(R("Lw", 0, 512), R("Lh", 0, 512))
         iota(R("rp2", 0, 256), [[0, 2], [512, 4], [0, 32]], 512, 0)
         tt(R("rp2", 256, 512), R("rpm"), R("rp2", 0, 256), A.subtract)
-        copy(R("po"), R("rp2", 256, 512))
+        fcopy(R("po"), R("rp2", 256, 512))
 
     def lay(grp, col, L):
         for m, a, w in grp:
-            if m == 1: ts(R("off", col + a, col + a + w), sub(L, a, a + w), 2048.0, None, A.add)
+            if m == 1: lin(R("off", col + a, col + a + w), sub(L, a, a + w), 1, 2048, kind="l")
         grp = [z for z in grp if z[0] > 1]
         if not grp: return
         b = bank(n_of(L))
@@ -323,99 +364,78 @@ def build(T, rank, topo, core, phys, cfg):
             parts(m)
             n = w // m
             for t in range(m): mm([(sub(b, a + t * n, a + t * n + n), move(m, t, s), sub(L, a + s, a + w, m)) for s in range(m)])
-        runs = []
-        for m, a, w in grp:
-            if runs and runs[-1][1] == a: runs[-1][1] = a + w
-            else: runs.append([a, a + w])
-        for a, e_ in runs: ts(R("off", col + a, col + e_), sub(b, a, e_), 2048.0, None, A.add)
-
-    def wide(col, w):
-        b = bank(w)
-        mm([(b, I, R("Lh", col, col + w))])
-        fcopy(R("Lw", col, col + w), b, kind="l")
+        a, e_ = grp[0][1], grp[-1][1] + grp[-1][2]
+        lin(R("off", col + a, col + e_), sub(b, a, e_), 1, 2048, kind="l")
 
     def first_lists(l, rnd):
         a = 512 * (l - 1)
-        if rnd == 0: ts(R("Lh", a, a + 512), raw(a, 512), -2048.0, None, A.add)
-        lay([(cfg["m"][rnd, l][k], c, w) for k, c, w in chunks(l)], ocol(rnd, l), R("Lh", a, a + 512))
+        if rnd == 0: lin(R("Lh", a, a + 512), raw(a, 512), 1, -2048, kind="l")
+        lay([(cfg["m"][rnd, l][k], c, w) for k, c, w in chunks(rnd, l)], ocol(rnd, l), R("Lh", a, a + 512))
 
-    def state(forms, n0, w, srcs, neg, old, new, after, sig):
-        cb = bank(BS)
+    def state(n0, w, srcs, kind, old, new, after):
+        cb = new and bank(BS)
         x_ = R("x", n0, n0 + w)
-        first = True
-        if old:
-            mm(olds(cb, old, n0 % 512, w), stop=False, after=[after]); first = False
-        for z in range(2):
-            b, t = bank(w), pick("ta" if z == 0 else "tb", 3, w)
-            if forms[z] == "v":
-                mm([(b, (I, P)[z], x_)], after=[after])
-                tt(t, srcs[z], b, A.is_lt)
-            else:
-                mm([(b, (I, P)[z], x_)], stop=False, after=[after])
-                mm([(b, In, srcs[z])], start=False)
-                relu(t, b)
-            mm([(cb, row(2 * (j + n0 % 512 // BS) + z, ((3, 0), (1, 2))[neg][z]), sub(t, j * BS, j * BS + BS)) for j in range(w // BS)], start=first, stop=z == 1)
-            first = False
-        c_, d_ = R("col", 3 + neg, 4 + neg), R("col", 5 + neg, 6 + neg)
-        v = vts(new, cb, c_, None, A.is_ge)
-        if not sig: return op([v], [cb, c_], [new], kind="i")
-        return op([("scalar", (BS, 0, 1, 0), lambda e: e.activation(ap(new), ap(cb), AF.Sigmoid, bias=ap(d_), scale=256.0)), v], [cb, c_, d_], [new], kind="i")
-
-    def sides(tab, n0, w, t, names, after=None):
+        if old and new: mm(olds(cb, old, n0 % 512, w, kind), stop=False, after=[after])
         out = []
         for z in range(2):
-            b = bank(w)
-            mm([(b, (I, P)[z], R(tab, n0, n0 + w))] + spread(b, names[z], t, n0 % 512), after=[after])
-            out.append(b)
-        return out
+            b, t = bank(w), pick("ta" if z == 0 else "tb", NT, w)
+            mm([(b, (I, P)[z], x_)], stop=False, after=[after])
+            mm([(b, In, srcs[z])], start=False)
+            relu(t, b, kind="a")
+            if new: mm([(cb, row(4 * (j + n0 % 512 // BS) + z, ((1, 2), (3, 0))[kind][z]), sub(t, j * BS, j * BS + BS)) for j in range(w // BS)], start=not old and not z, stop=z == 1)
+            out.append(t)
+        return new and ts(new, cb, (cD, cU)[kind], None, A.is_ge, kind="i"), out
 
     def least(rnd, l, k, c, w):
         m = cfg["m"][rnd, l][k]
         h = 16 // m
-        so = pick("so", NSO, w * h)
-        gp = cfg["gg"] if l == 4 else cfg["gp"]
-        wp, ws = min(w, gp // h), min(w, max(gp, cfg["sp"]) // h)
-        for j0 in range(0, w, ws):
-            v0 = min(ws, w - j0)
-            gb = pick("g", NG, v0 * h)
-            for j in range(j0, j0 + v0, wp):
-                v = min(wp, j0 + v0 - j)
-                for t in range(m):
-                    a = ocol(rnd, l) + c + (t * w + j) // m
-                    i = (gmin if t else gather)(sub(gb, (j - j0) * h, (j - j0 + v) * h), R("F", 0, 4097), R("off", a, a + v // m))
-                    if t == 0: g0 = i
-            if (h, v0) not in made:
-                made.add((h, v0))
-                have = max([0] + [z[1] for z in made if isinstance(z, tuple) and z[0] == h and z[1] != v0])
-                if have < v0:
-                    fill(R("mk%d" % h, have * h, v0 * h), 0); fill(R("mk%d" % h, have * h, v0 * h, h), 255)
-            g0 = scan(sub(so, j0 * h, (j0 + v0) * h), R("mk%d" % h, 0, v0 * h), gb)
-        return sub(so, h - 1, w * h, h), (g0 if cfg["pre"] else i), i
+        so, v = ring("so", w * h), cfg["gp"] // h
+        for j in range(0, w, v):
+            gb = ring("gr", v * h)
+            for t in range(m):
+                a = ocol(rnd, l) + c + (t * w + j) // m
+                (gmin if t else gather)(gb, R("F", 0, 4097), R("off", a, a + v // m))
+            if ("mk", h) not in made:
+                made.add(("mk", h))
+                zero(R("mk%d" % h)); fill(R("mk%d" % h, 0, 1024, h), 255)
+            g0 = scan(sub(so, j * h, (j + v) * h), R("mk%d" % h), gb)
+        return sub(so, h - 1, w * h, h), g0
 
     lastup = {}
+
+    def fresh(rnd, n0, w): return R("as%d" % rnd, n0, n0 + w) if rnd and n0 < 512 else R("o", n0, n0 + w)
 
     def down(rnd, l):
         ph[0] = "%dD%d" % (rnd, l)
         todo = []
-        for k, c, w in chunks(l):
+        for k, c, w in chunks(rnd, l):
             n0 = 512 * l + c
-            o_ = R("o", n0, n0 + w)
-            g0 = gl = None
-            if l: src, g0, gl = least(rnd, l, k, c, w)
-            else: src = R("as%d" % rnd, c, c + w) if rnd else o_
+            g0 = None
+            if l: src, g0 = least(rnd, l, k, c, w)
+            else: src = fresh(rnd, n0, w)
             if l == 0 and rnd: g0 = lastup[0]
-            state(cfg["td"][rnd], n0, w, (src, src), True, cur[l, 1] if rnd else None, tile(l, k, 0, c, w), g0, cfg["sig"] and rnd)
-            if rnd:
+            old = cur[l, 1] if rnd else None
+            todo.append((c, n0, w, src, state(n0, w, (src, src), 0, old, tile(l, k, 0, c, w), g0)[1]))
+            if rnd == 2:
                 b = bank(w)
-                mm([(b, I, src)] + spread(b, "U", cur[l, 1], c))
-                tt(o_, b, R("kx", n0, n0 + w), A.min)
-            elif l: pcopy(o_, src)
-            todo.append((k, n0, w, o_ if rnd else src))
-        if cfg["ew"][rnd][l] == "w": todo = [(0, 512 * l, 512, R("o", 512 * l, 512 * l + 512))]
-        for k, n0, w, src in todo:
-            for z, b in enumerate(sides("x", n0, w, cur[l, 0], ("S", "Sn"), gl)):
-                tt(R("F", 2 * n0 + z, 2 * n0 + 2 * w, 2), src, b, A.max, kind="e")
-        if rnd == 2: store("ys", 512 * l, 512 * l + 512, R("o", 512 * l, 512 * l + 512))
+                mm([(b, I, src)] + spread(b, "UN", old, c))
+                relu(R("o", n0, n0 + w), b, kind="o")
+            elif l: pcopy(R("o", n0, n0 + w), src)
+        for c, n0, w, src, rs in todo:
+            for z in range(2):
+                b, f_ = bank(w), R("F", 2 * n0 + z, 2 * n0 + 2 * w, 2)
+                two = spread(b, ("SA", "SB")[z], cur[l, 0], c)
+                if rnd == 0 and cfg["pf"][l][c > 0] == "p":
+                    mm([(b, (I, P)[z], R("x", n0, n0 + w))], stop=False, after=[g0]); mm(two, start=False)
+                    tt(f_, b, src, A.max, kind="e")
+                    continue
+                mm([(b, I, src)], stop=False); mm([(b, I, rs[z])], start=False, stop=False); mm(two, start=False)
+                if rnd: tt(f_, b, R("kx", n0, n0 + w), A.max, kind="e")
+                else: fcopy(f_, b, kind="e")
+        if rnd == 2:
+            a, k_, y_ = 512 * l, R("kx", 512 * l, 512 * l + 512), ("ys", 512 * l, 512 * l + 512, 1)
+            dma("sync", lambda: T["ys"][:, a:a + 512], lambda: ap(k_), [k_], [y_])
+            add(lambda: T["ys"][:, a:a + 512], R("o", a, a + 512), [y_])
 
     nremote = [0]
 
@@ -425,99 +445,106 @@ def build(T, rank, topo, core, phys, cfg):
         rid, pid = topo.addr(d)[:2]
         mask = sum(1 << e for e in topo.engines(core, d)[:8])
         i = op([("pool", (0, 0, 0, 1.0), lambda e: e.remote_dma(ap(dst), ap(src), T.sem["ra%d" % k], T.sem["la%d" % k], pid, rid, mask))], [src], [], sem=("la%d" % k, 8), kind="r")
-        op([(None, (0, 0, 0, 4.0 if k else 7.0), None)], [], [dst], sem=("ra%d" % k, 8), after=[i], kind="a")
+        op([(None, (0, 0, 0, 4.0 if k else 7.0), None)], [], [dst], sem=("ra%d" % k, 8), after=[i], kind="w")
 
     def ghosts(rnd):
         ph[0] = "%dG" % rnd
-        for k, c, w in chunks(4):
+        for k, c, w in chunks(rnd, 4):
             o_ = R("o", 2048 + c, 2048 + c + w)
-            pcopy(o_, least(rnd, 4, k, c, w)[0])
+            fcopy(o_, least(rnd, 4, k, c, w)[0], kind="c")
             if rnd < 2: send(o_, R("as%d" % (rnd + 1), c, c + w), rank + 1)
             else: store("ys", 2048 + c, 2048 + c + w, o_)
 
     def up(rnd, l):
         ph[0] = "%dU%d" % (rnd, l)
         cw = "cw%d" % rnd
-        for k, c, w in chunks(l, "uch"):
+        zd = rnd < 2 and l in cfg["zd"]
+        for k, c, w in chunks(rnd, l, "uch"):
             n0 = 512 * l + c
+            x_, c_ = R("x", n0, n0 + w), R(cw, n0, n0 + w)
             ab = (pick("ga", 3, w), pick("gb", 3, w))
-            gs = [gather(ab[z], R(cw, 512 * l + 512, 3072), R("po", 128 * z + n0 // 16, 128 * z + (n0 + w) // 16)) for z in range(2)]
+            gs = [gather(ab[z], R(cw, 512 * l + 512, 3072), R("po", 128 * z + n0 // 16, 128 * z + (n0 + w) // 16), clip=True) for z in range(2)]
+            direct = cfg["cu"][rnd][l] == "d"
             new = tile(l, k, 1, c, w)
-            lastup[0] = state(cfg["tu"][rnd], n0, w, ab, False, cur[l, 0], new, gs[0], cfg["sig"])
-            q = pick("qq", 2, w)
-            if cfg["cu"][rnd][l] == "v":
-                ba, bb = sides("zk", n0, w, cur[l, 1], ("Sn", "S"))
-                tt(ba, ab[0], ba, A.min)
-                tt(q, ab[1], bb, A.min)
-            else:
-                b, y = bank(w), pick("th", 2, w)
-                mm([(b, I, R("zk", n0, n0 + w))] + spread(b, "U", cur[l, 1], c))
-                flex(y, b, act(y, b, AF.Relu, bias=K, scale=-1.0), vts(y, b, 0.0, K, A.is_equal, A.mult))
-                bb, ba = bank(w), bank(w)
-                mm([(bb, I, ab[1])] + spread(bb, "Ra", cur[l, 1], c), stop=False)
-                mm([(bb, Pn, y)], start=False)
-                relu(q, bb)
-                mm([(ba, I, ab[0])] + spread(ba, "Rb", cur[l, 1], c), stop=False)
-                mm([(ba, In, y)], start=False)
-            tt(R(cw, n0, n0 + w), q, ba, A.max)
+            lastup[0], rs = state(n0, w, ab, 1, cur[l, 0], None if rnd == 2 and direct else new, gs[0])
+            q, now = pick("qq", 2, w), cur[l, 1]
+            ba, bb = bank(w), bank(w)
+            for z, (b, m_, nm) in enumerate(((ba, I256, "TA"), (bb, P256, "TB"))):
+                if direct:
+                    mm([(b, m_, x_)] + spread(b, nm, cur[l, 0], c), stop=False, after=[gs[1]])
+                    mm([(b, GS[2 * z], rs[0])], start=False, stop=False); mm([(b, GS[2 * z + 1], rs[1])], start=False)
+                else:
+                    mm([(b, m_, x_)], stop=False, after=[gs[1]]); mm(spread(b, nm, now, c), start=False)
+            tt(ba, ab[0], ba, A.min)
+            tt(q, ab[1], bb, A.min)
+            tt(c_, q, ba, A.max)
             if rnd == 2:
-                store("yc", n0, n0 + w, R(cw, n0, n0 + w))
+                y = pick("yo", 2, w)
+                relu(y, c_, kind="c")
+                store("yc", n0, n0 + w, y)
                 continue
-            if l:
+            if l and not zd:
                 b = bank(w)
-                mms(spread(b, "S", cur[l, 1], c))
+                mm(spread(b, "TA", now, c), each=True)
                 za, zb = R("Z", 2 * n0, 2 * n0 + 2 * w, 2), R("Z", 2 * n0 + 1, 2 * n0 + 2 * w, 2)
-                flex(za, b, act(za, b, AF.Relu, scale=-0.5 / K), vts(za, b, 0.0, None, A.is_lt), kind="z")
-                flex(zb, b, act(zb, b, AF.Relu, scale=1 / K), vts(zb, b, 0.0, None, A.is_gt), kind="z")
-            b = bank(w)
-            mm([(b, In, R("o", n0, n0 + w))] + spread(b, "U", cur[l, 1], c))
-            lin(R("kx", n0, n0 + w), b, -1, K, kind="k")
+                flex(za, b, act(za, b, AF.Relu, scale=1 / BIG, bias=-256 / BIG), vts(za, b, 1024.0, None, A.is_gt), kind="z")
+                flex(zb, b, act(zb, b, AF.Relu, scale=-1 / BIG, bias=256 / BIG), vts(zb, b, 0.0, None, A.is_lt), kind="z")
+            b, k_ = bank(w), R("kx", n0, n0 + w)
+            mm([(b, I, fresh(rnd, n0, w))] + spread(b, "UK", now, c))
+            if rnd and l in cfg["ka"]:
+                y = ring("nw", w)
+                relu(y, b, kind="k")
+                add(lambda k_=k_: ap(k_), y, [k_])
+            elif rnd: tt(k_, b, k_, A.max, kind="k")
+            else: relu(k_, b, kind="k")
+        if zd:
+            b, zf = bank(64), pick("zf", 3)
+            for z in range(2):
+                mm([(sub(b, 32 * z, 32 * z + 32), R("ez", 136 * z + 4 - j + z, 136 * z + 132 - j + z), sub(new, 32 * j, 32 * j + 32)) for j in range(4)])
+            for z in range(2): fcopy(sub(zf, z, 64, 2), sub(b, 32 * z, 32 * z + 32), kind="z")
+            dma("sync", lambda: T["Z"][0:128:16, 1024 * l:1024 * l + 1024], lambda: ap(zf), [zf], [R("Z", 1024 * l, 1024 * l + 1024)])
         if rnd < 2 and l == 0: send(R(cw, 0, 512), R("cw%d" % (rnd + 1), 2048, 2560), rank - 1)
 
     def splice(rnd, l):
         ph[0] = "%dS%d" % (rnd, l)
-        for grp in ([chunks(l)] if cfg["sw"][l] else [[z] for z in chunks(l)]):
-            c, w = grp[0][1], sum(z[2] for z in grp)
-            col = 512 * (l - 1) + c
-            L, fl = R("Lh", col, col + w), bank(w)
-            for k, c1, w1 in grp:
-                m = cfg["m"][rnd - 1, l][k]
-                h, n = 16 // m, w1 // m
-                for t in range(m):
-                    fg, a = pick("fg", NFG, w1 * h), col + c1 - c + t * n
-                    for j in range(0, n, cfg["fp"] // 16):
-                        v = min(cfg["fp"] // 16, n - j)
-                        gather(sub(fg, 16 * j, 16 * (j + v)), R("Z", 0, 4097), R("off", a + j, a + j + v))
-                    for r0 in range(0, h, 4):
-                        o_ = sub(fl, c1 - c, c1 - c + w1)
-                        last_mm = mm([(o_, blk("tri", t * h + r), sub(fg, r, w1 * h, h)) for r in range(r0, r0 + 4)] + ([] if t + r0 else [(o_, In4, R("kb", 0, w1))]),
-                                     start=t + r0 == 0, stop=t * h + r0 == 12)
-            L1 = pick("X", 2, w)
-            i = tt(L1, L, fl, A.max)
-            b = bank(w // 16)
-            mm([(b, row(q, 4), sub(L, q, w, 16)) for q in range(16)], stop=False, after=[last_mm])
-            mm([(b, row(q), sub(L1, q, w, 16)) for q in range(16)], start=False)
-            xi, xu = pick("xi", 2, w // 16), pick("xu", 2, w // 16)
-            ts(xi, b, -0.5, 1535.75, A.mult, A.add, kind="i")
-            i = copy(xu, xi, kind="i")
-            tg = pick("Tg", 2, w)
-            win, add = (R("raw", 0, 1537), -2048.0) if rnd == 1 else (R("Lw", 0, 1537), 0.0)
-            op([("vector", (0, w, 1, 0), lambda e, tg=tg, xu=xu, win=win, add=add: e.tensor_scalar(ap(tg), ap(win).indirect(ap(xu)), add, None, op0=A.add))], [win, xu], [tg])
-            b, hm = bank(w), pick("hm", 2, w)
-            mm([(b, P, L1)], after=[i])
-            tt(hm, tg, b, A.max)
-            b = bank(BS)
-            mm([(b, row(2 * j + 1), sub(hm, j * BS, j * BS + BS)) for j in range(w // BS)])
-            ot = pick("ot", 2, BS)
-            ts(ot, b, 32768.0, 8.0, A.is_ge, A.mult, kind="i")
-            lk, b = pick("Lk", 2, w), bank(w)
-            mm([(b, I, L)] + spread(b, "S", [(ot, 0, w)]))
-            tt(lk, L1, b, A.min)
-            b = bank(w)
-            mm([(b, P, tg), (b, I8, R("kb", 0, w))] + spread(b, "Sn", [(ot, 0, w)]))
-            tt(L, lk, b, A.min)
-            lay([(cfg["m"][rnd, l][k], c1 - c, w1) for k, c1, w1 in grp], col, L)
-            if rnd == 1 and l < 4: wide(col, w)
+        col, w = 512 * (l - 1), 512
+        L, fl = R("Lh", col, col + w), bank(w)
+        for k, c1, w1 in chunks(rnd - 1, l):
+            m = cfg["m"][rnd - 1, l][k]
+            h, n = 16 // m, w1 // m
+            for t in range(m):
+                fg, a = ring("fg", w1 * h), col + c1 + t * n
+                for j in range(0, n, cfg["fp"][l - 2] // 16):
+                    v = min(cfg["fp"][l - 2] // 16, n - j)
+                    gather(sub(fg, 16 * j, 16 * (j + v)), R("Z", 0, 4097), R("off", a + j, a + j + v))
+                for r0 in range(0, h, 4):
+                    o_ = sub(fl, c1, c1 + w1)
+                    last_mm = mm([(o_, blk("tri", t * h + r), sub(fg, r, w1 * h, h)) for r in range(r0, r0 + 4)] + ([] if t + r0 else [(o_, In4, R("kb", 0, w1))]),
+                                 start=t + r0 == 0, stop=t * h + r0 == 12, kind="r")
+        L1 = pick("X", 2, w)
+        tt(L1, L, fl, A.max)
+        b = bank(w // 16)
+        mm([(b, row(q, 4), sub(L, q, w, 16)) for q in range(16)], stop=False, after=[last_mm])
+        mm([(b, row(q), sub(L1, q, w, 16)) for q in range(16)], start=False)
+        xu = pick("xu", 2, w // 16)
+        i = ts(xu, b, -0.5, 1535.75, A.mult, A.add, kind="i")
+        tg = pick("Tg", 2, w)
+        gather(tg, R("raw" if rnd == 1 else "Lw", 0, 1537), xu, add=-2048.0 if rnd == 1 else 0.0, kind="u")
+        b, hm = bank(w), pick("hm", 2, w)
+        mm([(b, P, L1)], after=[i])
+        tt(hm, tg, b, A.max)
+        b = bank(BS)
+        mm([(b, row(4 * j, 1), sub(hm, j * BS, j * BS + BS)) for j in range(w // BS)])
+        ot = pick("ot", 2, BS)
+        ts(ot, b, cH, 2.0, A.is_ge, A.mult, kind="i")
+        lk, b = pick("Lk", 2, w), bank(w)
+        mm([(b, I, L)] + spread(b, "SA", [(ot, 0, w)]))
+        tt(lk, L1, b, A.min)
+        b = bank(w)
+        mm([(b, P, tg)] + spread(b, "SB", [(ot, 0, w)]))
+        tt(L, lk, b, A.min)
+        lay([(cfg["m"][rnd, l][k], c1, w1) for k, c1, w1 in chunks(rnd, l)], col, L)
+        if rnd == 1 and l < 4: pcopy(R("Lw", col, col + w), L)
 
     down(0, 0)
     for l in (1, 2, 3):
@@ -527,7 +554,8 @@ def build(T, rank, topo, core, phys, cfg):
     ph[0] = "late"
     first_lists(4, 0)
     late_consts()
-    if ocol(1, 1): first_lists(1, 1)
+    for rnd in (1, 2):
+        if ocol(rnd, 1) not in [ocol(r, 1) for r in range(rnd)]: first_lists(1, rnd)
     for rnd in range(3):
         if rnd:
             for l in (2, 3, 4): splice(rnd, l)
@@ -537,12 +565,17 @@ def build(T, rank, topo, core, phys, cfg):
     return ops
 
 
-MODELS = ((1.0, 1.1, 0.05, 0.1), (1.0, 1.55, 0.05, 0.08), (1.4, 2.0, 0.05, 0.12), (1.2, 1.3, 0.06, 0.25))
+MODELS = ((1.0, 1.04, 0.03, 0.2, 0.00045, 1.2, 2.0), (1.0, 1.55, 0.04, 0.1, 0.00045, 1.1, 0.5), (1.3, 1.9, 0.05, 0.2, 0.00045, 1.0, 3.0))
+LAND = 3.0
 QALL = (None, "vector", "scalar", "tensor", "pool", "sync")
 
 
 def cost(q, c, md):
-    if q == "tensor": return c[0] * 0.00045 * md[0] + c[2] * 0.006
+    if q == "tensor": return c[0] * md[4] * md[0] + c[2] * 0.006
+    if q == "pool": return (c[0] * 0.00083 * md[0] + c[3]) * md[5]
+    if q is None: return c[3] + md[6]
+    if q == "sync": return 0.4
+    if q == "scalar": return (max(64, c[0]) if c[0] else c[1] * md[1]) * 0.00083 * md[0] + md[2] + 0.025 + c[3]
     return ((max(64, c[0]) if c[0] else 0) + c[1] * md[1]) * 0.00083 * md[0] + c[2] * md[2] + c[3]
 
 
@@ -579,7 +612,7 @@ def plan(ops, md, cfg):
 
 
 def forward(ops, md, cfg, ends=None, asg0=None):
-    offs, look, vb = cfg["offs"], cfg["look"], cfg["vb"]
+    look, vb = cfg["look"], cfg["vb"]
     n = len(ops)
     us = [{x[0]: cost(x[0], x[1], md) for x in o["opts"]} for o in ops]
     lat = [(2.2 if o["sem"] and None not in o["qs"] else 0.0) + md[3] for o in ops]
@@ -594,7 +627,6 @@ def forward(ops, md, cfg, ends=None, asg0=None):
     pr = [0.0] * n
     for i in range(n - 1, -1, -1): pr[i] = max([pr[s] for s in succ[i]] or [0.0]) + lat[i] + min(us[i].values())
     if ends: pr = backward(ops, us, lat, succ, ends, asg0)
-    pr = [pr[i] + offs.get(ops[i]["name"], 0.0) + offs.get(ops[i]["name"][:-1], 0.0) for i in range(n)]
     opens = [any(users[b][0] == i for b in o["banks"]) for i, o in enumerate(ops)]
     rt, fin, asg = [0.0] * n, [0.0] * n, [None] * n
     free = {q: 0.0 for q in QALL}
@@ -624,11 +656,6 @@ def forward(ops, md, cfg, ends=None, asg0=None):
         bias = vb if bq == "vector" else 0.0
         key = lambda z: pr[z[1]] - (bias if len(us[z[1]]) > 1 else 0.0)
         now = [z for z in bc if z[0] <= bt + 1e-9]
-        if bq == "vector":
-            now = [z for z in now if len(us[z[1]]) == 1 or free["scalar"] - bt + sum(us[j]["scalar"] for j in ready["scalar"] if pr[j] > pr[z[1]]) >= cfg["back"] * us[z[1]][bq]]
-            if not now:
-                free[bq] = bt + 0.1
-                continue
         best = max(now, key=key)
         ahead = []
         if bq in ("vector", "scalar") and us[best[1]][bq] > 0.3:
@@ -695,73 +722,288 @@ def replay(ops, pl, md):
     return max(fin.values())
 
 
-def polish(ops, pl, tries, temp=0.05):
-    order, asg, phys, prev = list(pl[0]), list(pl[1]), pl[2], pl[3]
+def search(ops, pl, cfg, tries, temp, seed, lags):
+    order, asg = list(pl[0]), [QALL.index(q) for q in pl[1]]
     n = len(ops)
-    pre = []
+    anc, pre = [0] * n, []
     for i, o in enumerate(ops):
-        d = {j: k != "w" and not ops[j]["sem"] for j, k in o["deps"].items()}
-        for j in prev.get(i, ()): d.setdefault(j, True)
+        d = {j: int(w != "w" and not ops[j]["sem"]) for j, w in o["deps"].items()}
+        far = 0
+        for j in d: far |= anc[j]
+        anc[i] = far | sum(1 << j for j in d)
+        d = {j: s for j, s in d.items() if not far >> j & 1}
         if None in o["qs"]:
-            for j in o["after"]: d[j] = None
+            for j in o["after"]: d[j] = 2
         pre.append(list(d.items()))
     succ = [[] for _ in range(n)]
     for i in range(n):
-        for j, _ in pre[i]: succ[j].append(i)
-    us = [[{x[0]: cost(x[0], x[1], md) for x in o["opts"]} for o in ops] for md in MODELS]
-    tail = [2.2 if o["sem"] and None not in o["qs"] else 0.0 for o in ops]
-    wt = [1 / (m[0] * (1 + m[1])) for m in MODELS]
+        for j, s in pre[i]: succ[j].append((i, s))
+    pj, sj = [[j for j, s in z] for z in pre], [[j for j, s in z] for z in succ]
+    users = {}
+    for i, o in enumerate(ops):
+        for b in o["banks"]: users.setdefault(b, []).append(i)
+    opens = {u[0]: b for b, u in users.items()}
+    lastof = {u[0]: u[-1] for u in users.values()}
+    us = [[[0.0] * 6 for o in ops] for md in MODELS]
+    for x, md in enumerate(MODELS):
+        for i, o in enumerate(ops):
+            for z in o["opts"]: us[x][i][QALL.index(z[0])] = cost(z[0], z[1], md)
+    both = [len(o["opts"]) > 1 for o in ops]
+    tail = [LAND if o["sem"] and None not in o["qs"] else 0.0 for o in ops]
+    ends = [i for i in range(n) if tail[i] and not succ[i]]
+    lag = [(i, lags[o["name"][1:]]) for i, o in enumerate(ops) if o["name"][1:] in lags]
+    wt = [w / (m[0] * (1 + m[1])) for m, w in zip(MODELS, cfg["wt"])]
+    w0, w1, w2 = (m[3] for m in MODELS)
+    u0, u1, u2 = us
+    bp, nb = [-1] * n, [-1] * n
+    for i, u in pl[3].items(): bp[i] = u[-1]; nb[u[-1]] = i
+    bk = dict(pl[2])
+    seq = [[i for i in order if asg[i] == q] for q in range(6)]
+    mp, mn = [-1] * (n + 1), [-1] * (n + 1)
+    for s in seq[1:]:
+        for a, b in zip(s, s[1:]): mp[b], mn[a] = a, b
+    pos = [0] * n
+    for p, j in enumerate(order): pos[j] = p
+    E_, H_, T_, J_ = ([[0.0] * (n + 1) for x in range(3)] for y in range(4))
+    marks = ([False] * (n + 1), [False] * (n + 1))
+    win = [0, n, n]
 
-    def run(k):
-        wake, u, fin, free, why, lastq = MODELS[k][3], us[k], [0.0] * n, {q: 0.0 for q in QALL}, [-1] * n, {}
-        st = [0.0] * n
-        for i in order:
+    def sweep(seeds, back):
+        (e0, e1, e2), (h0, h1, h2), near, far, bi, bo, mi, mo = (T_, J_, succ, pj, nb, bp, mn, mp) if back else (E_, H_, pre, sj, bp, nb, mp, mn)
+        left, log, mark = 0, [], marks[back]
+        mark[n] = True
+        for i in seeds:
+            if not mark[i]: mark[i] = True; left += 1
+        p = [pos[i] for i in seeds if i >= 0]
+        for i in (order[max(0, win[0] - 40):max(p) + 1][::-1] if back else order[min(p):win[2]]):
+            if not mark[i]: continue
+            mark[i] = False
             q = asg[i]
-            t, y = (free[q], lastq.get(q, -1)) if q else (0.0, -1)
-            for j, soft in pre[i]:
-                v = fin[j] - 2.2 if soft is None else fin[j] if soft and asg[j] == q else fin[j] + wake
-                if v > t: t, y = v, j
-            st[i] = t
-            t += u[i][q]
-            free[q], lastq[q], why[i], fin[i] = t, i, y, t + tail[i]
-        e_ = max(fin)
-        return e_, why, fin.index(e_), st
-    seed = [12345]
+            z = t0 = t1 = t2 = tail[i] if back else 0.0
+            for j, soft in near[i]:
+                if soft and (asg[j] == q or soft == 2): x0, x1, x2 = e0[j], e1[j], e2[j]
+                else:
+                    if not back: z = tail[j]
+                    x0, x1, x2 = e0[j] + w0 + z, e1[j] + w1 + z, e2[j] + w2 + z
+                if x0 > t0: t0 = x0
+                if x1 > t1: t1 = x1
+                if x2 > t2: t2 = x2
+            j = bi[i]
+            if j >= 0:
+                x0, x1, x2 = e0[j] + w0, e1[j] + w1, e2[j] + w2
+                if x0 > t0: t0 = x0
+                if x1 > t1: t1 = x1
+                if x2 > t2: t2 = x2
+            log.append((i, e0[i], e1[i], e2[i], h0[i], h1[i], h2[i]))
+            h0[i], h1[i], h2[i] = t0, t1, t2
+            j = mi[i]
+            if e0[j] > t0: t0 = e0[j]
+            if e1[j] > t1: t1 = e1[j]
+            if e2[j] > t2: t2 = e2[j]
+            t0 += u0[i][q]; t1 += u1[i][q]; t2 += u2[i][q]
+            if e0[i] != t0 or e1[i] != t1 or e2[i] != t2:
+                e0[i], e1[i], e2[i] = t0, t1, t2
+                for j in far[i]:
+                    if not mark[j]: mark[j] = True; left += 1
+                j = mo[i]
+                if not mark[j]: mark[j] = True; left += 1
+                j = bo[i]
+                if not mark[j]: mark[j] = True; left += 1
+            left -= 1
+            if not left: break
+        return log
+
+    def undo(log):
+        for i, a, b, c, d, e, f in log: E_[0][i], E_[1][i], E_[2][i], H_[0][i], H_[1][i], H_[2][i] = a, b, c, d, e, f
+
+    def end():
+        if win[2] >= n: M = [max(e[i] for i in ends) + LAND for e in E_]
+        else:
+            zone = order[win[1]:win[2]]
+            M = [max([e[i] + t[i] - u[i][asg[i]] for i in zone]) for e, t, u in zip(E_, T_, us)]
+        return M, M[0] * wt[0] + M[1] * wt[1] + M[2] * wt[2]
+
+    def put(i, q, a):
+        s = seq[asg[i]]
+        s.remove(i)
+        mn[mp[i]], mp[mn[i]] = mn[i], mp[i]
+        s = seq[q]
+        mp[i], mn[i] = s[a - 1] if a else -1, s[a] if a < len(s) else -1
+        s.insert(a, i)
+        mn[mp[i]] = mp[mn[i]] = i
+        asg[i] = q
+
+    def deal(f):
+        held = [-1] * 8
+        bp[:], nb[:] = [-1] * n, [-1] * n
+        for p, i in enumerate(order):
+            if i in opens:
+                b = min((b for b in range(8) if held[b] < 0 or pos[held[b]] < p), key=lambda b: f[held[b]] if held[b] >= 0 else -1.0)
+                if held[b] >= 0: bp[i] = held[b]; nb[held[b]] = i
+                bk[opens[i]], held[b] = b, lastof[i]
+
+    def sort(lo, hi):
+        part = order[lo:hi + 1]
+        left = dict.fromkeys(part, 0)
+        for i in part:
+            for j in pj[i] + [bp[i], mp[i]]:
+                if j in left: left[i] += 1
+        out = [i for i in part if not left[i]]
+        for i in out:
+            for j in sj[i] + [mn[i], nb[i]]:
+                if j in left:
+                    left[j] -= 1
+                    if not left[j]: out.append(j)
+        if len(out) == len(part): order[lo:hi + 1] = out
+        return len(out) == len(part)
+
+    def holds(lo, hi, old, seeds, most):
+        for c in range(lo, hi + 1): pos[order[c]] = c
+        log = sweep(seeds, False)
+        r = end()
+        if r[1] <= most: return r
+        undo(log)
+        order[lo:hi + 1] = old
+        for c in range(lo, hi + 1): pos[order[c]] = c
+    seed = [seed]
 
     def rnd(m):
-        seed[0] = (seed[0] * 1103515245 + 12345) % 2 ** 31
+        seed[0] = (seed[0] * 1103515245 + 12345) % 2147483648
         return (seed[0] >> 8) % m
-    res = [run(k) for k in range(len(MODELS))]
-    now = sum(r[0] * w for r, w in zip(res, wt))
-    best = (now, list(order), list(asg))
-    for it in range(tries):
-        why, i = res[rnd(len(res))][1:3]
-        chain = []
-        while i >= 0: chain.append(i); i = why[i]
-        i = chain[rnd(len(chain))]
-        q, p = asg[i], order.index(i)
-        if q is None: continue
-        kind = rnd(5)
-        if kind == 0 and len(us[0][i]) < 2: kind = 1
-        if kind == 0: asg[i] = "vector" if q == "scalar" else "scalar"
-        step, hops, stop = (-1, 1 + rnd(3), set(j for j, _ in pre[i])) if kind < 3 else (1, 1 + rnd(3), set(succ[i]))
-        if kind == 0: hops -= 1
-        a = b = p
-        while hops and 0 <= a + step < n and order[a + step] not in stop:
-            a += step
-            if asg[order[a]] == asg[i]: hops -= 1; b = a
-        if b == p and kind: continue
-        order.insert(b, order.pop(p))
-        new = [run(k) for k in range(len(MODELS))]
-        v = sum(r[0] * w for r, w in zip(new, wt))
-        if v <= now + temp * (1 - it / tries) * rnd(1000) / 1000:
-            now, res = v, new
-            st = new[1][3]
-            order.sort(key=lambda j: st[j])
-            if v < best[0]: best = (v, list(order), list(asg))
-        else:
-            order.insert(p, order.pop(b)); asg[i] = q
-    return best[1], best[2], phys, prev
+    sweep(order, False); sweep(order, True)
+    M, now = end()
+    best = (now, list(order), list(asg), dict(bk))
+    until, crit = [0] * n, {}
+    X = (0, 1, 2)
+    e1, t1 = E_[1], T_[1]
+    for it in range(1, tries + 1):
+        if it % cfg["stay"] == 1 or it == tries:
+            for i, v in lag: tail[i] = v * max(0.0, 1 - it / (0.5 * tries))
+            win[:] = 0, n, n
+            marks[0][:] = marks[1][:] = [False] * (n + 1)
+            sweep(order, False)
+            order.sort(key=lambda j: e1[j] - u1[j][asg[j]])
+            for c, j in enumerate(order): pos[j] = c
+            M, now = end()
+            if now < best[0] - 1e-9 and (not lag or it > 0.5 * tries): best = (now, list(order), list(asg), dict(bk))
+            was = (list(bp), list(nb), dict(bk))
+            deal(e1)
+            log = sweep(order, False)
+            M2, v = end()
+            if v <= now + 0.02: M, now = M2, v
+            else:
+                undo(log)
+                bp[:], nb[:] = was[:2]
+                bk.update(was[2])
+            sweep(order, True)
+            a = max(0, rnd(n + cfg["wide"] // 2) - cfg["wide"] // 2)
+            win[:] = a, a + cfg["wide"], a + cfg["wide"] + cfg["zone"]
+            crit = {}
+        km = rnd(3)
+        if km not in crit:
+            lim, e, t, u = M[km] - 1e-6, E_[km], T_[km], us[km]
+            crit[km] = [i for i in order[win[0]:win[1]] if e[i] + t[i] - u[i][asg[i]] > lim and asg[i]]
+        cr, cand, T = crit[km], None, temp * (1 - it / tries)
+        if cr and rnd(100) < cfg["swap"]:
+            i = cr[rnd(len(cr))]
+            p = pos[i] + rnd(81) - 40
+            if not win[0] <= p < min(n, win[1]): continue
+            j = order[p]
+            q, q2 = asg[i], asg[j]
+            if i == j or q > 2 or q2 > 2 or not q2 or (q != q2 and not (both[i] and both[j])) or abs(u1[i][q] - u1[j][q2]) > 0.3: continue
+            if anc[i] >> j & 1 or anc[j] >> i & 1: continue
+            a, b = seq[q].index(i), seq[q2].index(j)
+            near = [mp[i], mn[i], mp[j], mn[j]]
+            there, back = ((i, q2, b), (j, q, a)), ((j, q2, b), (i, q, a))
+            if q == q2 and a > b: there, back = there[::-1], back[::-1]
+            for z in there: put(*z)
+            lo, hi = min(pos[i], p), max(pos[i], p)
+            for z in (i, j):
+                lo = min([lo] + [pos[y] for y in sj[z] + [nb[z], mn[z]] if y >= 0])
+                hi = max([hi] + [pos[y] for y in pj[z] + [bp[z], mp[z]] if y >= 0])
+            old = order[lo:hi + 1]
+            r = sort(lo, hi) and holds(lo, hi, old, [i, j] + near + sj[i] + sj[j], now + T * rnd(1000) / 1000)
+            if r:
+                (M, now), crit = r, {}
+                sweep([i, j] + near + pj[i] + pj[j], True)
+            else:
+                for z in back: put(*z)
+            continue
+        for _ in range(cfg["ns"] if cr else 0):
+            i = cr[rnd(len(cr))]
+            if until[i] > it: continue
+            q = asg[i]
+            low = [0.0 if E_[x][i] + T_[x][i] - us[x][i][q] > M[x] - 1e-6 else M[x] for x in X]
+            h1i, j1i = H_[1][i] + 1e-9, J_[1][i] + 1e-9
+            for step, on, off, A_, B_, C_, D_, lim in ((-1, mp, mn, E_, H_, T_, J_, h1i), (1, mn, mp, T_, J_, E_, H_, j1i)):
+                v = on[i]
+                if v < 0 or B_[km][i] >= A_[km][v] - 1e-9: continue
+                tt = [C_[x][off[i]] for x in X]
+                for a in range(1, 9):
+                    if v < 0 or A_[1][v] <= lim: break
+                    est, y_ = rnd(100) * 1e-4, on[v]
+                    for x in X:
+                        y = D_[x][v]
+                        if tt[x] > y: y = tt[x]
+                        y += us[x][v][q]; tt[x] = y
+                        r = B_[x][i]
+                        if A_[x][y_] > r: r = A_[x][y_]
+                        z = D_[x][i]
+                        L = r + us[x][i][q] + (y if y > z else z)
+                        est += wt[x] * (L if L > low[x] else low[x])
+                    if cand is None or est < cand[0]: cand = (est, i, q, a * step)
+                    v = y_
+            if both[i]:
+                q2 = 3 - q
+                s2 = seq[q2]
+                lo, hi = 0, len(s2)
+                while lo < hi:
+                    mid = (lo + hi) // 2
+                    if e1[s2[mid]] <= h1i: lo = mid + 1
+                    else: hi = mid
+                low = [max(low[x], E_[x][mp[i]] + T_[x][mn[i]]) for x in X]
+                for a in range(lo, min(len(s2), lo + 6) + 1):
+                    u, v = s2[a - 1] if a else -1, s2[a] if a < len(s2) else -1
+                    if a and t1[u] <= j1i: break
+                    est = rnd(100) * 1e-4
+                    for x in X:
+                        r = H_[x][i]
+                        if E_[x][u] > r: r = E_[x][u]
+                        z = J_[x][i]
+                        if T_[x][v] > z: z = T_[x][v]
+                        L = r + us[x][i][q2] + z
+                        est += wt[x] * (L if L > low[x] else low[x])
+                    if cand is None or est < cand[0]: cand = (est, i, q2, a)
+        if cand is None: continue
+        est, i, q2, a = cand
+        until[i] = it + 10 + rnd(30)
+        if est > now + T * rnd(1000) / 1000: continue
+        q, at, a0, b0 = asg[i], pos[i], mp[i], mn[i]
+        p = seq[q].index(i)
+        put(i, q2, a + p if q == q2 else a)
+        lo = max([pos[j] for j in pj[i] + [bp[i], mp[i]] if j >= 0] or [-1])
+        hi = min([pos[j] for j in sj[i] + [nb[i], mn[i]] if j >= 0] or [n])
+        lo, hi, plain = (min(at, hi), max(at, lo), 0) if lo > hi else (at, lo, 1) if lo > at else (hi, at, -1) if hi < at else (at, at, 1)
+        old = order[lo:hi + 1]
+        if plain: order[lo:hi + 1] = old[plain:] + old[:plain]
+        r = (plain or sort(lo, hi)) and holds(lo, hi, old, [i, b0, mn[i]] + sj[i], now + T)
+        if r:
+            (M, now), crit = r, {}
+            sweep([i, a0, mp[i]] + pj[i], True)
+        else: put(i, q, p)
+    prev, held = {}, {}
+    for i in best[1]:
+        if i in opens:
+            b = best[3][opens[i]]
+            if b in held: prev[i] = held[b]
+            held[b] = users[opens[i]]
+    return best[1], [QALL[q] for q in best[2]], best[3], prev
+
+
+def schedule(pinned, ops, cfg):
+    pl = plan(pinned, MODELS[1], cfg)
+    for k, (tries, temp) in enumerate(cfg["cycles"]): pl = search(ops, pl, cfg, tries, temp, cfg["seed"] + 100 * k, {} if k else cfg["lag"])
+    return pl
 
 
 def rank_program(g, core, T, topo):
@@ -769,8 +1011,8 @@ def rank_program(g, core, T, topo):
     if rank is None:
         return
     phys = {}
-    ops = build(T, rank, topo, core, phys, CFG)
-    if "p" not in PLAN: PLAN["p"] = polish(ops, plan(ops, MODELS[1], CFG), CFG["tries"], 0.02)
+    ops = build(T, rank, topo, core, phys, dict(CFG, pin={}))
+    if "p" not in PLAN: PLAN["p"] = schedule(build(T, rank, topo, core, {}, CFG), ops, CFG)
     order, asg, ph, prev = PLAN["p"][:4]
     phys.update(ph)
     pos = {j: k for k, j in enumerate(order)}

from concourse.mybir import AluOpType as A, ActivationFunctionType as AF

K = 512.0
KC = 4096
BIG = 2.0 ** 43
H = (256, 256)
CFG = {
    "dch": {(r, l): (512,) if r and not l else H for r in range(3) for l in range(5)},
    "m": {(r, l): (4, 4) if r and l < 3 else (1, 2) for r in range(3) for l in range(1, 5)},
    "uch": {(r, l): (H if (r, l) == (2, 0) else (512,)) for r in range(3) for l in range(4)},
    "cu": ("vddv", "vddv", "dddd"),
    "pf": ("pp", "qp", "qp", "qp"),
    "zd": (2, 3), "ka": (1, 2, 3),
    "gp": 1024, "fp": (1024, 2048, 2048),
    "pin": {}, "look": 0.3, "vb": 10.0, "it": 2, "gap": 3.0, "keep": 4, "far": 3.0,
    "wt": (1.5, 1, 0.8), "ns": 3, "stay": 50, "wide": 100, "zone": 100, "swap": 10, "seed": 1,
    "lag": {"S4l": 5, "S3l": 2, "S2l": 2}, "cycles": ((50000, .6), (45000, .5), (45000, .45), (45000, .4), (60000, .45), (40000, .35)),
}
for _r in range(3):
    for _p in ("D0", "D1", "D2", "D3", "G", "U0", "U1", "U2", "U3", "S2", "S3", "S4"):
        for _k in "gaveulkzcyi": CFG["pin"]["%d%s%s" % (_r, _p, _k)] = "s"
    CFG["pin"]["%dS2g" % _r] = "svsvsvs"
    CFG["pin"]["0D%dg" % (_r + 1)] = "vs"
NT = 4
SCRATCH = {
    "raw": ("sbuf", [128, 2056], "int32"), "rpm": ("sbuf", [128, 256], "int32"), "po": ("sbuf", [128, 256], "uint16"),
    "off": ("sbuf", [128, 3072], "uint16"), "Lh": ("sbuf", [128, 2048], "float16"), "Lw": ("sbuf", [128, 1544], "float32"),
    "F": ("sbuf", [128, 4112], "bfloat16"), "Z": ("sbuf", [128, 4112], "bfloat16"),
    "x": ("sbuf", [128, 2048], "bfloat16"), "o": ("sbuf", [128, 2560], "bfloat16"), "kx": ("sbuf", [128, 2048], "bfloat16"),
    "as1": ("sbuf", [128, 512], "bfloat16"), "as2": ("sbuf", [128, 512], "bfloat16"),
    "ob": ("sbuf", [128, 128], "bfloat16"), "kb": ("sbuf", [128, 512], "bfloat16"), "zb": ("sbuf", [128, 512], "bfloat16"),
    "mb": ("sbuf", [128, 128 * 9], "bfloat16"), "iw": ("sbuf", [128, 152 * 7], "bfloat16"), "W": ("sbuf", [128, 720], "bfloat16"),
    "tri": ("sbuf", [128, 2048], "bfloat16"), "ez": ("sbuf", [128, 272], "bfloat16"), "rp2": ("sbuf", [128, 512], "int32"),
    "mo": ("sbuf", [128, 128 * 13], "bfloat16"), "tl": ("sbuf", [128, 128 * 36], "bfloat16"), "g0": ("sbuf", [128, 512], "bfloat16"),
    "b4": ("sbuf", [128, 512], "bfloat16"), "nw": ("sbuf", [128, 2048], "bfloat16"), "ip": ("sbuf", [128, 8], "int32"),
    "col": ("sbuf", [128, 16], "float32"),
}
SPREAD = {"SA": (0, 2048, -1024, 0), "SB": (2048, 0, -1024, 0), "TA": (BIG, -BIG, 0, 256), "TB": (-BIG, BIG, 0, 256),
          "UK": (K, K, -K, -K), "UN": (-K, -K, 0, 0)}
for _k in SPREAD: SCRATCH[_k] = ("sbuf", [128, 512], "bfloat16")
for _k in (4, 8, 16): SCRATCH["mk%d" % _k] = ("sbuf", [128, 1024], "bfloat16")
for _k in range(3): SCRATCH["cw%d" % _k] = ("sbuf", [128, 3072], "bfloat16")
for _n, _k in (("gr", 10240), ("fg", 16384), ("so", 10240)): SCRATCH[_n] = ("sbuf", [128, _k], "bfloat16")
for _k in range(NT):
    for _n in ("ta", "tb"): SCRATCH["%s%d" % (_n, _k)] = ("sbuf", [128, 512], "bfloat16")
for _k in range(3):
    for _n in ("ga", "gb"): SCRATCH["%s%d" % (_n, _k)] = ("sbuf", [128, 512], "bfloat16")
    SCRATCH["zf%d" % _k] = ("sbuf", [128, 64], "bfloat16")
for _k in range(2):
    for _n in ("qq", "yo"): SCRATCH["%s%d" % (_n, _k)] = ("sbuf", [128, 512], "bfloat16")
    SCRATCH["ot%d" % _k] = ("sbuf", [128, 128], "bfloat16")
    for _n in ("X", "Tg", "hm", "Lk"): SCRATCH["%s%d" % (_n, _k)] = ("sbuf", [128, 512], "float16")
    SCRATCH["xu%d" % _k] = ("sbuf", [128, 32], "uint16")
for _k in range(8): SCRATCH["ps%d" % _k] = ("psum", [128, 512], "float32")
NDMA = 60
QS = ("vector", "scalar", "tensor", "pool")
SEMAPHORES = ["q_" + q for q in QS] + ["d%d" % k for k in range(NDMA)] + ["ra%d" % k for k in range(6)] + ["la%d" % k for k in range(6)]

SZ = {"float32": 4, "int32": 4, "bfloat16": 2, "uint16": 2, "float16": 2}
PLAN = {}
BS = 128


def conflict(a, b):
    if a[1] >= b[2] or b[1] >= a[2]: return False
    return not (a[3] == 2 and b[3] == 2 and (a[1] - b[1]) % 2)


def build(T, rank, topo, core, phys, cfg):
    ops = []
    last = {}
    ndma = [0]
    ph = ["init"]
    rot = {}

    def isps(r): return r[0][0] == "#"

    def ap(r):
        t = T["ps%d" % phys[r[0]]] if isps(r) else T[r[0]]
        return t[:, r[1]:r[2]] if r[3] == 1 else t[:, r[1]:r[2]:r[3]]

    def R(name, lo=0, hi=None, st=1):
        return (name, lo, SCRATCH[name][1][1] if hi is None else hi, st)

    def sub(r, a, b, st=1):
        return (r[0], r[1] + a * r[3], r[1] + (b - 1) * r[3] + 1, r[3] * st)

    def n_of(r): return (r[2] - r[1] + r[3] - 1) // r[3]

    def sz(r): return 4 if isps(r) else SZ[SCRATCH[r[0]][2]]

    def op(opts, rd, wr, sem=None, kind="v", after=()):
        i = len(ops)
        deps = {}
        pin = cfg["pin"].get(ph[0] + kind)
        if pin and len(opts) > 1:
            c = rot[ph[0] + kind] = rot.get(ph[0] + kind, -1) + 1
            opts = [o for o in opts if o[0][0] == pin[min(c, len(pin) - 1)]]
        qs = set(o[0] for o in opts)
        banks = set()
        for w, lst in ((0, rd), (1, wr)):
            for r in lst:
                if isps(r): banks.add(r[0])
                for (j, rr, ww) in last.setdefault(r[0], []):
                    if j == i: continue
                    if isps(r):
                        if qs == {"tensor"} and ops[j]["qs"] == {"tensor"}: k = "acc"
                        else: k = "w" if (w or ww) and conflict(r, rr) else "ord"
                    else:
                        if not (w or ww) or not conflict(r, rr): continue
                        k = "w"
                    if deps.get(j) != "w": deps[j] = k
        ops.append(dict(opts=opts, deps=deps, sem=sem, qs=qs, name=ph[0] + kind, after=[a for a in after if a is not None], banks=banks))
        for w, lst in ((1, wr), (0, rd)):
            for r in lst:
                h = last[r[0]]
                if w and not isps(r) and r[3] == 1: h[:] = [e for e in h if not (r[1] <= e[1][1] and e[1][2] <= r[2])]
                h.append((i, r, w))
        return i

    def bank(w):
        rot["#"] = rot.get("#", 0) + 1
        return ("#%d" % rot["#"], 0, w, 1)

    def pick(name, n, w=None):
        k = rot.get(name, 0); rot[name] = k + 1
        return R("%s%d" % (name, k % n), 0, w)

    def ring(name, w):
        a = rot.get(name, 0)
        if a + w > SCRATCH[name][1][1]: a = 0
        rot[name] = a + w
        return R(name, a, a + w)

    def half(*rs): return 0.5 if all(sz(r) == 2 for r in rs) else 1

    def tt(out, a, b, f, **k):
        per = 1 if (isps(a) or isps(b)) else 2
        return op([("vector", (n_of(out) * per, 0, 1, 0), lambda e: e.tensor_tensor(ap(out), ap(a), ap(b), f))], [a, b], [out], **k)

    def sc(s): return ap(s) if isinstance(s, tuple) else s

    def vts(out, a, s1, s2, f, f2=None):
        kw = {} if f2 is None else {"op1": f2}
        return ("vector", (n_of(out) * half(out, a), 0, 1, 0), lambda e: e.tensor_scalar(ap(out), ap(a), sc(s1), sc(s2), op0=f, **kw))

    def act(out, a, f, bias=0.0, scale=1.0):
        return ("scalar", (n_of(out), 0, 1, 0), lambda e: e.activation(ap(out), ap(a), f, bias=bias, scale=sc(scale)))

    def ts(out, a, s1, s2, f, f2=None, **k):
        return op([vts(out, a, s1, s2, f, f2)], [a] + [s for s in (s1, s2) if isinstance(s, tuple)], [out], **k)

    def flex(out, a, o1, o2, **k): return op([o1, o2], [a], [out], **k)

    def fcopy(out, a, **k):
        return flex(out, a, act(out, a, AF.Copy), ("vector", (n_of(out) * half(out, a), 0, 1, 0), lambda e: e.tensor_copy(ap(out), ap(a))), **k)

    def relu(out, a, **k): return flex(out, a, act(out, a, AF.Relu), vts(out, a, 0.0, None, A.max), **k)

    def lin(out, a, m, c, **k): return flex(out, a, act(out, a, AF.Copy, bias=float(c), scale=float(m)), vts(out, a, float(m), float(c), A.mult, A.add), **k)

    def mset(out, c): return op([("vector", (n_of(out) * 0.5, 0, 1, 0), lambda e: e.memset(ap(out), c))], [], [out])

    def mm(lst, start=True, stop=True, each=False, kind="t", after=()):
        def fn(e):
            for j, (o_, l_, r_) in enumerate(lst): ins = e.matmul(ap(o_), ap(l_), ap(r_), each or (start and j == 0), each or (stop and j == len(lst) - 1))
            return ins
        rd, wr = [], []
        for (o_, l_, r_) in lst:
            for z, y in ((l_, rd), (r_, rd), (o_, wr)):
                if z not in y: y.append(z)
        return op([("tensor", (sum(max(64, n_of(z[0])) for z in lst), 0, len(lst), 0), fn)], rd, wr, kind=kind, after=after)

    def gather(out, win, offs_, add=None, clip=False, kind="g"):
        c = (0, n_of(out), 1, 0)
        if add is None and not clip: v = lambda e: e.tensor_copy(ap(out), ap(win).indirect(ap(offs_)))
        else: v = lambda e: e.tensor_scalar(ap(out), ap(win).indirect(ap(offs_)), add or 0.0, None, op0=A.max if clip else A.add)
        return op([("scalar", c, lambda e: e.activation(ap(out), ap(win).indirect(ap(offs_)), AF.Relu if clip else AF.Copy, bias=add or 0.0)),
                   ("vector", c, v)], [win, offs_], [out], kind=kind)

    def gmin(out, win, offs_):
        return op([("vector", (0, n_of(out), 1, 0), lambda e: e.tensor_tensor(ap(out), ap(win).indirect(ap(offs_)), ap(out), A.min))], [win, offs_, out], [out], kind="f")

    def scan(out, m_, g_):
        return op([("vector", (n_of(out) * 0.5, 0, 1, 0), lambda e: e.tensor_tensor_scan(ap(out), ap(m_), ap(g_), 0.0, A.max, A.min))], [g_, m_], [out], kind="s")

    def dma(q, out, in_, rd, wr):
        s = "d%d" % ndma[0]; ndma[0] += 1
        return op([(q, (0, 0, 0, 0.1), lambda e: e.dma_start(out(), in_()))], rd, wr, sem=(s, 16), kind="d")

    def add(out, r, wr):
        s = "d%d" % ndma[0]; ndma[0] += 1
        return op([("pool", (0, 0, 0, 1.0), lambda e: e.dma_start(out(), ap(r), accum_op=A.add))], [r] + wr, wr, sem=(s, 16), kind="d")

    def load(q, r, src, lo, hi): return dma(q, lambda: ap(r), lambda: T[src][:, lo:hi], [], [r])

    def store(dst, lo, hi, r): return dma("sync", lambda: T[dst][:, lo:hi], lambda: ap(r), [r], [])

    def gsel(out, src, pattern, cmp, base, cm, fill=0.0):
        return op([("pool", (2 * n_of(out), 0, 0, 0.22), lambda e: e.affine_select(ap(out), ap(src), pattern, cmp, fill, base, cm))], [src], [out], kind="p")

    def iota(out, pattern, base, cm):
        kw = {} if SCRATCH[out[0]][2] == "int32" else {"allow_small_or_imprecise_dtypes": True}
        return op([("pool", (2 * n_of(out), 0, 0, 0.18), lambda e: e.iota(ap(out), pattern, base, cm, **kw))], [], [out], kind="p")

    def pcopy(out, a): return gsel(out, a, [[0, n_of(out)]], A.is_ge, 0, 0)

    def fill(out, c): return iota(out, [[0, n_of(out)]], int(c), 0)

    def zero(out):
        for a in range(0, n_of(out), 512):
            r, z = sub(out, a, min(a + 512, n_of(out))), R("zb", 0, min(512, n_of(out) - a))
            dma("sync", lambda r=r: ap(r), lambda z=z: ap(z), [z], [r])

    I = R("iw", 12, 140)
    P, In, In4, I256, P256 = (R("mb", 128 * k, 128 * k + 128) for k in range(5))
    GS = [R("mb", 128 * k, 128 * k + 128) for k in range(5, 9)]
    MO = (R("mo", 0, 128), R("mo", 128, 256))

    WT = ((1, 0), (-1, 1), (-KC, 0), (1, -KC))

    def row(j, v=0): return R("W", 144 * v + 15 - j, 144 * v + 143 - j)

    def blk(nm, k): return R(nm, 128 * k, 128 * k + 128)

    def move(m, t, s):
        a = 152 * (1 + t + (2 if m == 4 else 0)) + 12 - (s - t) * (16 // m)
        return R("iw", a, a + 128)

    def chunks(rnd, l, which="dch"):
        a, out = 0, []
        for k, w in enumerate(cfg[which][rnd, l]):
            out.append((k, a, w)); a += w
        return out

    made = set()

    def weights(nm, a=0, b=4, zs=range(4)):
        s_ = R(nm, 128 * a, 128 * b)
        for z in zs:
            w = SPREAD[nm][z]
            if not w or (nm, a, z) in made: continue
            src = s_ if (nm, a) in made else R("zb", 0, 128 * (b - a))
            made.add((nm, a)); made.add((nm, a, z))
            gsel(s_, src, [[-4, b - a], [-16, 8], [0, 16]], A.not_equal, -4 * a - z, 1, fill=float(w))

    cur = {}

    def tile(l, k, kind, c, w):
        a = BS * (3 * (3 * l + kind + (kind and ph[0][0] == "1")) + k)
        if k == 0: cur[l, kind] = []
        cur[l, kind].append((R("tl", a, a + BS), c, w))
        return cur[l, kind][-1][0]

    def spread(b, nm, tiles, c=0):
        return [(sub(b, j - c, j - c + BS), blk(nm, j // BS), [t for t, a, w in tiles if a <= j < a + w][0]) for j in range(c, c + n_of(b), BS)]

    masked = {}

    def olds(b, tiles, c, w, kind):
        cover = [z for z in tiles if z[1] < c + w and c < z[1] + z[2]]
        if len(cover) == 1: return [(b, MO[kind], cover[0][0])]
        out = []
        for t, a, v in cover:
            lo, hi = max(a, c), min(a + v, c + w)
            if (kind, lo, hi) not in masked:
                z = masked[kind, lo, hi] = R("mo", 256 + 128 * len(masked), 384 + 128 * len(masked))
                if lo: gsel(z, MO[kind], [[0, 8], [1, 16]], A.is_ge, -4 * (lo // BS), 0)
                if hi < 512: gsel(z, z if lo else MO[kind], [[0, 8], [-1, 16]], A.is_ge, 4 * (hi // BS) - 1, 0)
            out.append((b, masked[kind, lo, hi], t))
        return out

    forms1 = []

    def ocol(rnd, l):
        if l > 1: return 512 * (l - 1)
        f = (cfg["dch"][rnd, 1], cfg["m"][rnd, 1])
        if f not in forms1: forms1.append(f)
        k = forms1.index(f)
        return 1536 + 512 * k if k else 0

    load("sync", R("o", 0, 512), "safe", 0, 512)
    load("scalar", R("x", 0, 512), "piv", 0, 512)
    load("sync", R("raw", 0, 512), "uses", 0, 512)
    load("scalar", R("x", 512, 2048), "piv", 512, 2048)
    def raw(a, w): return R("raw", a + 8 * (a >= 1536), a + 8 * (a >= 1536) + w)
    for l in range(1, 4): load("sync", raw(512 * l, 512), "uses", 512 * l, 512 * l + 512)
    load("sync", R("rpm"), "prem", 0, 256)
    load("sync", R("cw0", 2048, 2560), "lem", 0, 512)
    for k in range(3): load("sync", R("cw%d" % k, 2560, 3072), "leaf", 0, 512)
    mset(R("ob"), 1.0); mset(R("iw", 0, 152), 0.0); mset(R("zb"), 0.0); mset(R("W"), 0.0)
    mset(R("iw", 152, 456), 0.0); mset(R("iw", 456, 1064), 0.0)
    gsel(I, R("ob"), [[-1, 128]], A.is_equal, 0, 1)
    gsel(P, R("ob"), [[-16, 8], [8, 2], [-1, 8]], A.is_equal, -8, 1)
    w8 = R("W", 15, 143, 16)
    gsel(w8, R("ob", 0, 8), [[-16, 8]], A.is_ge, 0, 1)
    gsel(w8, w8, [[16, 8]], A.is_ge, 15, -1)
    for v in (1, 2, 3):
        for z in range(2):
            if WT[v][z]: lin(R("W", 144 * v + 15 + z, 144 * v + 143, 16), w8, WT[v][z], 0)
    lin(In, I, -1, 0)
    iota(R("ip", 0, 1), [[0, 1]], 0, 1)
    r4 = R("ip", 4, 5)
    ts(r4, R("ip", 0, 1), 3, None, A.bitwise_and)
    cD, cU, cH, c3 = (R("col", k, k + 1) for k in range(4))
    ts(c3, r4, -1.0, 3.0, A.mult, A.add)
    ts(cD, r4, c3, None, A.min)

    def parts(m):
        if m > 1 and m not in made:
            made.add(m)
            for t in range(m): gsel(move(m, t, t), I, [[0, 8], [1, m], [0, 16 // m]], A.is_equal, -t, 0)
    for a in (0, 2):
        weights("SA", a, a + 2, (1,)); weights("SB", a, a + 2, (0,))
    mset(R("F", 1024, 4112), 255.0)

    def late_consts():
        for a in (0, 2): weights("SA", a, a + 2); weights("SB", a, a + 2)
        b4, p4 = R("b4"), [[-4, 4], [-16, 8], [0, 16]]
        gsel(b4, R("zb"), p4, A.is_gt, -3, 1, fill=1.0)
        gsel(b4, b4, p4, A.is_ge, 0, 1)
        cn, ck, ca, cb, c1, c2 = (R("col", k, k + 1) for k in range(6, 12))
        ts(cn, r4, 2.0, -K, A.is_lt, A.mult); ts(ck, cn, -2.0, -K, A.mult, A.add)
        ts(c1, r4, 2 * BIG / K, -BIG / K, A.mult, A.add); ts(c2, r4, 3.0, 256.0, A.is_equal, A.mult)
        ts(ca, c1, cn, c2, A.mult, A.add); ts(c1, c1, -1.0, None, A.mult); ts(cb, c1, cn, c2, A.mult, A.add)
        weights("UN")
        for nm, c in (("TA", ca), ("TB", cb), ("UK", ck)): op([act(R(nm), b4, AF.Copy, scale=c), vts(R(nm), b4, c, None, A.mult)], [b4, c], [R(nm)])
        z1 = R("zb", 0, 128)
        for z, v in ((I256, -256.0), (In4, -4.0)): gsel(z, z1, [[-1, 128]], A.not_equal, 0, 1, fill=v)
        gsel(P256, z1, [[-16, 8], [8, 2], [-1, 8]], A.not_equal, -8, 1, fill=-256.0)
        for z, v in zip(GS, (2 ** 30, -2 ** 17, -2 ** 30, 2 ** 17)):
            gsel(z, z1, [[-16, 8], [0, 16]], A.is_gt, -15, 1, fill=float(v)); gsel(z, z, [[-16, 8], [0, 16]], A.is_ge, 0, 1)
        for kind in (1, 0):
            zero(MO[kind])
            for a, b, v in ((0, 0, 1), (1, 0, -1), (0, 1, -1), (1, 1, 1)) + (((2, 2, 1),) if kind else ((0, 2, 1), (1, 2, 1))):
                gsel(sub(MO[kind], b, 128, 4), sub(MO[kind], b, 128, 4), [[-4, 32]], A.not_equal, -a, 1, fill=v * 2.0 ** 25)
        gsel(R("g0"), R("zb"), [[0, 4], [-16, 8], [0, 16]], A.not_equal, 0, 1, fill=-2.0 * KC)
        for a in range(0, 16, 4):
            t_ = R("tri", 128 * a, 128 * a + 512)
            gsel(t_, R("g0"), [[-1, 4], [0, 8], [1, 16]], A.is_gt, -a, 0)
            gsel(t_, t_, [[-1, 4], [-256, 8], [1, 16]], A.not_equal, -a, 16, fill=float(KC))
        ts(cU, r4, 3.0, None, A.is_lt)
        ts(cH, r4, 65535.0, -32767.5, A.mult, A.add)
        w4 = R("W", 144 * 4 + 15, 144 * 4 + 143, 16)
        gsel(w4, R("zb", 0, 8), [[-16, 8]], A.is_gt, -15, 1, fill=-1.0); gsel(w4, w4, [[-16, 8]], A.is_ge, 0, 1)
        fill(R("kb"), K); fill(R("raw", 1536, 1544), 4096); fill(R("Lw", 1536, 1544), 2048)
        fill(R("Z", 4096, 4112), 0)
        for l in range(4):
            if l == 0 or l in cfg["zd"]: zero(R("Z", 1024 * l, 1024 * l + 1024))
        fill(R("ez"), 0)
        for z in range(2): gsel(R("ez", 136 * z + 4, 136 * z + 132), I, [[0, 32], [1, 4]], A.is_equal, -z, 0)
        pcopy(R("Lw", 0, 512), R("Lh", 0, 512))
        iota(R("rp2", 0, 256), [[0, 2], [512, 4], [0, 32]], 512, 0)
        tt(R("rp2", 256, 512), R("rpm"), R("rp2", 0, 256), A.subtract)
        fcopy(R("po"), R("rp2", 256, 512))

    def lay(grp, col, L):
        for m, a, w in grp:
            if m == 1: lin(R("off", col + a, col + a + w), sub(L, a, a + w), 1, 2048, kind="l")
        grp = [z for z in grp if z[0] > 1]
        if not grp: return
        b = bank(n_of(L))
        for m, a, w in grp:
            parts(m)
            n = w // m
            for t in range(m): mm([(sub(b, a + t * n, a + t * n + n), move(m, t, s), sub(L, a + s, a + w, m)) for s in range(m)])
        a, e_ = grp[0][1], grp[-1][1] + grp[-1][2]
        lin(R("off", col + a, col + e_), sub(b, a, e_), 1, 2048, kind="l")

    def first_lists(l, rnd):
        a = 512 * (l - 1)
        if rnd == 0: lin(R("Lh", a, a + 512), raw(a, 512), 1, -2048, kind="l")
        lay([(cfg["m"][rnd, l][k], c, w) for k, c, w in chunks(rnd, l)], ocol(rnd, l), R("Lh", a, a + 512))

    def state(n0, w, srcs, kind, old, new, after):
        cb = new and bank(BS)
        x_ = R("x", n0, n0 + w)
        if old and new: mm(olds(cb, old, n0 % 512, w, kind), stop=False, after=[after])
        out = []
        for z in range(2):
            b, t = bank(w), pick("ta" if z == 0 else "tb", NT, w)
            mm([(b, (I, P)[z], x_)], stop=False, after=[after])
            mm([(b, In, srcs[z])], start=False)
            relu(t, b, kind="a")
            if new: mm([(cb, row(4 * (j + n0 % 512 // BS) + z, ((1, 2), (3, 0))[kind][z]), sub(t, j * BS, j * BS + BS)) for j in range(w // BS)], start=not old and not z, stop=z == 1)
            out.append(t)
        return new and ts(new, cb, (cD, cU)[kind], None, A.is_ge, kind="i"), out

    def least(rnd, l, k, c, w):
        m = cfg["m"][rnd, l][k]
        h = 16 // m
        so, v = ring("so", w * h), cfg["gp"] // h
        for j in range(0, w, v):
            gb = ring("gr", v * h)
            for t in range(m):
                a = ocol(rnd, l) + c + (t * w + j) // m
                (gmin if t else gather)(gb, R("F", 0, 4097), R("off", a, a + v // m))
            if ("mk", h) not in made:
                made.add(("mk", h))
                zero(R("mk%d" % h)); fill(R("mk%d" % h, 0, 1024, h), 255)
            g0 = scan(sub(so, j * h, (j + v) * h), R("mk%d" % h), gb)
        return sub(so, h - 1, w * h, h), g0

    lastup = {}

    def fresh(rnd, n0, w): return R("as%d" % rnd, n0, n0 + w) if rnd and n0 < 512 else R("o", n0, n0 + w)

    def down(rnd, l):
        ph[0] = "%dD%d" % (rnd, l)
        todo = []
        for k, c, w in chunks(rnd, l):
            n0 = 512 * l + c
            g0 = None
            if l: src, g0 = least(rnd, l, k, c, w)
            else: src = fresh(rnd, n0, w)
            if l == 0 and rnd: g0 = lastup[0]
            old = cur[l, 1] if rnd else None
            todo.append((c, n0, w, src, state(n0, w, (src, src), 0, old, tile(l, k, 0, c, w), g0)[1]))
            if rnd == 2:
                b = bank(w)
                mm([(b, I, src)] + spread(b, "UN", old, c))
                relu(R("o", n0, n0 + w), b, kind="o")
            elif l: pcopy(R("o", n0, n0 + w), src)
        for c, n0, w, src, rs in todo:
            for z in range(2):
                b, f_ = bank(w), R("F", 2 * n0 + z, 2 * n0 + 2 * w, 2)
                two = spread(b, ("SA", "SB")[z], cur[l, 0], c)
                if rnd == 0 and cfg["pf"][l][c > 0] == "p":
                    mm([(b, (I, P)[z], R("x", n0, n0 + w))], stop=False, after=[g0]); mm(two, start=False)
                    tt(f_, b, src, A.max, kind="e")
                    continue
                mm([(b, I, src)], stop=False); mm([(b, I, rs[z])], start=False, stop=False); mm(two, start=False)
                if rnd: tt(f_, b, R("kx", n0, n0 + w), A.max, kind="e")
                else: fcopy(f_, b, kind="e")
        if rnd == 2:
            a, k_, y_ = 512 * l, R("kx", 512 * l, 512 * l + 512), ("ys", 512 * l, 512 * l + 512, 1)
            dma("sync", lambda: T["ys"][:, a:a + 512], lambda: ap(k_), [k_], [y_])
            add(lambda: T["ys"][:, a:a + 512], R("o", a, a + 512), [y_])

    nremote = [0]

    def send(src, dst, to):
        k = nremote[0]; nremote[0] += 1
        d = T.cores[to % 4]
        rid, pid = topo.addr(d)[:2]
        mask = sum(1 << e for e in topo.engines(core, d)[:8])
        i = op([("pool", (0, 0, 0, 1.0), lambda e: e.remote_dma(ap(dst), ap(src), T.sem["ra%d" % k], T.sem["la%d" % k], pid, rid, mask))], [src], [], sem=("la%d" % k, 8), kind="r")
        op([(None, (0, 0, 0, 4.0 if k else 7.0), None)], [], [dst], sem=("ra%d" % k, 8), after=[i], kind="w")

    def ghosts(rnd):
        ph[0] = "%dG" % rnd
        for k, c, w in chunks(rnd, 4):
            o_ = R("o", 2048 + c, 2048 + c + w)
            fcopy(o_, least(rnd, 4, k, c, w)[0], kind="c")
            if rnd < 2: send(o_, R("as%d" % (rnd + 1), c, c + w), rank + 1)
            else: store("ys", 2048 + c, 2048 + c + w, o_)

    def up(rnd, l):
        ph[0] = "%dU%d" % (rnd, l)
        cw = "cw%d" % rnd
        zd = rnd < 2 and l in cfg["zd"]
        for k, c, w in chunks(rnd, l, "uch"):
            n0 = 512 * l + c
            x_, c_ = R("x", n0, n0 + w), R(cw, n0, n0 + w)
            ab = (pick("ga", 3, w), pick("gb", 3, w))
            gs = [gather(ab[z], R(cw, 512 * l + 512, 3072), R("po", 128 * z + n0 // 16, 128 * z + (n0 + w) // 16), clip=True) for z in range(2)]
            direct = cfg["cu"][rnd][l] == "d"
            new = tile(l, k, 1, c, w)
            lastup[0], rs = state(n0, w, ab, 1, cur[l, 0], None if rnd == 2 and direct else new, gs[0])
            q, now = pick("qq", 2, w), cur[l, 1]
            ba, bb = bank(w), bank(w)
            for z, (b, m_, nm) in enumerate(((ba, I256, "TA"), (bb, P256, "TB"))):
                if direct:
                    mm([(b, m_, x_)] + spread(b, nm, cur[l, 0], c), stop=False, after=[gs[1]])
                    mm([(b, GS[2 * z], rs[0])], start=False, stop=False); mm([(b, GS[2 * z + 1], rs[1])], start=False)
                else:
                    mm([(b, m_, x_)], stop=False, after=[gs[1]]); mm(spread(b, nm, now, c), start=False)
            tt(ba, ab[0], ba, A.min)
            tt(q, ab[1], bb, A.min)
            tt(c_, q, ba, A.max)
            if rnd == 2:
                y = pick("yo", 2, w)
                relu(y, c_, kind="c")
                store("yc", n0, n0 + w, y)
                continue
            if l and not zd:
                b = bank(w)
                mm(spread(b, "TA", now, c), each=True)
                za, zb = R("Z", 2 * n0, 2 * n0 + 2 * w, 2), R("Z", 2 * n0 + 1, 2 * n0 + 2 * w, 2)
                flex(za, b, act(za, b, AF.Relu, scale=1 / BIG, bias=-256 / BIG), vts(za, b, 1024.0, None, A.is_gt), kind="z")
                flex(zb, b, act(zb, b, AF.Relu, scale=-1 / BIG, bias=256 / BIG), vts(zb, b, 0.0, None, A.is_lt), kind="z")
            b, k_ = bank(w), R("kx", n0, n0 + w)
            mm([(b, I, fresh(rnd, n0, w))] + spread(b, "UK", now, c))
            if rnd and l in cfg["ka"]:
                y = ring("nw", w)
                relu(y, b, kind="k")
                add(lambda k_=k_: ap(k_), y, [k_])
            elif rnd: tt(k_, b, k_, A.max, kind="k")
            else: relu(k_, b, kind="k")
        if zd:
            b, zf = bank(64), pick("zf", 3)
            for z in range(2):
                mm([(sub(b, 32 * z, 32 * z + 32), R("ez", 136 * z + 4 - j + z, 136 * z + 132 - j + z), sub(new, 32 * j, 32 * j + 32)) for j in range(4)])
            for z in range(2): fcopy(sub(zf, z, 64, 2), sub(b, 32 * z, 32 * z + 32), kind="z")
            dma("sync", lambda: T["Z"][0:128:16, 1024 * l:1024 * l + 1024], lambda: ap(zf), [zf], [R("Z", 1024 * l, 1024 * l + 1024)])
        if rnd < 2 and l == 0: send(R(cw, 0, 512), R("cw%d" % (rnd + 1), 2048, 2560), rank - 1)

    def splice(rnd, l):
        ph[0] = "%dS%d" % (rnd, l)
        col, w = 512 * (l - 1), 512
        L, fl = R("Lh", col, col + w), bank(w)
        for k, c1, w1 in chunks(rnd - 1, l):
            m = cfg["m"][rnd - 1, l][k]
            h, n = 16 // m, w1 // m
            for t in range(m):
                fg, a = ring("fg", w1 * h), col + c1 + t * n
                for j in range(0, n, cfg["fp"][l - 2] // 16):
                    v = min(cfg["fp"][l - 2] // 16, n - j)
                    gather(sub(fg, 16 * j, 16 * (j + v)), R("Z", 0, 4097), R("off", a + j, a + j + v))
                for r0 in range(0, h, 4):
                    o_ = sub(fl, c1, c1 + w1)
                    last_mm = mm([(o_, blk("tri", t * h + r), sub(fg, r, w1 * h, h)) for r in range(r0, r0 + 4)] + ([] if t + r0 else [(o_, In4, R("kb", 0, w1))]),
                                 start=t + r0 == 0, stop=t * h + r0 == 12, kind="r")
        L1 = pick("X", 2, w)
        tt(L1, L, fl, A.max)
        b = bank(w // 16)
        mm([(b, row(q, 4), sub(L, q, w, 16)) for q in range(16)], stop=False, after=[last_mm])
        mm([(b, row(q), sub(L1, q, w, 16)) for q in range(16)], start=False)
        xu = pick("xu", 2, w // 16)
        i = ts(xu, b, -0.5, 1535.75, A.mult, A.add, kind="i")
        tg = pick("Tg", 2, w)
        gather(tg, R("raw" if rnd == 1 else "Lw", 0, 1537), xu, add=-2048.0 if rnd == 1 else 0.0, kind="u")
        b, hm = bank(w), pick("hm", 2, w)
        mm([(b, P, L1)], after=[i])
        tt(hm, tg, b, A.max)
        b = bank(BS)
        mm([(b, row(4 * j, 1), sub(hm, j * BS, j * BS + BS)) for j in range(w // BS)])
        ot = pick("ot", 2, BS)
        ts(ot, b, cH, 2.0, A.is_ge, A.mult, kind="i")
        lk, b = pick("Lk", 2, w), bank(w)
        mm([(b, I, L)] + spread(b, "SA", [(ot, 0, w)]))
        tt(lk, L1, b, A.min)
        b = bank(w)
        mm([(b, P, tg)] + spread(b, "SB", [(ot, 0, w)]))
        tt(L, lk, b, A.min)
        lay([(cfg["m"][rnd, l][k], c1, w1) for k, c1, w1 in chunks(rnd, l)], col, L)
        if rnd == 1 and l < 4: pcopy(R("Lw", col, col + w), L)

    down(0, 0)
    for l in (1, 2, 3):
        ph[0] = "init"
        first_lists(l, 0)
        down(0, l)
    ph[0] = "late"
    first_lists(4, 0)
    late_consts()
    for rnd in (1, 2):
        if ocol(rnd, 1) not in [ocol(r, 1) for r in range(rnd)]: first_lists(1, rnd)
    for rnd in range(3):
        if rnd:
            for l in (2, 3, 4): splice(rnd, l)
            for l in range(4): down(rnd, l)
        ghosts(rnd)
        for l in (3, 2, 1, 0): up(rnd, l)
    return ops


MODELS = ((1.0, 1.04, 0.03, 0.2, 0.00045, 1.2, 2.0), (1.0, 1.55, 0.04, 0.1, 0.00045, 1.1, 0.5), (1.3, 1.9, 0.05, 0.2, 0.00045, 1.0, 3.0))
LAND = 3.0
QALL = (None, "vector", "scalar", "tensor", "pool", "sync")


def cost(q, c, md):
    if q == "tensor": return c[0] * md[4] * md[0] + c[2] * 0.006
    if q == "pool": return (c[0] * 0.00083 * md[0] + c[3]) * md[5]
    if q is None: return c[3] + md[6]
    if q == "sync": return 0.4
    if q == "scalar": return (max(64, c[0]) if c[0] else c[1] * md[1]) * 0.00083 * md[0] + md[2] + 0.025 + c[3]
    return ((max(64, c[0]) if c[0] else 0) + c[1] * md[1]) * 0.00083 * md[0] + c[2] * md[2] + c[3]


def backward(ops, us, lat, succ, ends, asg):
    n = len(ops)
    left = [len(s) for s in succ]
    rt, pr, free = [0.0] * n, [0.0] * n, {}
    ready = {q: [] for q in QALL}
    for i in range(n):
        if not left[i]: ready[asg[i]].append(i)
    for _ in range(n):
        t, q = min((max(min(rt[i] for i in c), free.get(q, 0.0)), k) for k, (q, c) in enumerate(ready.items()) if c)
        q = QALL[q]
        i = max((i for i in ready[q] if rt[i] <= t + 1e-9), key=lambda i: ends[i])
        ready[q].remove(i)
        pr[i] = t + us[i][q]
        if q is not None: free[q] = pr[i]
        for j in set(ops[i]["deps"]) | set(ops[i]["after"]):
            hard = ops[i]["deps"].get(j)
            rt[j] = max(rt[j], pr[i] + (lat[j] if hard and hard != "acc" else 0.0 if hard or q is None else -us[j][asg[j]]))
            left[j] -= 1
            if not left[j]: ready[asg[j]].append(j)
    return pr


def plan(ops, md, cfg):
    best = pl = None
    for _ in range(cfg["it"] + 1):
        pl = forward(ops, md, cfg, *((pl[5], pl[1]) if pl else ()))
        if pl is None: break
        v = sum(replay(ops, pl, m) / (m[0] * (1 + m[1])) for m in MODELS)
        if best is None or v < best[0]: best = (v, pl)
    return best and best[1]


def forward(ops, md, cfg, ends=None, asg0=None):
    look, vb = cfg["look"], cfg["vb"]
    n = len(ops)
    us = [{x[0]: cost(x[0], x[1], md) for x in o["opts"]} for o in ops]
    lat = [(2.2 if o["sem"] and None not in o["qs"] else 0.0) + md[3] for o in ops]
    succ = [[] for _ in range(n)]
    left = [0] * n
    users = {}
    for i, o in enumerate(ops):
        p = set(o["deps"]) | set(o["after"])
        left[i] = len(p)
        for j in p: succ[j].append(i)
        for b in o["banks"]: users.setdefault(b, []).append(i)
    pr = [0.0] * n
    for i in range(n - 1, -1, -1): pr[i] = max([pr[s] for s in succ[i]] or [0.0]) + lat[i] + min(us[i].values())
    if ends: pr = backward(ops, us, lat, succ, ends, asg0)
    opens = [any(users[b][0] == i for b in o["banks"]) for i, o in enumerate(ops)]
    rt, fin, asg = [0.0] * n, [0.0] * n, [None] * n
    free = {q: 0.0 for q in QALL}
    ready = {q: [] for q in QALL}
    for i in range(n):
        if not left[i]:
            for q in us[i]: ready[q].append(i)
    phys, prev, held = {}, {}, [None] * 8
    bfree = [0.0] * 8
    togo = {b: len(u) for b, u in users.items()}
    order = []
    while len(order) < n:
        bt, bq, bc = None, None, None
        fb = [k for k in range(8) if held[k] is None or not togo[held[k]]]
        tb = min([bfree[k] for k in fb] or [1e9])
        for q in QALL:
            c = ready[q]
            if not c: continue
            if q == "tensor":
                top = max(pr[i] for z in ready.values() for i in z) - cfg["far"] if len(fb) <= cfg["keep"] else -1e9
                c = [(max(rt[i], tb) if opens[i] else rt[i], i) for i in c if not opens[i] or pr[i] >= top]
                if not c: continue
            else: c = [(rt[i], i) for i in c]
            t = max(min(c)[0], free[q])
            if bt is None or t < bt: bt, bq, bc = t, q, c
        if bt is None or bt >= 1e9: return None
        bias = vb if bq == "vector" else 0.0
        key = lambda z: pr[z[1]] - (bias if len(us[z[1]]) > 1 else 0.0)
        now = [z for z in bc if z[0] <= bt + 1e-9]
        best = max(now, key=key)
        ahead = []
        if bq in ("vector", "scalar") and us[best[1]][bq] > 0.3:
            other = "vector" if bq == "scalar" else "scalar"
            tq, lf, at = {"tensor": free["tensor"], other: max(free[other], bt)}, {}, {}
            todo = [(j, "tensor") for j in ready["tensor"]] + [(j, other) for j in ready[other] if len(us[j]) == 1]
            while todo:
                t, _, j, q = min((max(rt[j], at.get(j, 0.0), tq[q]), -pr[j], j, q) for j, q in todo)
                if t > bt + look * us[best[1]][bq]: break
                todo.remove((j, q))
                t = tq[q] = t + us[j][q]
                for k in succ[j]:
                    lf[k] = lf.get(k, left[k]) - 1
                    at[k] = max(at.get(k, 0.0), t + md[3])
                    if lf[k]: continue
                    if bq in us[k]: ahead.append((max(rt[k], at[k]), k))
                    elif "tensor" in us[k] or other in us[k]: todo.append((k, "tensor" if "tensor" in us[k] else other))
        soon = [z for z in bc + ahead if z[0] > bt + 1e-9 and key(z) > key(best) + cfg["gap"] and z[0] < bt + look * us[best[1]][bq]
                and (len(us[z[1]]) == 1 or bq == "scalar")]
        if soon:
            u = min(soon)
            fit = [z for z in now if bt + us[z[1]][bq] <= u[0] + 0.1]
            if not fit and u in ahead:
                free[bq] = u[0]
                continue
            best = max(fit, key=key) if fit else u
        t, i = max(bt, best[0]), best[1]
        for q in us[i]: ready[q].remove(i)
        for b in ops[i]["banks"]:
            if b not in phys:
                k = min((k for k in fb if bfree[k] <= t + 1e-9), key=lambda k: bfree[k])
                if held[k] is not None: prev[i] = users[held[k]]
                phys[b], held[k] = k, b
        f = t + us[i][bq]
        if bq is not None: free[bq] = f
        asg[i], fin[i] = bq, f + lat[i] - md[3]
        order.append(i)
        for b in ops[i]["banks"]:
            togo[b] -= 1
            bfree[phys[b]] = max(bfree[phys[b]], f + md[3])
        for j in succ[i]:
            hard = ops[j]["deps"].get(i)
            d = f if hard == "acc" else f + lat[i] if (hard or ops[j]["qs"] == {None}) else t
            rt[j] = max(rt[j], d)
            left[j] -= 1
            if not left[j]:
                for q in us[j]: ready[q].append(j)
    return order, asg, phys, prev, max(fin), fin


def replay(ops, pl, md):
    order, asg, phys, prev = pl[:4]
    fin, free = {}, {}
    for i in order:
        o, q = ops[i], asg[i]
        t = free.get(q, 0.0) if q is not None else 0.0
        for j, k in o["deps"].items():
            t = max(t, fin[j] + (0.0 if asg[j] == q and k != "w" and not ops[j]["sem"] else md[3]))
        for j in prev.get(i, ()): t = max(t, fin[j] + (0.0 if asg[j] == q else md[3]))
        if q is None: t = max([t] + [fin[j] - 2.2 for j in o["after"]])
        f = t + [cost(q, x[1], md) for x in o["opts"] if x[0] == q][0]
        free[q] = f
        fin[i] = f + (2.2 if o["sem"] and q is not None else 0.0)
    return max(fin.values())


def search(ops, pl, cfg, tries, temp, seed, lags):
    order, asg = list(pl[0]), [QALL.index(q) for q in pl[1]]
    n = len(ops)
    anc, pre = [0] * n, []
    for i, o in enumerate(ops):
        d = {j: int(w != "w" and not ops[j]["sem"]) for j, w in o["deps"].items()}
        far = 0
        for j in d: far |= anc[j]
        anc[i] = far | sum(1 << j for j in d)
        d = {j: s for j, s in d.items() if not far >> j & 1}
        if None in o["qs"]:
            for j in o["after"]: d[j] = 2
        pre.append(list(d.items()))
    succ = [[] for _ in range(n)]
    for i in range(n):
        for j, s in pre[i]: succ[j].append((i, s))
    pj, sj = [[j for j, s in z] for z in pre], [[j for j, s in z] for z in succ]
    users = {}
    for i, o in enumerate(ops):
        for b in o["banks"]: users.setdefault(b, []).append(i)
    opens = {u[0]: b for b, u in users.items()}
    lastof = {u[0]: u[-1] for u in users.values()}
    us = [[[0.0] * 6 for o in ops] for md in MODELS]
    for x, md in enumerate(MODELS):
        for i, o in enumerate(ops):
            for z in o["opts"]: us[x][i][QALL.index(z[0])] = cost(z[0], z[1], md)
    both = [len(o["opts"]) > 1 for o in ops]
    tail = [LAND if o["sem"] and None not in o["qs"] else 0.0 for o in ops]
    ends = [i for i in range(n) if tail[i] and not succ[i]]
    lag = [(i, lags[o["name"][1:]]) for i, o in enumerate(ops) if o["name"][1:] in lags]
    wt = [w / (m[0] * (1 + m[1])) for m, w in zip(MODELS, cfg["wt"])]
    w0, w1, w2 = (m[3] for m in MODELS)
    u0, u1, u2 = us
    bp, nb = [-1] * n, [-1] * n
    for i, u in pl[3].items(): bp[i] = u[-1]; nb[u[-1]] = i
    bk = dict(pl[2])
    seq = [[i for i in order if asg[i] == q] for q in range(6)]
    mp, mn = [-1] * (n + 1), [-1] * (n + 1)
    for s in seq[1:]:
        for a, b in zip(s, s[1:]): mp[b], mn[a] = a, b
    pos = [0] * n
    for p, j in enumerate(order): pos[j] = p
    E_, H_, T_, J_ = ([[0.0] * (n + 1) for x in range(3)] for y in range(4))
    marks = ([False] * (n + 1), [False] * (n + 1))
    win = [0, n, n]

    def sweep(seeds, back):
        (e0, e1, e2), (h0, h1, h2), near, far, bi, bo, mi, mo = (T_, J_, succ, pj, nb, bp, mn, mp) if back else (E_, H_, pre, sj, bp, nb, mp, mn)
        left, log, mark = 0, [], marks[back]
        mark[n] = True
        for i in seeds:
            if not mark[i]: mark[i] = True; left += 1
        p = [pos[i] for i in seeds if i >= 0]
        for i in (order[max(0, win[0] - 40):max(p) + 1][::-1] if back else order[min(p):win[2]]):
            if not mark[i]: continue
            mark[i] = False
            q = asg[i]
            z = t0 = t1 = t2 = tail[i] if back else 0.0
            for j, soft in near[i]:
                if soft and (asg[j] == q or soft == 2): x0, x1, x2 = e0[j], e1[j], e2[j]
                else:
                    if not back: z = tail[j]
                    x0, x1, x2 = e0[j] + w0 + z, e1[j] + w1 + z, e2[j] + w2 + z
                if x0 > t0: t0 = x0
                if x1 > t1: t1 = x1
                if x2 > t2: t2 = x2
            j = bi[i]
            if j >= 0:
                x0, x1, x2 = e0[j] + w0, e1[j] + w1, e2[j] + w2
                if x0 > t0: t0 = x0
                if x1 > t1: t1 = x1
                if x2 > t2: t2 = x2
            log.append((i, e0[i], e1[i], e2[i], h0[i], h1[i], h2[i]))
            h0[i], h1[i], h2[i] = t0, t1, t2
            j = mi[i]
            if e0[j] > t0: t0 = e0[j]
            if e1[j] > t1: t1 = e1[j]
            if e2[j] > t2: t2 = e2[j]
            t0 += u0[i][q]; t1 += u1[i][q]; t2 += u2[i][q]
            if e0[i] != t0 or e1[i] != t1 or e2[i] != t2:
                e0[i], e1[i], e2[i] = t0, t1, t2
                for j in far[i]:
                    if not mark[j]: mark[j] = True; left += 1
                j = mo[i]
                if not mark[j]: mark[j] = True; left += 1
                j = bo[i]
                if not mark[j]: mark[j] = True; left += 1
            left -= 1
            if not left: break
        return log

    def undo(log):
        for i, a, b, c, d, e, f in log: E_[0][i], E_[1][i], E_[2][i], H_[0][i], H_[1][i], H_[2][i] = a, b, c, d, e, f

    def end():
        if win[2] >= n: M = [max(e[i] for i in ends) + LAND for e in E_]
        else:
            zone = order[win[1]:win[2]]
            M = [max([e[i] + t[i] - u[i][asg[i]] for i in zone]) for e, t, u in zip(E_, T_, us)]
        return M, M[0] * wt[0] + M[1] * wt[1] + M[2] * wt[2]

    def put(i, q, a):
        s = seq[asg[i]]
        s.remove(i)
        mn[mp[i]], mp[mn[i]] = mn[i], mp[i]
        s = seq[q]
        mp[i], mn[i] = s[a - 1] if a else -1, s[a] if a < len(s) else -1
        s.insert(a, i)
        mn[mp[i]] = mp[mn[i]] = i
        asg[i] = q

    def deal(f):
        held = [-1] * 8
        bp[:], nb[:] = [-1] * n, [-1] * n
        for p, i in enumerate(order):
            if i in opens:
                b = min((b for b in range(8) if held[b] < 0 or pos[held[b]] < p), key=lambda b: f[held[b]] if held[b] >= 0 else -1.0)
                if held[b] >= 0: bp[i] = held[b]; nb[held[b]] = i
                bk[opens[i]], held[b] = b, lastof[i]

    def sort(lo, hi):
        part = order[lo:hi + 1]
        left = dict.fromkeys(part, 0)
        for i in part:
            for j in pj[i] + [bp[i], mp[i]]:
                if j in left: left[i] += 1
        out = [i for i in part if not left[i]]
        for i in out:
            for j in sj[i] + [mn[i], nb[i]]:
                if j in left:
                    left[j] -= 1
                    if not left[j]: out.append(j)
        if len(out) == len(part): order[lo:hi + 1] = out
        return len(out) == len(part)

    def holds(lo, hi, old, seeds, most):
        for c in range(lo, hi + 1): pos[order[c]] = c
        log = sweep(seeds, False)
        r = end()
        if r[1] <= most: return r
        undo(log)
        order[lo:hi + 1] = old
        for c in range(lo, hi + 1): pos[order[c]] = c
    seed = [seed]

    def rnd(m):
        seed[0] = (seed[0] * 1103515245 + 12345) % 2147483648
        return (seed[0] >> 8) % m
    sweep(order, False); sweep(order, True)
    M, now = end()
    best = (now, list(order), list(asg), dict(bk))
    until, crit = [0] * n, {}
    X = (0, 1, 2)
    e1, t1 = E_[1], T_[1]
    for it in range(1, tries + 1):
        if it % cfg["stay"] == 1 or it == tries:
            for i, v in lag: tail[i] = v * max(0.0, 1 - it / (0.5 * tries))
            win[:] = 0, n, n
            marks[0][:] = marks[1][:] = [False] * (n + 1)
            sweep(order, False)
            order.sort(key=lambda j: e1[j] - u1[j][asg[j]])
            for c, j in enumerate(order): pos[j] = c
            M, now = end()
            if now < best[0] - 1e-9 and (not lag or it > 0.5 * tries): best = (now, list(order), list(asg), dict(bk))
            was = (list(bp), list(nb), dict(bk))
            deal(e1)
            log = sweep(order, False)
            M2, v = end()
            if v <= now + 0.02: M, now = M2, v
            else:
                undo(log)
                bp[:], nb[:] = was[:2]
                bk.update(was[2])
            sweep(order, True)
            a = max(0, rnd(n + cfg["wide"] // 2) - cfg["wide"] // 2)
            win[:] = a, a + cfg["wide"], a + cfg["wide"] + cfg["zone"]
            crit = {}
        km = rnd(3)
        if km not in crit:
            lim, e, t, u = M[km] - 1e-6, E_[km], T_[km], us[km]
            crit[km] = [i for i in order[win[0]:win[1]] if e[i] + t[i] - u[i][asg[i]] > lim and asg[i]]
        cr, cand, T = crit[km], None, temp * (1 - it / tries)
        if cr and rnd(100) < cfg["swap"]:
            i = cr[rnd(len(cr))]
            p = pos[i] + rnd(81) - 40
            if not win[0] <= p < min(n, win[1]): continue
            j = order[p]
            q, q2 = asg[i], asg[j]
            if i == j or q > 2 or q2 > 2 or not q2 or (q != q2 and not (both[i] and both[j])) or abs(u1[i][q] - u1[j][q2]) > 0.3: continue
            if anc[i] >> j & 1 or anc[j] >> i & 1: continue
            a, b = seq[q].index(i), seq[q2].index(j)
            near = [mp[i], mn[i], mp[j], mn[j]]
            there, back = ((i, q2, b), (j, q, a)), ((j, q2, b), (i, q, a))
            if q == q2 and a > b: there, back = there[::-1], back[::-1]
            for z in there: put(*z)
            lo, hi = min(pos[i], p), max(pos[i], p)
            for z in (i, j):
                lo = min([lo] + [pos[y] for y in sj[z] + [nb[z], mn[z]] if y >= 0])
                hi = max([hi] + [pos[y] for y in pj[z] + [bp[z], mp[z]] if y >= 0])
            old = order[lo:hi + 1]
            r = sort(lo, hi) and holds(lo, hi, old, [i, j] + near + sj[i] + sj[j], now + T * rnd(1000) / 1000)
            if r:
                (M, now), crit = r, {}
                sweep([i, j] + near + pj[i] + pj[j], True)
            else:
                for z in back: put(*z)
            continue
        for _ in range(cfg["ns"] if cr else 0):
            i = cr[rnd(len(cr))]
            if until[i] > it: continue
            q = asg[i]
            low = [0.0 if E_[x][i] + T_[x][i] - us[x][i][q] > M[x] - 1e-6 else M[x] for x in X]
            h1i, j1i = H_[1][i] + 1e-9, J_[1][i] + 1e-9
            for step, on, off, A_, B_, C_, D_, lim in ((-1, mp, mn, E_, H_, T_, J_, h1i), (1, mn, mp, T_, J_, E_, H_, j1i)):
                v = on[i]
                if v < 0 or B_[km][i] >= A_[km][v] - 1e-9: continue
                tt = [C_[x][off[i]] for x in X]
                for a in range(1, 9):
                    if v < 0 or A_[1][v] <= lim: break
                    est, y_ = rnd(100) * 1e-4, on[v]
                    for x in X:
                        y = D_[x][v]
                        if tt[x] > y: y = tt[x]
                        y += us[x][v][q]; tt[x] = y
                        r = B_[x][i]
                        if A_[x][y_] > r: r = A_[x][y_]
                        z = D_[x][i]
                        L = r + us[x][i][q] + (y if y > z else z)
                        est += wt[x] * (L if L > low[x] else low[x])
                    if cand is None or est < cand[0]: cand = (est, i, q, a * step)
                    v = y_
            if both[i]:
                q2 = 3 - q
                s2 = seq[q2]
                lo, hi = 0, len(s2)
                while lo < hi:
                    mid = (lo + hi) // 2
                    if e1[s2[mid]] <= h1i: lo = mid + 1
                    else: hi = mid
                low = [max(low[x], E_[x][mp[i]] + T_[x][mn[i]]) for x in X]
                for a in range(lo, min(len(s2), lo + 6) + 1):
                    u, v = s2[a - 1] if a else -1, s2[a] if a < len(s2) else -1
                    if a and t1[u] <= j1i: break
                    est = rnd(100) * 1e-4
                    for x in X:
                        r = H_[x][i]
                        if E_[x][u] > r: r = E_[x][u]
                        z = J_[x][i]
                        if T_[x][v] > z: z = T_[x][v]
                        L = r + us[x][i][q2] + z
                        est += wt[x] * (L if L > low[x] else low[x])
                    if cand is None or est < cand[0]: cand = (est, i, q2, a)
        if cand is None: continue
        est, i, q2, a = cand
        until[i] = it + 10 + rnd(30)
        if est > now + T * rnd(1000) / 1000: continue
        q, at, a0, b0 = asg[i], pos[i], mp[i], mn[i]
        p = seq[q].index(i)
        put(i, q2, a + p if q == q2 else a)
        lo = max([pos[j] for j in pj[i] + [bp[i], mp[i]] if j >= 0] or [-1])
        hi = min([pos[j] for j in sj[i] + [nb[i], mn[i]] if j >= 0] or [n])
        lo, hi, plain = (min(at, hi), max(at, lo), 0) if lo > hi else (at, lo, 1) if lo > at else (hi, at, -1) if hi < at else (at, at, 1)
        old = order[lo:hi + 1]
        if plain: order[lo:hi + 1] = old[plain:] + old[:plain]
        r = (plain or sort(lo, hi)) and holds(lo, hi, old, [i, b0, mn[i]] + sj[i], now + T)
        if r:
            (M, now), crit = r, {}
            sweep([i, a0, mp[i]] + pj[i], True)
        else: put(i, q, p)
    prev, held = {}, {}
    for i in best[1]:
        if i in opens:
            b = best[3][opens[i]]
            if b in held: prev[i] = held[b]
            held[b] = users[opens[i]]
    return best[1], [QALL[q] for q in best[2]], best[3], prev


def schedule(pinned, ops, cfg):
    pl = plan(pinned, MODELS[1], cfg)
    for k, (tries, temp) in enumerate(cfg["cycles"]): pl = search(ops, pl, cfg, tries, temp, cfg["seed"] + 100 * k, {} if k else cfg["lag"])
    return pl


def rank_program(g, core, T, topo):
    rank = T.rank_of(core)
    if rank is None:
        return
    phys = {}
    ops = build(T, rank, topo, core, phys, dict(CFG, pin={}))
    if "p" not in PLAN: PLAN["p"] = schedule(build(T, rank, topo, core, {}, CFG), ops, CFG)
    order, asg, ph, prev = PLAN["p"][:4]
    phys.update(ph)
    pos = {j: k for k, j in enumerate(order)}
    eng = {"vector": g.vector, "scalar": g.scalar, "tensor": g.tensor, "pool": g, "sync": g.sync}
    count = {}
    done = {}
    clock = {}
    know = {q: {} for q in eng}
    for i in order:
        o, q = ops[i], asg[i]
        if q is None:
            done[i] = o["sem"]; clock[i] = {}
            continue
        need = {}
        deps = dict(o["deps"])
        for j in prev.get(i, ()): deps.setdefault(j, "ord")
        for j, kind in deps.items():
            if asg[j] == q and kind != "w" and not ops[j]["sem"] and not o["sem"]: continue
            s, v = done[j]
            if need.get(s, (0, 0))[0] < v: need[s] = (v, j)
        kn = know[q]
        for s, (v, j) in sorted(need.items(), key=lambda z: -pos[z[1][1]]):
            if kn.get(s, 0) >= v: continue
            eng[q].wait_ge(T.sem[s], v)
            for s2, v2 in clock[j].items():
                if kn.get(s2, 0) < v2: kn[s2] = v2
            kn[s] = max(kn.get(s, 0), v)
        ins = [x[2] for x in o["opts"] if x[0] == q][0](eng[q])
        clock[i] = dict(kn)
        if o["sem"]:
            done[i] = o["sem"]
            if o["sem"][0][0] == "d": ins.then_inc(T.sem[o["sem"][0]], o["sem"][1])
        else:
            s = "q_" + q
            count[s] = count.get(s, 0) + 1
            ins.then_inc(T.sem[s], 1)
            done[i] = (s, count[s])
    fin = dict(count)
    for o in ops:
        if o["sem"]: fin[o["sem"][0]] = o["sem"][1]
    for s in sorted(fin): g.wait_ge(T.sem[s], fin[s])
